import numpy as np, ml_dtypes
CORES = [1,5,17,21,33,37,49,53]
N = 8
import mx_ref
BF = ml_dtypes.bfloat16
def entries(a):
    return np.ascontiguousarray(a.T).reshape(-1)
def table(e):
    return np.ascontiguousarray(np.reshape(e, (-1, 16)).T).astype(np.int32)
def pick(q, e):
    c = np.concatenate([q[0].reshape(128, -1, 4), np.zeros((128, 1, 4), np.uint8)], axis=1); s = np.concatenate([q[1], np.ones((16, 1), np.uint8)], axis=1)
    return (np.ascontiguousarray(c[:, e].reshape(128, -1)), np.ascontiguousarray(s[:, e]))
def join(*qs):
    return (np.concatenate([q[0] for q in qs], axis=1), np.concatenate([q[1] for q in qs], axis=1))
def put(q, e, v):
    c, s = q[0].reshape(128, -1, 4).copy(), q[1].copy(); c[:, e] = v[0].reshape(128, -1, 4); s[:, e] = v[1]
    return (c.reshape(128, -1), s)
def pk(c, s):
    return (np.ascontiguousarray(c), mx_ref.live(s))
def emit(q):
    return q[0], q[1]
def decode(q):
    o = []
    for b in range(4):
        e = np.zeros((128, 128, 4), np.float32); e[np.arange(128), np.arange(128), b] = 1
        o.append(mx_ref.matmul(mx_ref.quantize(e.reshape(128, 512).astype(BF)), q))
    return np.stack(o, axis=2).reshape(128, -1)
def cut(t, i, w=512):
    return t[:, w * i:w * i + w]
def f(rng, *shape):
    return mx_ref.flush((rng.standard_normal(shape, dtype=np.float32) * np.exp2(rng.integers(-2, 3, shape[:-1] + (1,)))).astype(BF))
def wide(rng, *shape, cols=0):
    v = rng.standard_normal(shape, dtype=np.float32) * np.exp2(rng.integers(-12, 13, shape)).astype(np.float32)
    if cols: v *= np.repeat(np.exp2(rng.integers(-cols, cols + 1, shape[:-2] + (1, shape[-1] // 4))) * (rng.random(shape[:-2] + (1, shape[-1] // 4)) > 0.0625), 4, axis=-1).astype(np.float32)
    return mx_ref.flush(v.astype(BF))
P, S, K, R, B, M, O = 256, 32, 32, 3, 48, 4, 2
def big(v):
    v = np.array(v).astype(np.float32)
    v[np.abs(v) < np.float32(2.0 ** -16)] = 0
    return v.astype(BF)
def link(adj, a, b):
    a, b = int(a), int(b)
    if a != b and len(adj[a]) < M and len(adj[b]) < M and b not in adj[a]:
        adj[a].append(b)
        adj[b].append(a)
def inner(rng, adj, e):
    for t in range(2 * M):
        a = rng.permutation(e)
        for i in range(0, a.size - 1, 2): link(adj, a[i], a[i + 1])
def across(rng, adj, ranks):
    for r in ranks:
        for q in ranks:
            if r < q:
                a, c = P * r + rng.permutation(P), P * q + rng.permutation(P)
                n = int(rng.integers(B // 2, B + 1))
                for i in range(n):
                    link(adj, a[i], c[i])
                    if i % 3 == 0: link(adj, a[i], c[(i + 1) % n])
def graph(rng):
    adj = [[] for a in range(N * P)]
    across(rng, adj, range(N))
    for r in range(N): inner(rng, adj, np.arange(P * r, P * r + P))
    return adj
def seeds(rng):
    return np.stack([rng.permutation(P)[:S] for r in range(N)])
def lists(rng, adj, s, late=False):
    at = np.argsort(rng.random((N * P, M)), axis=1)
    seed = np.zeros(N * P, bool)
    for r in range(N): seed[P * r + s[r]] = True
    n = np.full((N, M, P), -1)
    for a in range(N * P):
        k, e = at[a, :len(adj[a])], adj[a]
        if late: k, e = np.sort(k), sorted(e, key=lambda c: bool(seed[c]))
        for i, c in zip(k, e): n[a // P, i, a % P] = c
    return {"nb": np.stack([table(v.reshape(-1)) for v in n]), "sd": np.stack([table(v) for v in s])}
def plain(rng):
    return {"x": big(f(rng, N, 128, 4 * P)), "w": f(rng, N, 128, 512 * O)}
def setup_inputs(rng):
    return {**plain(rng), **lists(rng, graph(rng), seeds(rng))}
def setup_inputs_caps(rng):
    o = np.stack([rng.permutation(P) for r in range(N)])
    adj = [[] for a in range(N * P)]
    dense = int(rng.integers(0, N))
    for r in range(N):
        q = (r + 1) % N
        if r == dense:
            a = P * r + np.concatenate([o[r, S:S + K], o[r, K + B:2 * B]])
            c = P * q + np.concatenate([o[q, :S // 2], rng.permutation(np.concatenate([o[q, S // 2:S], o[q, S + K:K + B]]))])
            for i in range(B):
                for j in range(i - i % M, min(i - i % M + M, B)): link(adj, a[i], c[j])
        else:
            for i in range(K):
                link(adj, P * r + o[r, S + i], P * q + o[q, i])
                link(adj, P * r + o[r, S + i], P * q + o[q, S + K + i % (B - S)])
    for r in range(N): inner(rng, adj, P * r + o[r, S:])
    return {**plain(rng), **lists(rng, adj, o[:, :S])}
def setup_inputs_few(rng):
    adj, s, o, n, m = [[] for a in range(N * P)], seeds(rng), rng.permutation(N), K // 2 - 1, S // 2
    some, rest = int(o[1]), sorted(o[2:].tolist())
    ends = np.unique([0, 127, P - 1])
    s[some] = rng.permutation(np.setdiff1d(np.arange(P), ends))[:S]
    free, at, zero = rng.permutation(np.setdiff1d(np.arange(P), np.concatenate([s[some], ends]))), 0, []
    for i in range(K // 2):
        end = s[some, i]
        for t in range(1 + i % R):
            link(adj, P * some + end, P * some + free[at])
            end = free[at]
            at += 1
        if i < K // 4: zero.append(int(end))
    idle = np.sort(free[at:])
    lone = np.concatenate([ends, idle[:n - ends.size]])
    idle = rng.permutation(idle[n - ends.size:])
    for i in range(idle.size): link(adj, P * some + idle[i - 1], P * some + idle[i])
    for r in rest[:2]:
        g, e = rng.permutation(P // 8)[:n], P // 8 + rng.permutation(P // 8)[:m]
        s[r] = rng.permutation(np.setdiff1d(np.arange(P), np.concatenate([g, e])))[:S]
        high = rng.permutation(np.setdiff1d(np.arange(3 * P // 8, P), s[r]))
        for i in range(K): link(adj, P * r + s[r, i], P * r + high[i])
        for i in range(n):
            link(adj, P * r + s[r, i], P * r + g[i])
            link(adj, P * some + lone[i], P * r + g[i])
        for i in range(m):
            link(adj, P * r + s[r, n + i], P * r + e[i])
            link(adj, P * some + s[some, m + i], P * r + e[i])
    across(rng, adj, rest)
    for r in rest: inner(rng, adj, np.arange(P * r, P * r + P))
    sign = np.ones(N)
    sign[rest[::2]] = -0.75
    j = np.arange(P)
    v = f(rng, N, 128, 4 * P).astype(np.float32).reshape(N, 128, P, 4)
    v[:, :64] = 0
    for r in range(N):
        on = np.isin(j, s[r])
        v[r][64:96][:, ~on] = 0
        v[r][96:][:, on] = 0
        v[r, 0, :, 0] = 1024.0 * np.where(on, 1.0, sign[r])
        v[r, 40, :, 0] = np.where(on, rng.integers(1, 3, P), 0.125 * (8 * j // P))
    for r in rest[:2]: v[r, 40, s[r, n:n + m], 0] = 2.0
    v[some, 40, s[some, m:], 0] = 1.0
    v[some, 0, lone, 0] = 4096.0
    v[some][:, zero] = 0
    return {**plain(rng), "x": big(v.reshape(N, 128, 4 * P)), **lists(rng, adj, s)}
def setup_inputs_huge(rng):
    s = seeds(rng)
    v = rng.random((N, 128, P, 4), dtype=np.float32)
    for r in range(N):
        on = np.isin(np.arange(P), s[r])[None, :, None]
        u = ((0.7 + 0.85 * rng.random(P)) * (1 - 2 * (r % 2)))[None, :, None]
        v[r] = np.where(on, 1.7 + 0.28 * v[r], (0.8 + 0.45 * v[r]) * u)
    return {**plain(rng), "x": big((v * np.float32(2.0 ** 29)).reshape(N, 128, 4 * P)), **lists(rng, graph(rng), s)}
def setup_inputs_spread(rng):
    return {**setup_inputs(rng), "x": big(wide(rng, N, 128, 4 * P, cols=6))}
def setup_inputs_ties(rng):
    g = rng.integers(4, 8, (128, 3, 4)) * np.exp2(rng.integers(-2, 1, (128, 3, 4))) * rng.choice([-1.0, 1.0], (128, 3, 4)) * np.exp2(rng.integers(-2, 3, (128, 3, 1)))
    h = rng.integers(0, 3, (N, P))
    h[::2] = 0
    return {**plain(rng), "x": big(np.stack([g[:, h[r]].reshape(128, -1) for r in range(N)])), **lists(rng, graph(rng), seeds(rng), late=True)}
def check_inputs(d):
    b = []
    for k, low in (("x", 2.0 ** -16), ("w", 2.0 ** -30)):
        v = np.abs(d[k].astype(np.float32))
        if not (np.isfinite(v).all() and ((v == 0) | (v >= low) & (v <= 2.0 ** 30)).all()): b.append("a value of " + k)
    for r in range(N):
        e = entries(d["sd"][r])
        if e.min() < 0 or e.max() >= P or np.unique(e).size != S: b.append("sd")
    e = np.concatenate([entries(d["nb"][r]).reshape(M, P) for r in range(N)], axis=1).astype(np.int64)
    if e.min() < -1 or e.max() >= N * P: return b + ["nb"]
    k, j = np.nonzero(e >= 0)
    n = e[k, j]
    a, c = j * (N * P) + n, n * (N * P) + j
    if (n == j).any() or np.unique(a).size != a.size: b.append("nb names a place twice or itself")
    if not np.array_equal(np.sort(a), np.sort(c)): b.append("nb isn't symmetric")
    for r in range(N):
        for q in range(N):
            if q != r and np.count_nonzero((e[:, P * r:P * r + P] // P == q).any(axis=0)) > B: b.append("places with neighbours on one other rank")
    return b
def reference(x, w, nb, sd):
    first = join(*[mx_ref.quantize(np.ascontiguousarray(x[r])) for r in range(N)])
    now = first
    near = np.concatenate([entries(nb[r]).reshape(M, P) for r in range(N)], axis=1)
    parent = np.full(N * P, -1)
    fresh = np.concatenate([P * r + entries(sd[r]) for r in range(N)])
    parent[fresh] = fresh
    score = np.full((M, N * P), -np.inf, np.float32)
    for t in range(R):
        spot = np.full(N * P + 1, -1)
        spot[fresh] = np.arange(fresh.size)
        side = pick(now, np.concatenate([fresh, np.full(4 + -fresh.size % 4, -1)]))
        z = np.concatenate([mx_ref.matmul(pick(first, np.arange(i, i + 128)), side) for i in range(0, N * P, 128)])
        k, j = np.nonzero(spot[near] >= 0)
        score[k, j] = z[j, spot[near[k, j]]] + np.float32(0)
        best, at = score.max(axis=0), score.argmax(axis=0)
        chosen = []
        for r in range(N):
            mine = np.arange(P * r, P * r + P)
            c = mine[(parent[mine] < 0) & np.isfinite(best[mine])]
            chosen.append(c[np.argsort(-best[c], kind="stable")[:K]])
        fresh = np.concatenate(chosen)
        parent[fresh] = near[at[fresh], fresh]
        pad = np.full(4 + -fresh.size % 4, -1)
        v = decode(pick(now, np.concatenate([fresh, pad, parent[fresh], pad])))
        h = v.shape[1] // 2
        new = mx_ref.quantize(np.ascontiguousarray(((v[:, :h] + v[:, h:]) * np.float32(0.5)).astype(BF)))
        now = put(now, fresh, pick(new, np.arange(fresh.size)))
    y, pa = np.zeros((N, 128, O * P), np.float32), np.zeros((N, 1, P), np.float32)
    oc, osc = np.zeros((N, 128, 4 * P), np.uint8), np.zeros((N, 16, P), np.uint8)
    for r in range(N):
        mine = np.arange(P * r, P * r + P)
        q = pick(now, mine)
        for o in range(O): y[r, :, P * o:P * o + P] = mx_ref.matmul(mx_ref.quantize(np.ascontiguousarray(cut(w[r], o))), q)
        oc[r], osc[r] = emit(q)
        pa[r, 0] = parent[mine]
    return {"y": y, "oc": oc, "osc": osc, "pa": pa}

@@ -1,0 +1,490 @@
+import numpy as np
+from concourse.bass import DstId, RemoteDMATransfer
+from concourse.mybir import dt, AluOpType as Op, AxisListType, ActivationFunctionType as Fn
+
+F8 = "float8_e4m3fn_x4"
+W1, W2, WF = 608, 864, 448
+SCRATCH = {
+    "xt": ("sbuf", [128, 1024], "bfloat16"), "wt": ("sbuf", [128, 1024], "bfloat16"),
+    "qx": ("sbuf", [128, 256], F8), "qxs": ("sbuf", [128, 256], "uint8"),
+    "qw": ("sbuf", [128, 256], F8), "qws": ("sbuf", [128, 256], "uint8"),
+    "et": ("sbuf", [128, 2048], "bfloat16"), "eq": ("sbuf", [128, 512], F8), "eqs": ("sbuf", [128, 512], "uint8"),
+    "comb0": ("sbuf", [128, 256], F8), "comb0s": ("sbuf", [128, 256], "uint8"),
+    "comb1": ("sbuf", [128, W1], F8), "comb1s": ("sbuf", [128, W1], "uint8"),
+    "comb2": ("sbuf", [128, W2], F8), "comb2s": ("sbuf", [128, W2], "uint8"),
+    "finw": ("sbuf", [128, WF], F8), "finws": ("sbuf", [128, WF], "uint8"),
+    "fin": ("sbuf", [128, 256], F8), "fins": ("sbuf", [128, 256], "uint8"),
+    "pko": ("sbuf", [128, 128], F8), "pkos": ("sbuf", [128, 128], "uint8"),
+    "pkp": ("sbuf", [128, 128], F8), "pkps": ("sbuf", [128, 128], "uint8"),
+    "ht": ("sbuf", [128, 512], "bfloat16"),
+    "sdw": ("sbuf", [128, 2], "int32"), "nbw": ("sbuf", [128, 64], "int32"),
+    "sdu": ("sbuf", [128, 2], "uint16"), "sdf": ("sbuf", [128, 4], "float32"),
+    "nbofi": ("sbuf", [128, 4], "int32"), "nbof": ("sbuf", [128, 2], "uint16"), "nbo": ("sbuf", [128, 16], "float32"),
+    "nbx": ("sbuf", [128, 8], "float32"),
+    "pint": ("sbuf", [128, 1], "int32"), "pidx": ("sbuf", [128, 1], "float32"), "icol": ("sbuf", [128, 128], "float32"),
+    "ici": ("sbuf", [128, 256], "int32"), "icj": ("sbuf", [128, 256], "int32"), "ic64": ("sbuf", [128, 64], "float32"),
+    "ci": ("sbuf", [128, 16], "int32"), "cf": ("sbuf", [128, 32], "float32"),
+    "plm": ("sbuf", [128, 256], "float32"), "thr": ("sbuf", [128, 512], "bfloat16"),
+    "ones32": ("sbuf", [128, 32], "float32"), "c19": ("sbuf", [128, 32], "float32"), "ones": ("sbuf", [128, 256], "bfloat16"),
+    "dg": ("sbuf", [128, 96], "float32"), "m16": ("sbuf", [128, 256], "float32"), "seg": ("sbuf", [128, 256], "float32"),
+    "c8": ("sbuf", [128, 8], "float32"),
+    "my0": ("sbuf", [128, 4], "float32"), "my1": ("sbuf", [128, 4], "float32"), "my2": ("sbuf", [128, 4], "float32"),
+    "land0": ("sbuf", [128, 8], "float32"), "land1": ("sbuf", [128, 8], "float32"), "land2": ("sbuf", [128, 8], "float32"),
+    "rpf": ("sbuf", [128, 256], "float16"), "ff": ("sbuf", [128, 256], "float16"),
+    "eqx": ("sbuf", [128, 2048], "bfloat16"), "sc": ("sbuf", [128, 2048], "bfloat16"), "prod": ("sbuf", [128, 2048], "float32"),
+    "t8": ("sbuf", [128, 8], "float32"), "u8": ("sbuf", [128, 8], "float32"), "pl8": ("sbuf", [128, 8], "float32"),
+    "pkb": ("sbuf", [128, 8], "float32"), "sb": ("sbuf", [128, 16], "float32"), "bst": ("sbuf", [128, 2], "float32"),
+    "ib": ("sbuf", [128, 2], "float32"), "rpa": ("sbuf", [128, 64], "float32"), "row": ("sbuf", [128, 256], "float32"),
+    "ed": ("sbuf", [128, 512], "bfloat16"), "cm": ("sbuf", [128, 512], "bfloat16"), "rk": ("sbuf", [128, 2], "float32"),
+    "e8": ("sbuf", [128, 8], "float32"), "q2": ("sbuf", [128, 2], "float32"), "qi": ("sbuf", [128, 4], "int32"),
+    "pay": ("sbuf", [128, 2], "float32"), "rpb": ("sbuf", [128, 64], "float32"), "tb": ("sbuf", [128, 64], "float32"),
+    "part": ("sbuf", [128, 1], "float32"), "rpc": ("sbuf", [128, 32], "float32"), "p4": ("sbuf", [128, 128], "float32"),
+    "l64": ("sbuf", [128, 64], "float32"), "l32": ("sbuf", [128, 32], "float32"), "dd": ("sbuf", [128, 96], "float32"),
+    "vals": ("sbuf", [128, 4], "float32"), "okv": ("sbuf", [128, 4], "float32"), "vz": ("sbuf", [128, 4], "float32"),
+    "vi": ("sbuf", [128, 12], "int32"), "offu": ("sbuf", [128, 4], "uint16"),
+    "tk": ("sbuf", [128, 2], "float32"), "nf": ("sbuf", [128, 2], "float32"), "nfm": ("sbuf", [128, 2], "float32"),
+    "fx": ("sbuf", [128, 2], "float32"), "fl": ("sbuf", [128, 2], "float32"), "pa2": ("sbuf", [128, 2], "float32"),
+    "w2": ("sbuf", [128, 2], "float32"), "w3": ("sbuf", [128, 2], "float32"), "rpd": ("sbuf", [128, 64], "float32"),
+    "flt": ("sbuf", [128, 64], "float32"), "flr": ("sbuf", [128, 256], "float32"), "flm": ("sbuf", [128, 256], "float32"),
+    "fls": ("sbuf", [128, 256], "float32"), "fo": ("sbuf", [128, 16], "uint16"), "sy": ("sbuf", [128, 512], "float32"),
+    "dec": ("psum", [128, 2048], "float32"), "zz": ("psum", [128, 1024], "float32"), "yy": ("psum", [128, 1024], "float32"),
+}
+SEMAPHORES = ["v", "s", "p", "gp", "dsd", "dx", "dnb", "dw", "arl0", "arl1", "arl2", "arc0", "arc1", "arc2",
+              "dc0", "dc1", "df0", "df1", "dout", "dpa", "sent"]
+
+
+def r(name, c0, c1, p0=0, p1=128, st=1):
+    return (name, c0, c1, p0, p1, st)
+
+
+def meet(a, b):
+    if a[0] != b[0] or a[1] >= b[2] or b[1] >= a[2] or a[3] >= b[4] or b[3] >= a[4]:
+        return False
+    return not (a[5] == b[5] and a[5] > 1 and (a[1] - b[1]) % a[5])
+
+
+def inside(a, b):
+    return a[1] >= b[1] and a[2] <= b[2] and a[3] >= b[3] and a[4] <= b[4] and b[5] == 1
+
+
+def rank_program(g, core, T, topo):
+    rank = T.rank_of(core)
+    if rank is None:
+        return
+    cores = list(T.cores)
+    n = len(cores)
+    S, P, R = 32, 256, 3
+
+    eng = {"v": g.vector, "s": g.scalar, "p": g.tensor, "y": g.sync, "g": g}
+    own = {"v": "v", "s": "s", "p": "p", "g": "gp"}
+    known = {e: {} for e in eng}
+    cnt = {}
+    hist = {}
+    seq = [0]
+
+    def need(e, toks):
+        for sem, val, clock, q in sorted(toks, key=lambda t: -t[3]):
+            if known[e].get(sem, 0) < val:
+                eng[e].wait_ge(T.sem[sem], val)
+                known[e][sem] = val
+                for k, c in clock.items():
+                    known[e][k] = max(known[e].get(k, 0), c)
+
+    def before(e, reads, writes):
+        toks = []
+        for a in reads:
+            for b, kind, tok, f in hist.get(a[0], []):
+                if kind == "w" and meet(a, b):
+                    toks.append(tok)
+        for a in writes:
+            for b, kind, tok, f in hist.get(a[0], []):
+                if meet(a, b) and (kind == "w" or f != e):
+                    toks.append(tok)
+        need(e, toks)
+
+    def note(e, reads, writes, tok):
+        for a in writes:
+            hist[a[0]] = [h for h in hist.get(a[0], []) if not inside(h[0], a)] + [(a, "w", tok, e)]
+        for a in reads:
+            hist[a[0]] = [h for h in hist.get(a[0], []) if not (h[1] == "r" and h[3] == e and inside(h[0], a))] + [(a, "r", tok, e)]
+
+    def token(sem, clock):
+        seq[0] += 1
+        return (sem, cnt[sem], dict(clock), seq[0])
+
+    def op(e, fn, reads, writes):
+        before(e, reads, writes)
+        sem = own[e]
+        cnt[sem] = cnt.get(sem, 0) + 1
+        fn().then_inc(T.sem[sem], 1)
+        note(e, reads, writes, token(sem, known[e]))
+
+    def dmas(sem, lst):
+        for e, out, in_, reads, writes in lst:
+            before(e, reads, writes)
+            cnt[sem] = cnt.get(sem, 0) + 16
+            eng[e].dma_start(out, in_).then_inc(T.sem[sem], 16)
+        for e, out, in_, reads, writes in lst:
+            note("dma", reads, writes, token(sem, {}))
+
+    def ap(q):
+        name, c0, c1, p0, p1, st = q
+        return T[name][p0:p1, c0:c1] if st == 1 else T[name][p0:p1, c0:c1:st]
+
+    def tup(*xs):
+        return [x for x in xs if isinstance(x, tuple)]
+
+    def sv(x):
+        return ap(x) if isinstance(x, tuple) else x
+
+    def ts(out, a, s1, op0, s2=None, op1=None):
+        if op1 is None:
+            op("v", lambda: g.vector.tensor_scalar(ap(out), ap(a), sv(s1), None, op0), [a] + tup(s1), [out])
+        else:
+            op("v", lambda: g.vector.tensor_scalar(ap(out), ap(a), sv(s1), sv(s2), op0, op1), [a] + tup(s1, s2), [out])
+
+    def tt(out, a, b, o):
+        op("v", lambda: g.vector.tensor_tensor(ap(out), ap(a), ap(b), o), [a, b], [out])
+
+    def red(out, a, o, absolute=False):
+        if absolute:
+            op("v", lambda: g.vector.tensor_reduce(ap(out), ap(a), AxisListType.X, o, apply_absolute_value=True), [a], [out])
+        else:
+            op("v", lambda: g.vector.tensor_reduce(ap(out), ap(a), AxisListType.X, o), [a], [out])
+
+    def cp(out, a):
+        op("v", lambda: g.vector.tensor_copy(ap(out), ap(a)), [a], [out])
+
+    def tr(out, a):
+        op("v", lambda: g.vector.transpose(ap(out), ap(a)), [a], [out])
+
+    def scan(out, a, b, init, o0, o1):
+        op("v", lambda: g.vector.tensor_tensor_scan(ap(out), ap(a), ap(b), init, o0, o1), [a, b], [out])
+
+    def fill(out, c):
+        op("v", lambda: g.vector.memset(ap(out), c), [], [out])
+
+    def act(out, a, func, bias=0.0, scale=1.0, accum=None):
+        w = [out] + tup(accum)
+        op("s", lambda: g.scalar.activation(ap(out), ap(a), func, bias=sv(bias), scale=sv(scale), accum_out=None if accum is None else ap(accum)),
+           [a] + tup(bias, scale), w)
+
+    def quant(c, s, a, b, src, x0, x1):
+        op("v", lambda: g.vector.quantize_mx(T[c][:, a:b], T[s][:, a:b], T[src][:, x0:x1]), [r(src, x0, x1)], [r(c, a, b), r(s, a, b)])
+
+    def pick(c2, a2, c1, w, off, o0, o1):
+        k = 16 * (o1 - o0)
+        s2, s1 = c2 + "s", c1 + "s"
+        op("v", lambda: g.vector.tensor_copy(T[c2][:, a2:a2 + k].bitcast(dt.uint32), T[c1][:, 0:w].bitcast(dt.uint32).indirect(T[off][:, o0:o1])),
+           [r(c1, 0, w), r(off, o0, o1)], [r(c2, a2, a2 + k)])
+        op("s", lambda: g.scalar.activation(T[s2][:, a2:a2 + k], T[s1][:, 0:w].indirect(T[off][:, o0:o1]), Fn.Copy),
+           [r(s1, 0, w), r(off, o0, o1)], [r(s2, a2, a2 + k)])
+
+    def mm(out, bank, width, c1, a1, c2, a2, start, stop):
+        op("p", lambda: g.tensor.matmul_mx(T[out][:, 512 * bank:512 * bank + width], T[c1][:, a1:a1 + 128], T[c1 + "s"][:, a1:a1 + 128],
+                                           T[c2][:, a2:a2 + width], T[c2 + "s"][:, a2:a2 + width], start, stop),
+           [r(c1, a1, a1 + 128), r(c1 + "s", a1, a1 + 128), r(c2, a2, a2 + width), r(c2 + "s", a2, a2 + width)],
+           [r(out, 512 * bank, 512 * bank + 512)] if start else [])
+        if not start:
+            note("p", [], [r(out, 512 * bank, 512 * bank + 512)], token("p", known["p"]))
+
+    far = [q for q in range(n) if q != rank and topo.chip(cores[q]) != topo.chip(core)]
+    near = [q for q in range(n) if q != rank and topo.chip(cores[q]) == topo.chip(core)]
+    fe = topo.engines(core, cores[far[0]])
+    ne = [e for e in topo.engines(core, cores[near[0]]) if e not in fe] if near else []
+
+    def dest(q):
+        a = topo.addr(cores[q])
+        return DstId(rid=a[0], pnc=a[1])
+
+    def send(sem, src, dst_of, reads):
+        before("g", reads, [])
+        ts_ = []
+        for qs, es in ((far, fe), (near, ne)):
+            if qs:
+                ts_.append(RemoteDMATransfer(dst_ids=[dest(q) for q in qs], dma_engine_mask=sum(1 << e for e in es), remote_sem=T.sem[sem],
+                                             srcs=[src], dsts=[dst_of((rank - q - 1) % n) for q in qs], alu_op=0))
+                cnt["sent"] = cnt.get("sent", 0) + len(es)
+        g.remote_dma_fused(ts_, local_sem=T.sem["sent"])
+
+    arrive = len(fe) * len(far) + len(ne) * len(near)
+
+    def landed(sem, total, regions):
+        cnt[sem] = total
+        seq[0] += 1
+        for a in regions:
+            note("far", [], [a], (sem, total, {}, seq[0]))
+
+    def send_list(t):
+        send("arl%d" % t, T["my%d" % t][:, 0:1], lambda m: T["land%d" % t][:, m:m + 1], [r("my%d" % t, 0, 1)])
+        landed("arl%d" % t, arrive, [r("land%d" % t, 0, 7)])
+
+    def send_cols(t):
+        c, b = "comb%d" % t, P * t
+        o = b + 224
+        send("arc%d" % t, T[c][:, o:o + S].bitcast(dt.uint8), lambda m: T[c][:, b + S * m:b + S * m + S].bitcast(dt.uint8), [r(c, o, o + S)])
+        send("arc%d" % t, T[c + "s"][:, o:o + S], lambda m: T[c + "s"][:, b + S * m:b + S * m + S], [r(c + "s", o, o + S)])
+        landed("arc%d" % t, 2 * arrive, [r(c, b, b + 224), r(c + "s", b, b + 224)])
+
+    sdl = [(16 * a, T.sdw[16 * a:16 * a + 16, :], r("sdw", 0, 2, 16 * a, 16 * a + 16)) for a in range(8)]
+    dmas("dx", [("s", T.xt[:], T.x[:], [], [r("xt", 0, 1024)])])
+    dmas("dsd", [("y" if i % 2 == 0 else "s", o, T.sd[:], [], [w]) for i, (a, o, w) in enumerate(sdl)])
+    dmas("dnb", [("y", T.nbw[16 * a:16 * a + 16, :], T.nb[:], [], [r("nbw", 0, 64, 16 * a, 16 * a + 16)]) for a in range(8)])
+    dmas("dw", [("y", T.wt[:], T.w[:], [], [r("wt", 0, 1024)])])
+
+    op("g", lambda: g.iota(T.pint[:], [[0, 1]], 0, 1), [], [r("pint", 0, 1)])
+    op("g", lambda: g.iota(T.pidx[:], [[0, 1]], 0, 1, allow_small_or_imprecise_dtypes=True), [], [r("pidx", 0, 1)])
+    op("g", lambda: g.iota(T.icol[:], [[1, 128]], 0, 0, allow_small_or_imprecise_dtypes=True), [], [r("icol", 0, 128)])
+    op("g", lambda: g.iota(T.ic64[:], [[128, 2], [1, 32]], 0, 0, allow_small_or_imprecise_dtypes=True), [], [r("ic64", 0, 64)])
+    op("g", lambda: g.iota(T.ici[:], [[1, 256]], 0, 0), [], [r("ici", 0, 256)])
+    pint, pidx = r("pint", 0, 1), r("pidx", 0, 1)
+    ci = lambda i: r("ci", i, i + 1)
+    cf = lambda i: r("cf", i, i + 1)
+    fill(r("ones32", 0, 32), 1.0)
+    fill(r("ones", 0, 256), 1.0)
+    fill(r("c19", 0, 32), float(2 ** 19))
+    ts(ci(0), pint, 31, Op.bitwise_and)
+    ts(ci(1), pint, 15, Op.bitwise_and)
+    ts(ci(2), pint, 96, Op.bitwise_and)
+    ts(ci(3), pint, 32, Op.bitwise_and)
+    ts(ci(4), pint, 64, Op.bitwise_and)
+    cp(r("cf", 0, 5), r("ci", 0, 5))
+    ts(cf(5), cf(0), 16.0, Op.is_ge)
+    ts(cf(6), cf(0), float(2 ** 19), Op.mult)
+    cp(cf(8), pidx)
+    ts(cf(9), pidx, 128.0, Op.add)
+    place = lambda h: r("cf", 8 + h, 9 + h)
+    place2 = r("cf", 8, 10)
+
+    cp(r("sdu", 0, 2), r("sdw", 0, 2))
+    cp(r("sdf", 0, 2), r("sdw", 0, 2))
+    tt(r("sdf", 2, 3), r("sdf", 1, 2), r("sdf", 0, 1), Op.subtract)
+    ts(r("sdf", 3, 4), r("sdf", 2, 3), cf(5), Op.mult, r("sdf", 0, 1), Op.add)
+    ts(r("my0", 0, 1), r("sdf", 3, 4), float(P * rank), Op.add)
+    send_list(0)
+    quant("qx", "qxs", 0, 256, "xt", 0, 1024)
+    pick("comb0", 224, "qx", 256, "sdu", 0, 2)
+    send_cols(0)
+
+    ts(ci(5), pint, 3, Op.bitwise_and)
+    ts(ci(6), pint, 4, Op.bitwise_and)
+    ts(ci(7), pint, 4, Op.arith_shift_right)
+    cp(r("cf", 16, 19), r("ci", 5, 8))
+    ts(cf(19), cf(16), 16.0, Op.mult, cf(18), Op.add)
+    ts(cf(20), cf(17), 2.0, Op.mult, cf(19), Op.add)
+    cp(r("nbof", 0, 1), cf(20))
+    cp(r("nbof", 1, 2), cf(20))
+    op("v", lambda: g.vector.tensor_copy(T.nbo[:, 0:16], T.nbw[:, 0:64].indirect(T.nbof[:, 0:1])), [r("nbw", 0, 64), r("nbof", 0, 1)], [r("nbo", 0, 16)])
+    nbo = r("nbo", 0, 8)
+    ts(r("rpa", 0, 32), r("ones32", 0, 32), r("sdf", 3, 4), Op.mult)
+    tr(r("tb", 0, 32), r("rpa", 0, 32))
+    for h in (0, 1):
+        ts(r("rpb", 32 * h, 32 * h + 32), r("tb", 0, 32), place(h), Op.is_equal)
+        red(r("tk", h, h + 1), r("rpb", 32 * h, 32 * h + 32), Op.add)
+    fill(r("sb", 0, 16), -9e29)
+    fill(r("pl8", 0, 8), -1e5)
+
+    def settle(first):
+        if first:
+            ts(r("nf", 0, 2), r("tk", 0, 2), -1.0, Op.mult, 1.0, Op.add)
+        else:
+            tt(r("nf", 0, 2), r("nf", 0, 2), r("tk", 0, 2), Op.subtract)
+        ts(r("nfm", 0, 2), r("nf", 0, 2), -1.0, Op.add)
+        ts(r("fx", 0, 2), r("nfm", 0, 2), 9e29, Op.mult)
+        for h in (0, 1):
+            ts(r("nbx", 4 * h, 4 * h + 4), r("nbo", 4 * h, 4 * h + 4), r("nf", h, h + 1), Op.mult, r("nfm", h, h + 1), Op.add)
+        for h in (0, 1):
+            ts(r("sb", 8 * h, 8 * h + 4), r("sb", 8 * h, 8 * h + 4), r("nf", h, h + 1), Op.mult, r("fx", h, h + 1), Op.add)
+
+    settle(True)
+    for k in range(4):
+        fill(r("c8", k, 8, st=4), float((3 - k) * 1024 - 100000))
+
+    def masks(t):
+        for m in range(8):
+            src = r("my%d" % t, 0, 1) if m == 7 else r("land%d" % t, m, m + 1)
+            ts(r("rpf", 32 * m, 32 * m + 32), r("ones32", 0, 32), src, Op.mult)
+        tr(r("ff", 0, 256), r("rpf", 0, 256))
+        for i in range(8):
+            ts(r("eqx", 256 * i, 256 * i + 256), r("ff", 0, 256), r("nbx", i, i + 1), Op.is_equal, 256.0, Op.mult)
+        for i in range(8):
+            scan(r("sc", 256 * i, 256 * i + 256), r("eqx", 256 * i, 256 * i + 256), r("ones", 0, 256), 0.0, Op.max, Op.subtract)
+        pos = r("sc", 255, 2048, st=256)
+        ts(r("pkb", 0, 8), pos, 0.0, Op.is_lt, -9e29 / 256, Op.mult)
+        ts(r("t8", 0, 8), pos, 0.0, Op.is_ge, float(100000 + 256 * t), Op.mult)
+        tt(r("u8", 0, 8), r("t8", 0, 8), pos, Op.add)
+        tt(r("t8", 0, 8), r("u8", 0, 8), r("c8", 0, 8), Op.add)
+        tt(r("pl8", 0, 8), r("pl8", 0, 8), r("t8", 0, 8), Op.max)
+
+    fill(r("et", 0, 2048), 0.0)
+    for b in range(4):
+        ts(r("et", 512 * b + b, 512 * b + 512, st=4), r("icol", 0, 128), pidx, Op.is_equal)
+        quant("eq", "eqs", 128 * b, 128 * b + 128, "et", 512 * b, 512 * b + 512)
+    fill(r("ht", 0, 512), 0.0)
+    quant("pko", "pkos", 0, 128, "xt", 0, 512)
+    quant("pkp", "pkps", 0, 128, "xt", 0, 512)
+    cp(r("plm", 0, 1), cf(2))
+    ts(cf(21), cf(3), -2.0, Op.mult, cf(2), Op.add)
+    ts(cf(22), cf(4), -2.0, Op.mult, cf(2), Op.add)
+    ts(cf(23), cf(4), -2.0, Op.mult, cf(21), Op.add)
+    for d, b in enumerate((2, 21, 22, 23)):
+        ts(r("plm", 64 * d, 64 * d + 64), r("ic64", 0, 64), cf(b), Op.add, float(32 * d), Op.add)
+    for h in (0, 1):
+        ts(r("thr", 256 * h, 256 * h + 256), r("plm", 0, 256), place(h), Op.is_lt, 2.0 ** -120, Op.mult)
+    ts(cf(24), cf(1), 16.0, Op.add)
+    for i, c in enumerate((1, 24, 0)):
+        ts(r("dg", 32 * i, 32 * i + 32), r("icol", 0, 32), cf(c), Op.not_equal, float(2 ** 22), Op.mult)
+    masks(0)
+    cp(r("fl", 0, 2), place2)
+    ts(r("w2", 0, 2), place2, float(P * rank + 1), Op.add)
+    tt(r("w3", 0, 2), r("w2", 0, 2), r("tk", 0, 2), Op.mult)
+    ts(r("pa2", 0, 2), r("w3", 0, 2), -1.0, Op.add)
+
+    def late():
+        quant("finw", "finws", 0, 256, "xt", 0, 1024)
+        quant("qw", "qws", 0, 256, "wt", 0, 1024)
+        ts(r("icj", 0, 256), r("ici", 0, 256), 15, Op.bitwise_and)
+        ts(r("m16", 0, 256), r("icj", 0, 256), cf(1), Op.is_equal)
+        ts(r("seg", 0, 256), r("icj", 0, 256), 0.0, Op.not_equal)
+
+    def spread(buf, w):
+        for b in range(4):
+            cp(r(buf, w, 2 * w, 32 * b, 32 * b + 32), r(buf, 0, w, 32 * (b ^ 1), 32 * (b ^ 1) + 32))
+        for b in (0, 1):
+            cp(r(buf, 2 * w, 4 * w, 64 * b, 64 * b + 64), r(buf, 0, 2 * w, 64 * (1 - b), 64 * (1 - b) + 64))
+
+    for t in range(R):
+        c = "comb%d" % t
+        for h in (0, 1):
+            mm("zz", h, 256, "qx", 128 * h, c, P * t, True, True)
+        for i in range(8):
+            h, k = i // 4, i % 4
+            blk = r("prod", 256 * i, 256 * i + 256)
+            tt(blk, r("zz", 512 * h, 512 * h + 256), r("eqx", 256 * i, 256 * i + 256), Op.mult)
+            act(blk, blk, Fn.Identity, bias=r("pkb", i, i + 1), scale=1.0 / 256, accum=r("sb", 8 * h + 4 + k, 8 * h + 5 + k))
+        if t < R - 1:
+            lst = []
+            for t2 in range(t + 1, R):
+                d = "comb%d" % t2
+                for s, cast in (("", True), ("s", False)):
+                    i_, o_ = T[c + s][:, P * t:P * t + P], T[d + s][:, P * t:P * t + P]
+                    lst.append(("y", o_.bitcast(dt.uint8) if cast else o_, i_.bitcast(dt.uint8) if cast else i_,
+                                [r(c + s, P * t, P * t + P)], [r(d + s, P * t, P * t + P)]))
+            dmas("dc%d" % t, lst)
+        for h in (0, 1):
+            red(r("bst", h, h + 1), r("sb", 8 * h, 8 * h + 8), Op.max)
+        for h in (0, 1):
+            ts(r("rpa", 32 * h, 32 * h + 32), r("ones32", 0, 32), r("bst", h, h + 1), Op.mult)
+        tr(r("row", 0, 64), r("rpa", 0, 64))
+        spread("row", 64)
+        for h in (0, 1):
+            act(r("ed", 256 * h, 256 * h + 256), r("row", 0, 256), Fn.Identity, bias=r("bst", h, h + 1), scale=-1.0)
+        ts(r("ib", 0, 2), r("bst", 0, 2), -5e29, Op.is_lt, 4.0, Op.mult)
+        for h in (0, 1):
+            tt(r("sb", 8 * h, 8 * h + 4), r("sb", 8 * h, 8 * h + 4), r("sb", 8 * h + 4, 8 * h + 8), Op.max)
+        for h in (0, 1):
+            ts(r("e8", 4 * h, 4 * h + 4), r("sb", 8 * h, 8 * h + 4), r("bst", h, h + 1), Op.is_equal)
+        for h in (0, 1):
+            x = r("cm", 256 * h, 256 * h + 256)
+            tt(x, r("ed", 256 * h, 256 * h + 256), r("thr", 256 * h, 256 * h + 256), Op.is_lt)
+            act(x, x, Fn.Identity, bias=r("ib", h, h + 1), accum=r("rk", h, h + 1))
+        tt(r("t8", 0, 8), r("e8", 0, 8), r("pl8", 0, 8), Op.mult)
+        for h in (0, 1):
+            red(r("q2", h, h + 1), r("t8", 4 * h, 4 * h + 4), Op.max)
+        cp(r("qi", 0, 2), r("q2", 0, 2))
+        ts(r("qi", 2, 4), r("qi", 0, 2), 1023, Op.bitwise_and)
+        for h in (0, 1):
+            ts(r("pay", h, h + 1), r("qi", 2 + h, 3 + h), 256.0, Op.mult, place(h), Op.add)
+        for h in (0, 1):
+            ts(r("rpb", 32 * h, 32 * h + 32), r("c19", 0, 32), r("rk", h, h + 1), Op.mult, r("pay", h, h + 1), Op.add)
+        tr(r("tb", 0, 64), r("rpb", 0, 64))
+        ts(r("rpb", 0, 64), r("tb", 0, 64), cf(6), Op.subtract)
+        red(r("part", 0, 1), r("rpb", 0, 64), Op.min, absolute=True)
+        ts(r("rpc", 0, 32), r("ones32", 0, 32), r("part", 0, 1), Op.mult)
+        tr(r("p4", 0, 32), r("rpc", 0, 32))
+        spread("p4", 32)
+        tt(r("l64", 0, 64), r("p4", 0, 64), r("p4", 64, 128), Op.min)
+        tt(r("l32", 0, 32), r("l64", 0, 32), r("l64", 32, 64), Op.min)
+        for i in range(3):
+            tt(r("dd", 32 * i, 32 * i + 32), r("l32", 0, 32), r("dg", 32 * i, 32 * i + 32), Op.add)
+        for i in range(3):
+            red(r("vals", i, i + 1), r("dd", 32 * i, 32 * i + 32), Op.min)
+        ts(r("okv", 0, 3), r("vals", 0, 3), float(2 ** 18), Op.is_lt)
+        tt(r("vz", 0, 3), r("vals", 0, 3), r("okv", 0, 3), Op.mult)
+        cp(r("vi", 0, 3), r("vz", 0, 3))
+        ts(r("vi", 4, 7), r("vi", 0, 3), 255, Op.bitwise_and)
+        ts(r("vi", 8, 10), r("vi", 0, 2), 8, Op.arith_shift_right)
+        cp(r("offu", 0, 2), r("vi", 4, 6))
+        cp(r("offu", 2, 4), r("vi", 8, 10))
+        pick("pko", 0, "qx", 256, "offu", 0, 2)
+        pick("pkp", 0, c, P * t + P, "offu", 2, 4)
+        if t < R - 1:
+            my = "my%d" % (t + 1)
+            ts(r("vz", 3, 4), r("okv", 2, 3), float(P * rank + 7), Op.mult, -7.0, Op.add)
+            tt(r(my, 0, 1), r("vi", 6, 7), r("vz", 3, 4), Op.add)
+            send_list(t + 1)
+        for b in range(4):
+            mm("dec", b, 128, "eq", 128 * b, "pko", 0, True, False)
+        for b in range(4):
+            mm("dec", b, 128, "eq", 128 * b, "pkp", 0, False, True)
+        ts(r("tk", 0, 2), r("rk", 0, 2), 31.5, Op.is_lt)
+        ts(r("w2", 0, 2), r("rk", 0, 2), float(P + S * t), Op.add)
+        tt(r("w3", 0, 2), r("w2", 0, 2), place2, Op.subtract)
+        tt(r("w2", 0, 2), r("w3", 0, 2), r("tk", 0, 2), Op.mult)
+        tt(r("fl", 0, 2), r("fl", 0, 2), r("w2", 0, 2), Op.add)
+        if t == R - 1:
+            for h in (0, 1):
+                ts(r("rpd", 32 * h, 32 * h + 32), r("ones32", 0, 32), r("fl", h, h + 1), Op.mult)
+            tr(r("flt", 0, 64), r("rpd", 0, 64))
+            for a in range(4):
+                i_, o_ = r("flt", 0, 64, 32 * a, 32 * a + 1), r("flr", 64 * a, 64 * a + 64)
+                op("g", lambda: g.partition_broadcast(ap(o_), ap(i_), 128), [i_], [o_])
+        for b in range(4):
+            o_, i_ = r("ht", b, 128, st=4), r("dec", 512 * b, 512 * b + 32)
+            if b < 2:
+                ts(o_, i_, 0.5, Op.mult)
+            else:
+                act(o_, i_, Fn.Copy, scale=0.5)
+        if t < R - 1:
+            d, o = "comb%d" % (t + 1), P * (t + 1) + 224
+            quant(d, d + "s", o, o + 128, "ht", 0, 512)
+            send_cols(t + 1)
+            f = P + S * t
+            dmas("df%d" % t, [("y", T.finw[:, f:f + S].bitcast(dt.uint8), T[d][:, o:o + S].bitcast(dt.uint8), [r(d, o, o + S)], [r("finw", f, f + S)]),
+                              ("y", T.finws[:, f:f + S], T[d + "s"][:, o:o + S], [r(d + "s", o, o + S)], [r("finws", f, f + S)])])
+        else:
+            quant("finw", "finws", 320, 448, "ht", 0, 512)
+        def parents():
+            for h in (0, 1):
+                ts(r("e8", 4 * h, 4 * h + 4), r("pl8", 4 * h, 4 * h + 4), r("q2", h, h + 1), Op.is_equal)
+            tt(r("u8", 0, 8), r("e8", 0, 8), nbo, Op.mult)
+            for h in (0, 1):
+                red(r("w2", h, h + 1), r("u8", 4 * h, 4 * h + 4), Op.add)
+            tt(r("w3", 0, 2), r("w2", 0, 2), r("pa2", 0, 2), Op.subtract)
+            tt(r("w2", 0, 2), r("w3", 0, 2), r("tk", 0, 2), Op.mult)
+            tt(r("pa2", 0, 2), r("pa2", 0, 2), r("w2", 0, 2), Op.add)
+        parents()
+        if t < R - 1:
+            settle(False)
+            masks(t + 1)
+            if t == 0:
+                late()
+
+    dmas("dpa", [("y", T.pa[0:1, 128 * h:128 * h + 128], T.pa2[:, h:h + 1], [r("pa2", h, h + 1)], []) for h in (0, 1)])
+    tt(r("flm", 0, 256), r("flr", 0, 256), r("m16", 0, 256), Op.mult)
+    scan(r("fls", 0, 256), r("seg", 0, 256), r("flm", 0, 256), 0.0, Op.mult, Op.add)
+    for h in (0, 1):
+        for u in (0, 1):
+            cp(r("fo", 8 * h + u, 8 * h + 8, st=2), r("fls", (2 * h + u) * 16 + 15, 256, st=64))
+    pick("fin", 0, "finw", 352, "fo", 0, 16)
+    for o in (0, 1):
+        mm("yy", o, 256, "qw", 128 * o, "fin", 0, True, True)
+    lst = [("y", T.oc[:], T.fin[:].bitcast(dt.uint8), [r("fin", 0, 256)], [])]
+    lst += [("y", T.osc[4 * k:4 * k + 4, :], T.fins[32 * k:32 * k + 4, :], [r("fins", 0, 256)], []) for k in range(4)]
+    cp(r("sy", 0, 256), r("yy", 0, 256))
+    act(r("sy", 256, 512), r("yy", 512, 768), Fn.Copy)
+    lst += [("y", T.y[:, 0:256], T.sy[:, 0:256], [r("sy", 0, 256)], []), ("s", T.y[:, 256:512], T.sy[:, 256:512], [r("sy", 256, 512)], [])]
+    dmas("dout", lst)
+    for sem in cnt:
+        if known["g"].get(sem, 0) < cnt[sem]:
+            g.wait_ge(T.sem[sem], cnt[sem])

@@ -3,45 +3,44 @@ from concourse.bass import DstId, RemoteDMATransfer
 from concourse.mybir import dt, AluOpType as Op, AxisListType, ActivationFunctionType as Fn
 
 F8 = "float8_e4m3fn_x4"
-W1, W2, WF = 608, 864, 448
+W0, W1, W2, WF = 352, 608, 864, 448
 SCRATCH = {
     "xt": ("sbuf", [128, 1024], "bfloat16"), "wt": ("sbuf", [128, 1024], "bfloat16"),
     "qx": ("sbuf", [128, 256], F8), "qxs": ("sbuf", [128, 256], "uint8"),
     "qw": ("sbuf", [128, 256], F8), "qws": ("sbuf", [128, 256], "uint8"),
     "et": ("sbuf", [128, 2048], "bfloat16"), "eq": ("sbuf", [128, 512], F8), "eqs": ("sbuf", [128, 512], "uint8"),
-    "comb0": ("sbuf", [128, 256], F8), "comb0s": ("sbuf", [128, 256], "uint8"),
+    "comb0": ("sbuf", [128, W0], F8), "comb0s": ("sbuf", [128, W0], "uint8"),
     "comb1": ("sbuf", [128, W1], F8), "comb1s": ("sbuf", [128, W1], "uint8"),
     "comb2": ("sbuf", [128, W2], F8), "comb2s": ("sbuf", [128, W2], "uint8"),
     "finw": ("sbuf", [128, WF], F8), "finws": ("sbuf", [128, WF], "uint8"),
     "fin": ("sbuf", [128, 256], F8), "fins": ("sbuf", [128, 256], "uint8"),
-    "pko": ("sbuf", [128, 128], F8), "pkos": ("sbuf", [128, 128], "uint8"),
-    "pkp": ("sbuf", [128, 128], F8), "pkps": ("sbuf", [128, 128], "uint8"),
-    "ht": ("sbuf", [128, 512], "bfloat16"),
+    "pk": ("sbuf", [128, 128], F8), "pks": ("sbuf", [128, 128], "uint8"),
+    "ht": ("sbuf", [128, 512], "bfloat16"), "od": ("sbuf", [128, 128], "float32"),
     "sdw": ("sbuf", [128, 2], "int32"), "nbw": ("sbuf", [128, 64], "int32"),
     "sdu": ("sbuf", [128, 2], "uint16"), "sdf": ("sbuf", [128, 4], "float32"),
-    "nbofi": ("sbuf", [128, 4], "int32"), "nbof": ("sbuf", [128, 2], "uint16"), "nbo": ("sbuf", [128, 16], "float32"),
-    "nbx": ("sbuf", [128, 8], "float32"),
+    "nbof": ("sbuf", [128, 2], "uint16"), "nbo": ("sbuf", [128, 16], "float32"), "nbx": ("sbuf", [128, 8], "float32"),
     "pint": ("sbuf", [128, 1], "int32"), "pidx": ("sbuf", [128, 1], "float32"), "icol": ("sbuf", [128, 128], "float32"),
-    "ici": ("sbuf", [128, 256], "int32"), "icj": ("sbuf", [128, 256], "int32"), "ic64": ("sbuf", [128, 64], "float32"),
-    "ci": ("sbuf", [128, 16], "int32"), "cf": ("sbuf", [128, 32], "float32"),
-    "plm": ("sbuf", [128, 256], "float32"), "thr": ("sbuf", [128, 512], "bfloat16"),
-    "ones32": ("sbuf", [128, 32], "float32"), "c19": ("sbuf", [128, 32], "float32"), "ones": ("sbuf", [128, 256], "bfloat16"),
-    "dg": ("sbuf", [128, 96], "float32"), "m16": ("sbuf", [128, 256], "float32"), "seg": ("sbuf", [128, 256], "float32"),
-    "c8": ("sbuf", [128, 8], "float32"),
+    "c16": ("sbuf", [128, 256], "float32"), "kk8": ("sbuf", [128, 8], "float32"), "plc": ("sbuf", [128, 8], "float32"),
+    "ic64": ("sbuf", [128, 64], "float32"), "ci": ("sbuf", [128, 16], "int32"), "cf": ("sbuf", [128, 32], "float32"),
+    "plm": ("sbuf", [128, 256], "float32"), "ste": ("sbuf", [128, 512], "bfloat16"),
+    "ones32": ("sbuf", [128, 32], "float32"), "c19": ("sbuf", [128, 32], "float32"), "ones": ("sbuf", [128, 2048], "bfloat16"),
+    "m16": ("sbuf", [128, 256], "float32"), "seg": ("sbuf", [128, 256], "float32"), "c8": ("sbuf", [128, 8], "float32"),
     "my0": ("sbuf", [128, 4], "float32"), "my1": ("sbuf", [128, 4], "float32"), "my2": ("sbuf", [128, 4], "float32"),
     "land0": ("sbuf", [128, 8], "float32"), "land1": ("sbuf", [128, 8], "float32"), "land2": ("sbuf", [128, 8], "float32"),
     "rpf": ("sbuf", [128, 256], "float16"), "ff": ("sbuf", [128, 256], "float16"),
     "eqx": ("sbuf", [128, 2048], "bfloat16"), "sc": ("sbuf", [128, 2048], "bfloat16"), "prod": ("sbuf", [128, 2048], "float32"),
+    "m8": ("sbuf", [128, 8], "float32"), "n8": ("sbuf", [128, 8], "float32"), "o8": ("sbuf", [128, 8], "float32"),
     "t8": ("sbuf", [128, 8], "float32"), "u8": ("sbuf", [128, 8], "float32"), "pl8": ("sbuf", [128, 8], "float32"),
-    "pkb": ("sbuf", [128, 8], "float32"), "sb": ("sbuf", [128, 16], "float32"), "bst": ("sbuf", [128, 2], "float32"),
+    "pkb": ("sbuf", [128, 8], "float32"), "pkc": ("sbuf", [128, 8], "float32"), "prc": ("sbuf", [128, 512], "float32"),
+    "sb": ("sbuf", [128, 16], "float32"), "sb1": ("sbuf", [128, 8], "float32"), "bst": ("sbuf", [128, 2], "float32"),
     "ib": ("sbuf", [128, 2], "float32"), "rpa": ("sbuf", [128, 64], "float32"), "row": ("sbuf", [128, 256], "float32"),
-    "ed": ("sbuf", [128, 512], "bfloat16"), "cm": ("sbuf", [128, 512], "bfloat16"), "rk": ("sbuf", [128, 2], "float32"),
+    "ed": ("sbuf", [128, 1024], "bfloat16"), "cm": ("sbuf", [128, 1024], "bfloat16"), "sg": ("sbuf", [128, 512], "bfloat16"),
+    "rs": ("sbuf", [128, 2], "float32"), "rk": ("sbuf", [128, 2], "float32"),
     "e8": ("sbuf", [128, 8], "float32"), "q2": ("sbuf", [128, 2], "float32"), "qi": ("sbuf", [128, 4], "int32"),
+    "qs": ("sbuf", [128, 2], "float32"), "x2": ("sbuf", [128, 2], "float32"), "y2": ("sbuf", [128, 2], "float32"),
     "pay": ("sbuf", [128, 2], "float32"), "rpb": ("sbuf", [128, 64], "float32"), "tb": ("sbuf", [128, 64], "float32"),
-    "part": ("sbuf", [128, 1], "float32"), "rpc": ("sbuf", [128, 32], "float32"), "p4": ("sbuf", [128, 128], "float32"),
-    "l64": ("sbuf", [128, 64], "float32"), "l32": ("sbuf", [128, 32], "float32"), "dd": ("sbuf", [128, 96], "float32"),
-    "vals": ("sbuf", [128, 4], "float32"), "okv": ("sbuf", [128, 4], "float32"), "vz": ("sbuf", [128, 4], "float32"),
-    "vi": ("sbuf", [128, 12], "int32"), "offu": ("sbuf", [128, 4], "uint16"),
+    "pt": ("sbuf", [128, 8], "float32"), "dx": ("sbuf", [128, 128], "float32"),
+    "vz": ("sbuf", [128, 8], "float32"), "vi": ("sbuf", [128, 12], "int32"), "offu": ("sbuf", [128, 4], "uint16"),
     "tk": ("sbuf", [128, 2], "float32"), "nf": ("sbuf", [128, 2], "float32"), "nfm": ("sbuf", [128, 2], "float32"),
     "fx": ("sbuf", [128, 2], "float32"), "fl": ("sbuf", [128, 2], "float32"), "pa2": ("sbuf", [128, 2], "float32"),
     "w2": ("sbuf", [128, 2], "float32"), "w3": ("sbuf", [128, 2], "float32"), "rpd": ("sbuf", [128, 64], "float32"),
@@ -50,7 +49,7 @@ SCRATCH = {
     "dec": ("psum", [128, 2048], "float32"), "zz": ("psum", [128, 1024], "float32"), "yy": ("psum", [128, 1024], "float32"),
 }
 SEMAPHORES = ["v", "s", "p", "gp", "dsd", "dx", "dnb", "dw", "arl0", "arl1", "arl2", "arc0", "arc1", "arc2",
-              "dc0", "dc1", "df0", "df1", "dout", "dpa", "sent"]
+              "arn0", "arn1", "arn2", "dc0", "dc1", "df0", "df1", "dfx", "dout", "dpa", "sent"]
 
 
 def r(name, c0, c1, p0=0, p1=128, st=1):
@@ -98,7 +97,7 @@ def rank_program(g, core, T, topo):
                     toks.append(tok)
         for a in writes:
             for b, kind, tok, f in hist.get(a[0], []):
-                if meet(a, b) and (kind == "w" or f != e):
+                if meet(a, b):
                     toks.append(tok)
         need(e, toks)
 
@@ -125,7 +124,7 @@ def rank_program(g, core, T, topo):
             cnt[sem] = cnt.get(sem, 0) + 16
             eng[e].dma_start(out, in_).then_inc(T.sem[sem], 16)
         for e, out, in_, reads, writes in lst:
-            note("dma", reads, writes, token(sem, {}))
+            note(sem, reads, writes, token(sem, {}))
 
     def ap(q):
         name, c0, c1, p0, p1, st = q
@@ -164,6 +163,12 @@ def rank_program(g, core, T, topo):
     def fill(out, c):
         op("v", lambda: g.vector.memset(ap(out), c), [], [out])
 
+    def iota(out, pattern, base, cm, flag=True):
+        if flag:
+            op("g", lambda: g.iota(ap(out), pattern, base, cm, allow_small_or_imprecise_dtypes=True), [], [out])
+        else:
+            op("g", lambda: g.iota(ap(out), pattern, base, cm), [], [out])
+
     def act(out, a, func, bias=0.0, scale=1.0, accum=None):
         w = [out] + tup(accum)
         op("s", lambda: g.scalar.activation(ap(out), ap(a), func, bias=sv(bias), scale=sv(scale), accum_out=None if accum is None else ap(accum)),
@@ -180,34 +185,33 @@ def rank_program(g, core, T, topo):
         op("s", lambda: g.scalar.activation(T[s2][:, a2:a2 + k], T[s1][:, 0:w].indirect(T[off][:, o0:o1]), Fn.Copy),
            [r(s1, 0, w), r(off, o0, o1)], [r(s2, a2, a2 + k)])
 
-    def mm(out, bank, width, c1, a1, c2, a2, start, stop):
+    def mm(out, bank, width, c1, a1, c2, a2):
         op("p", lambda: g.tensor.matmul_mx(T[out][:, 512 * bank:512 * bank + width], T[c1][:, a1:a1 + 128], T[c1 + "s"][:, a1:a1 + 128],
-                                           T[c2][:, a2:a2 + width], T[c2 + "s"][:, a2:a2 + width], start, stop),
+                                           T[c2][:, a2:a2 + width], T[c2 + "s"][:, a2:a2 + width], True, True),
            [r(c1, a1, a1 + 128), r(c1 + "s", a1, a1 + 128), r(c2, a2, a2 + width), r(c2 + "s", a2, a2 + width)],
-           [r(out, 512 * bank, 512 * bank + 512)] if start else [])
-        if not start:
-            note("p", [], [r(out, 512 * bank, 512 * bank + 512)], token("p", known["p"]))
+           [r(out, 512 * bank, 512 * bank + 512)])
 
-    far = [q for q in range(n) if q != rank and topo.chip(cores[q]) != topo.chip(core)]
+    far = [q for q in range(n) if topo.chip(cores[q]) != topo.chip(core)]
     near = [q for q in range(n) if q != rank and topo.chip(cores[q]) == topo.chip(core)]
+    mate = rank ^ 1
+    assert near == [mate]
+    even = [q for q in far if (q ^ rank) % 2 == 0]
     fe = topo.engines(core, cores[far[0]])
-    ne = [e for e in topo.engines(core, cores[near[0]]) if e not in fe] if near else []
+    ne = [e for e in topo.engines(core, cores[mate]) if e not in fe]
+    block = lambda q: n - 1 - (q ^ rank)
 
     def dest(q):
         a = topo.addr(cores[q])
         return DstId(rid=a[0], pnc=a[1])
 
-    def send(sem, src, dst_of, reads):
+    def send(parts, reads):
         before("g", reads, [])
-        ts_ = []
-        for qs, es in ((far, fe), (near, ne)):
-            if qs:
-                ts_.append(RemoteDMATransfer(dst_ids=[dest(q) for q in qs], dma_engine_mask=sum(1 << e for e in es), remote_sem=T.sem[sem],
-                                             srcs=[src], dsts=[dst_of((rank - q - 1) % n) for q in qs], alu_op=0))
-                cnt["sent"] = cnt.get("sent", 0) + len(es)
-        g.remote_dma_fused(ts_, local_sem=T.sem["sent"])
-
-    arrive = len(fe) * len(far) + len(ne) * len(near)
+        out = []
+        for qs, es, sem, src, dst_of in parts:
+            out.append(RemoteDMATransfer(dst_ids=[dest(q) for q in qs], dma_engine_mask=sum(1 << e for e in es), remote_sem=T.sem[sem],
+                                         srcs=[src], dsts=[dst_of(q) for q in qs], alu_op=0))
+            cnt["sent"] = cnt.get("sent", 0) + len(es)
+        g.remote_dma_fused(out, local_sem=T.sem["sent"])
 
     def landed(sem, total, regions):
         cnt[sem] = total
@@ -216,33 +220,39 @@ def rank_program(g, core, T, topo):
             note("far", [], [a], (sem, total, {}, seq[0]))
 
     def send_list(t):
-        send("arl%d" % t, T["my%d" % t][:, 0:1], lambda m: T["land%d" % t][:, m:m + 1], [r("my%d" % t, 0, 1)])
-        landed("arl%d" % t, arrive, [r("land%d" % t, 0, 7)])
+        src, dst = T["my%d" % t][:, 0:1], lambda q: T["land%d" % t][:, block(q):block(q) + 1]
+        send([(far, fe, "arl%d" % t, src, dst), (near, ne, "arl%d" % t, src, dst)], [r("my%d" % t, 0, 1)])
+        landed("arl%d" % t, len(fe) * len(far) + len(ne), [r("land%d" % t, 0, 7)])
 
     def send_cols(t):
-        c, b = "comb%d" % t, P * t
-        o = b + 224
-        send("arc%d" % t, T[c][:, o:o + S].bitcast(dt.uint8), lambda m: T[c][:, b + S * m:b + S * m + S].bitcast(dt.uint8), [r(c, o, o + S)])
-        send("arc%d" % t, T[c + "s"][:, o:o + S], lambda m: T[c + "s"][:, b + S * m:b + S * m + S], [r(c + "s", o, o + S)])
-        landed("arc%d" % t, 2 * arrive, [r(c, b, b + 224), r(c + "s", b, b + 224)])
+        c, b, fs, nr = "comb%d" % t, P * t, "arc%d" % t, "arn%d" % t
+        o, w = b + 224, b + 192
+        src, dst = T[c][:, o:o + S].bitcast(dt.uint8), lambda q: T[c][:, b + S * block(q):b + S * block(q) + S].bitcast(dt.uint8)
+        send([(far, fe, fs, src, dst), (near, ne, nr, src, dst)], [r(c, o, o + S)])
+        send([(near, ne, nr, T[c + "s"][:, o:o + S], lambda q: T[c + "s"][:, w:w + S])], [r(c + "s", o, o + S)])
+        landed(nr, 2 * len(ne), [r(c, w, w + S), r(c + "s", w, w + S)])
+        send([(even, fe, fs, T[c + "s"][:, w:w + 2 * S], lambda q: T[c + "s"][:, b + S * (block(q) - 1):b + S * (block(q) + 1)])],
+             [r(c + "s", w, w + 2 * S)])
+        landed(fs, len(fe) * (len(far) + len(even)), [r(c, b, w), r(c + "s", b, w)])
 
-    sdl = [(16 * a, T.sdw[16 * a:16 * a + 16, :], r("sdw", 0, 2, 16 * a, 16 * a + 16)) for a in range(8)]
+    sdl = [(T.sdw[16 * a:16 * a + 16, :], r("sdw", 0, 2, 16 * a, 16 * a + 16)) for a in range(8)]
     dmas("dx", [("s", T.xt[:], T.x[:], [], [r("xt", 0, 1024)])])
-    dmas("dsd", [("y" if i % 2 == 0 else "s", o, T.sd[:], [], [w]) for i, (a, o, w) in enumerate(sdl)])
+    dmas("dsd", [("y" if i % 2 == 0 else "s", o, T.sd[:], [], [w]) for i, (o, w) in enumerate(sdl)])
     dmas("dnb", [("y", T.nbw[16 * a:16 * a + 16, :], T.nb[:], [], [r("nbw", 0, 64, 16 * a, 16 * a + 16)]) for a in range(8)])
     dmas("dw", [("y", T.wt[:], T.w[:], [], [r("wt", 0, 1024)])])
 
-    op("g", lambda: g.iota(T.pint[:], [[0, 1]], 0, 1), [], [r("pint", 0, 1)])
-    op("g", lambda: g.iota(T.pidx[:], [[0, 1]], 0, 1, allow_small_or_imprecise_dtypes=True), [], [r("pidx", 0, 1)])
-    op("g", lambda: g.iota(T.icol[:], [[1, 128]], 0, 0, allow_small_or_imprecise_dtypes=True), [], [r("icol", 0, 128)])
-    op("g", lambda: g.iota(T.ic64[:], [[128, 2], [1, 32]], 0, 0, allow_small_or_imprecise_dtypes=True), [], [r("ic64", 0, 64)])
-    op("g", lambda: g.iota(T.ici[:], [[1, 256]], 0, 0), [], [r("ici", 0, 256)])
     pint, pidx = r("pint", 0, 1), r("pidx", 0, 1)
+    iota(pint, [[0, 1]], 0, 1, False)
+    iota(pidx, [[0, 1]], 0, 1)
+    iota(r("icol", 0, 128), [[1, 128]], 0, 0)
+    iota(r("ic64", 0, 64), [[128, 2], [1, 32]], 0, 0)
+    iota(r("kk8", 0, 8), [[0, 2], [-1, 4]], 3, 0)
+    iota(r("plc", 0, 8), [[128, 2], [0, 4]], 0, 1)
     ci = lambda i: r("ci", i, i + 1)
     cf = lambda i: r("cf", i, i + 1)
     fill(r("ones32", 0, 32), 1.0)
-    fill(r("ones", 0, 256), 1.0)
     fill(r("c19", 0, 32), float(2 ** 19))
+    fill(r("ones", 0, 2048), 1.0)
     ts(ci(0), pint, 31, Op.bitwise_and)
     ts(ci(1), pint, 15, Op.bitwise_and)
     ts(ci(2), pint, 96, Op.bitwise_and)
@@ -250,21 +260,28 @@ def rank_program(g, core, T, topo):
     ts(ci(4), pint, 64, Op.bitwise_and)
     cp(r("cf", 0, 5), r("ci", 0, 5))
     ts(cf(5), cf(0), 16.0, Op.is_ge)
-    ts(cf(6), cf(0), float(2 ** 19), Op.mult)
+    ts(cf(6), cf(1), float(2 ** 19), Op.mult)
+    ts(cf(7), cf(6), float(2 ** 23), Op.add)
     cp(cf(8), pidx)
     ts(cf(9), pidx, 128.0, Op.add)
+    ts(r("cf", 10, 12), r("cf", 8, 10), -0.5, Op.add)
+    fill(r("ste", 0, 512, st=2), 0.0)
+    fill(r("ste", 1, 512, st=2), 1.0)
     place = lambda h: r("cf", 8 + h, 9 + h)
     place2 = r("cf", 8, 10)
 
     cp(r("sdu", 0, 2), r("sdw", 0, 2))
     cp(r("sdf", 0, 2), r("sdw", 0, 2))
     tt(r("sdf", 2, 3), r("sdf", 1, 2), r("sdf", 0, 1), Op.subtract)
-    ts(r("sdf", 3, 4), r("sdf", 2, 3), cf(5), Op.mult, r("sdf", 0, 1), Op.add)
-    ts(r("my0", 0, 1), r("sdf", 3, 4), float(P * rank), Op.add)
+    ts(r("my0", 0, 1), r("sdf", 2, 3), cf(5), Op.mult, r("sdf", 0, 1), Op.add)
     send_list(0)
     quant("qx", "qxs", 0, 256, "xt", 0, 1024)
+    quant("comb0", "comb0s", 224, 352, "xt", 0, 512)
     pick("comb0", 224, "qx", 256, "sdu", 0, 2)
     send_cols(0)
+    dmas("dfx", [("y", T.finw[:, 0:P].bitcast(dt.uint8), T.qx[:].bitcast(dt.uint8), [r("qx", 0, P)], [r("finw", 0, P)]),
+                 ("y", T.finws[:, 0:P], T.qxs[:], [r("qxs", 0, P)], [r("finws", 0, P)])])
+    iota(r("c16", 0, 256), [[0, 16], [1, 16]], 0, 0)
 
     ts(ci(5), pint, 3, Op.bitwise_and)
     ts(ci(6), pint, 4, Op.bitwise_and)
@@ -276,13 +293,14 @@ def rank_program(g, core, T, topo):
     cp(r("nbof", 1, 2), cf(20))
     op("v", lambda: g.vector.tensor_copy(T.nbo[:, 0:16], T.nbw[:, 0:64].indirect(T.nbof[:, 0:1])), [r("nbw", 0, 64), r("nbof", 0, 1)], [r("nbo", 0, 16)])
     nbo = r("nbo", 0, 8)
-    ts(r("rpa", 0, 32), r("ones32", 0, 32), r("sdf", 3, 4), Op.mult)
+    ts(r("rpa", 0, 32), r("ones32", 0, 32), r("my0", 0, 1), Op.mult)
     tr(r("tb", 0, 32), r("rpa", 0, 32))
     for h in (0, 1):
         ts(r("rpb", 32 * h, 32 * h + 32), r("tb", 0, 32), place(h), Op.is_equal)
         red(r("tk", h, h + 1), r("rpb", 32 * h, 32 * h + 32), Op.add)
     fill(r("sb", 0, 16), -9e29)
-    fill(r("pl8", 0, 8), -1e5)
+    fill(r("pl8", 0, 8), float(-2 ** 22))
+    fill(r("qs", 0, 2), -1.0)
 
     def settle(first):
         if first:
@@ -297,55 +315,60 @@ def rank_program(g, core, T, topo):
             ts(r("sb", 8 * h, 8 * h + 4), r("sb", 8 * h, 8 * h + 4), r("nf", h, h + 1), Op.mult, r("fx", h, h + 1), Op.add)
 
     settle(True)
-    for k in range(4):
-        fill(r("c8", k, 8, st=4), float((3 - k) * 1024 - 100000))
+    ts(r("m8", 0, 8), r("kk8", 0, 8), float(2 ** 18), Op.mult, float(-2 ** 22), Op.add)
+    tt(r("c8", 0, 8), r("m8", 0, 8), r("plc", 0, 8), Op.add)
 
     def masks(t):
         for m in range(8):
             src = r("my%d" % t, 0, 1) if m == 7 else r("land%d" % t, m, m + 1)
-            ts(r("rpf", 32 * m, 32 * m + 32), r("ones32", 0, 32), src, Op.mult)
+            ts(r("rpf", 32 * m, 32 * m + 32), r("ones32", 0, 32), src, Op.mult, float(P * (rank ^ (n - 1 - m))), Op.add)
         tr(r("ff", 0, 256), r("rpf", 0, 256))
         for i in range(8):
             ts(r("eqx", 256 * i, 256 * i + 256), r("ff", 0, 256), r("nbx", i, i + 1), Op.is_equal, 256.0, Op.mult)
-        for i in range(8):
-            scan(r("sc", 256 * i, 256 * i + 256), r("eqx", 256 * i, 256 * i + 256), r("ones", 0, 256), 0.0, Op.max, Op.subtract)
+        scan(r("sc", 0, 2048), r("eqx", 0, 2048), r("ones", 0, 2048), 0.0, Op.max, Op.subtract)
         pos = r("sc", 255, 2048, st=256)
-        ts(r("pkb", 0, 8), pos, 0.0, Op.is_lt, -9e29 / 256, Op.mult)
-        ts(r("t8", 0, 8), pos, 0.0, Op.is_ge, float(100000 + 256 * t), Op.mult)
-        tt(r("u8", 0, 8), r("t8", 0, 8), pos, Op.add)
-        tt(r("t8", 0, 8), r("u8", 0, 8), r("c8", 0, 8), Op.add)
-        tt(r("pl8", 0, 8), r("pl8", 0, 8), r("t8", 0, 8), Op.max)
+        ts(r("pkc", 0, 8), pos, 192.0, Op.is_lt, -9e29 / 64, Op.mult)
+        ts(r("t8", 0, 8), pos, 0.0, Op.is_lt, -9e29 / 192, Op.mult)
+        ts(r("u8", 0, 8), pos, 192.0, Op.is_ge, -9e29 / 192, Op.mult)
+        tt(r("pkb", 0, 8), r("t8", 0, 8), r("u8", 0, 8), Op.add)
+
+    def chip_scores(t):
+        for h in (0, 1):
+            mm("yy", h, 128, "qx", 128 * h, "comb%d" % t, P * t + 192)
+        for i in range(8):
+            x = r("prc", 64 * i, 64 * i + 64)
+            tt(x, r("yy", 512 * (i // 4), 512 * (i // 4) + 64), r("eqx", 256 * i + 192, 256 * i + 256), Op.mult)
+            act(x, x, Fn.Identity, bias=r("pkc", i, i + 1), scale=1.0 / 256, accum=r("sb1", i, i + 1))
+        pos = r("sc", 255, 2048, st=256)
+        ts(r("m8", 0, 8), pos, 0.0, Op.is_ge, float(2 ** 22 + 65536 * t), Op.mult)
+        ts(r("n8", 0, 8), pos, 256.0, Op.mult)
+        for h in (0, 1):
+            tt(r("sb", 8 * h, 8 * h + 4), r("sb", 8 * h, 8 * h + 4), r("sb1", 4 * h, 4 * h + 4), Op.max)
+        tt(r("o8", 0, 8), r("n8", 0, 8), r("c8", 0, 8), Op.add)
+        tt(r("n8", 0, 8), r("m8", 0, 8), r("o8", 0, 8), Op.add)
+        tt(r("pl8", 0, 8), r("pl8", 0, 8), r("n8", 0, 8), Op.max)
 
     fill(r("et", 0, 2048), 0.0)
     for b in range(4):
-        ts(r("et", 512 * b + b, 512 * b + 512, st=4), r("icol", 0, 128), pidx, Op.is_equal)
+        ts(r("et", 512 * b + b, 512 * b + 512, st=4), r("icol", 0, 128), pidx, Op.is_equal, 0.5, Op.mult)
+    for b in range(4):
         quant("eq", "eqs", 128 * b, 128 * b + 128, "et", 512 * b, 512 * b + 512)
     fill(r("ht", 0, 512), 0.0)
-    quant("pko", "pkos", 0, 128, "xt", 0, 512)
-    quant("pkp", "pkps", 0, 128, "xt", 0, 512)
-    cp(r("plm", 0, 1), cf(2))
+    quant("pk", "pks", 0, 128, "xt", 0, 512)
     ts(cf(21), cf(3), -2.0, Op.mult, cf(2), Op.add)
     ts(cf(22), cf(4), -2.0, Op.mult, cf(2), Op.add)
     ts(cf(23), cf(4), -2.0, Op.mult, cf(21), Op.add)
     for d, b in enumerate((2, 21, 22, 23)):
         ts(r("plm", 64 * d, 64 * d + 64), r("ic64", 0, 64), cf(b), Op.add, float(32 * d), Op.add)
     for h in (0, 1):
-        ts(r("thr", 256 * h, 256 * h + 256), r("plm", 0, 256), place(h), Op.is_lt, 2.0 ** -120, Op.mult)
-    ts(cf(24), cf(1), 16.0, Op.add)
-    for i, c in enumerate((1, 24, 0)):
-        ts(r("dg", 32 * i, 32 * i + 32), r("icol", 0, 32), cf(c), Op.not_equal, float(2 ** 22), Op.mult)
-    masks(0)
+        ts(r("ed", 512 * h + 1, 512 * h + 512, st=2), r("plm", 0, 256), r("cf", 10 + h, 11 + h), Op.subtract, 2.0 ** -120, Op.mult)
     cp(r("fl", 0, 2), place2)
     ts(r("w2", 0, 2), place2, float(P * rank + 1), Op.add)
     tt(r("w3", 0, 2), r("w2", 0, 2), r("tk", 0, 2), Op.mult)
     ts(r("pa2", 0, 2), r("w3", 0, 2), -1.0, Op.add)
-
-    def late():
-        quant("finw", "finws", 0, 256, "xt", 0, 1024)
-        quant("qw", "qws", 0, 256, "wt", 0, 1024)
-        ts(r("icj", 0, 256), r("ici", 0, 256), 15, Op.bitwise_and)
-        ts(r("m16", 0, 256), r("icj", 0, 256), cf(1), Op.is_equal)
-        ts(r("seg", 0, 256), r("icj", 0, 256), 0.0, Op.not_equal)
+    ts(r("seg", 0, 256), r("c16", 0, 256), 0.0, Op.not_equal)
+    masks(0)
+    chip_scores(0)
 
     def spread(buf, w):
         for b in range(4):
@@ -353,14 +376,28 @@ def rank_program(g, core, T, topo):
         for b in (0, 1):
             cp(r(buf, 2 * w, 4 * w, 64 * b, 64 * b + 64), r(buf, 0, 2 * w, 64 * (1 - b), 64 * (1 - b) + 64))
 
+    def parents():
+        cp(r("qi", 0, 2), r("qs", 0, 2))
+        ts(r("qi", 2, 4), r("qi", 0, 2), 18, Op.arith_shift_right)
+        cp(r("w3", 0, 2), r("qi", 2, 4))
+        for h in (0, 1):
+            ts(r("e8", 4 * h, 4 * h + 4), r("kk8", 4 * h, 4 * h + 4), r("w3", h, h + 1), Op.is_equal)
+        tt(r("u8", 0, 8), r("e8", 0, 8), nbo, Op.mult)
+        for h in (0, 1):
+            red(r("w2", h, h + 1), r("u8", 4 * h, 4 * h + 4), Op.add)
+        ts(r("tk", 0, 2), r("qs", 0, 2), 0.0, Op.is_ge)
+        tt(r("x2", 0, 2), r("w2", 0, 2), r("pa2", 0, 2), Op.subtract)
+        tt(r("y2", 0, 2), r("x2", 0, 2), r("tk", 0, 2), Op.mult)
+        tt(r("pa2", 0, 2), r("pa2", 0, 2), r("y2", 0, 2), Op.add)
+
     for t in range(R):
         c = "comb%d" % t
         for h in (0, 1):
-            mm("zz", h, 256, "qx", 128 * h, c, P * t, True, True)
+            mm("zz", h, 192, "qx", 128 * h, c, P * t)
         for i in range(8):
             h, k = i // 4, i % 4
-            blk = r("prod", 256 * i, 256 * i + 256)
-            tt(blk, r("zz", 512 * h, 512 * h + 256), r("eqx", 256 * i, 256 * i + 256), Op.mult)
+            blk = r("prod", 256 * i, 256 * i + 192)
+            tt(blk, r("zz", 512 * h, 512 * h + 192), r("eqx", 256 * i, 256 * i + 192), Op.mult)
             act(blk, blk, Fn.Identity, bias=r("pkb", i, i + 1), scale=1.0 / 256, accum=r("sb", 8 * h + 4 + k, 8 * h + 5 + k))
         if t < R - 1:
             lst = []
@@ -378,99 +415,85 @@ def rank_program(g, core, T, topo):
         tr(r("row", 0, 64), r("rpa", 0, 64))
         spread("row", 64)
         for h in (0, 1):
-            act(r("ed", 256 * h, 256 * h + 256), r("row", 0, 256), Fn.Identity, bias=r("bst", h, h + 1), scale=-1.0)
-        ts(r("ib", 0, 2), r("bst", 0, 2), -5e29, Op.is_lt, 4.0, Op.mult)
+            act(r("ed", 512 * h, 512 * h + 512, st=2), r("row", 0, 256), Fn.Identity, bias=r("bst", h, h + 1), scale=-1.0)
+        ts(r("ib", 0, 2), r("bst", 0, 2), -5e29, Op.is_lt, float(2 ** 29), Op.mult)
         for h in (0, 1):
             tt(r("sb", 8 * h, 8 * h + 4), r("sb", 8 * h, 8 * h + 4), r("sb", 8 * h + 4, 8 * h + 8), Op.max)
         for h in (0, 1):
             ts(r("e8", 4 * h, 4 * h + 4), r("sb", 8 * h, 8 * h + 4), r("bst", h, h + 1), Op.is_equal)
         for h in (0, 1):
-            x = r("cm", 256 * h, 256 * h + 256)
-            tt(x, r("ed", 256 * h, 256 * h + 256), r("thr", 256 * h, 256 * h + 256), Op.is_lt)
-            act(x, x, Fn.Identity, bias=r("ib", h, h + 1), accum=r("rk", h, h + 1))
+            x = 512 * h
+            scan(r("cm", x, x + 512), r("ste", 0, 512), r("ed", x, x + 512), 0.0, Op.mult, Op.add)
+            act(r("sg", 256 * h, 256 * h + 256), r("cm", x + 1, x + 512, st=2), Fn.Sign, accum=r("rs", h, h + 1))
         tt(r("t8", 0, 8), r("e8", 0, 8), r("pl8", 0, 8), Op.mult)
         for h in (0, 1):
             red(r("q2", h, h + 1), r("t8", 4 * h, 4 * h + 4), Op.max)
         cp(r("qi", 0, 2), r("q2", 0, 2))
-        ts(r("qi", 2, 4), r("qi", 0, 2), 1023, Op.bitwise_and)
-        for h in (0, 1):
-            ts(r("pay", h, h + 1), r("qi", 2 + h, 3 + h), 256.0, Op.mult, place(h), Op.add)
+        ts(r("qi", 2, 4), r("qi", 0, 2), 2 ** 18 - 1, Op.bitwise_and)
+        tt(r("pay", 0, 2), r("qi", 2, 4), r("ib", 0, 2), Op.add)
+        ts(r("rk", 0, 2), r("rs", 0, 2), -0.5, Op.mult, 128.0, Op.add)
         for h in (0, 1):
             ts(r("rpb", 32 * h, 32 * h + 32), r("c19", 0, 32), r("rk", h, h + 1), Op.mult, r("pay", h, h + 1), Op.add)
         tr(r("tb", 0, 64), r("rpb", 0, 64))
-        ts(r("rpb", 0, 64), r("tb", 0, 64), cf(6), Op.subtract)
-        red(r("part", 0, 1), r("rpb", 0, 64), Op.min, absolute=True)
-        ts(r("rpc", 0, 32), r("ones32", 0, 32), r("part", 0, 1), Op.mult)
-        tr(r("p4", 0, 32), r("rpc", 0, 32))
-        spread("p4", 32)
-        tt(r("l64", 0, 64), r("p4", 0, 64), r("p4", 64, 128), Op.min)
-        tt(r("l32", 0, 32), r("l64", 0, 32), r("l64", 32, 64), Op.min)
-        for i in range(3):
-            tt(r("dd", 32 * i, 32 * i + 32), r("l32", 0, 32), r("dg", 32 * i, 32 * i + 32), Op.add)
-        for i in range(3):
-            red(r("vals", i, i + 1), r("dd", 32 * i, 32 * i + 32), Op.min)
-        ts(r("okv", 0, 3), r("vals", 0, 3), float(2 ** 18), Op.is_lt)
-        tt(r("vz", 0, 3), r("vals", 0, 3), r("okv", 0, 3), Op.mult)
-        cp(r("vi", 0, 3), r("vz", 0, 3))
-        ts(r("vi", 4, 7), r("vi", 0, 3), 255, Op.bitwise_and)
-        ts(r("vi", 8, 10), r("vi", 0, 2), 8, Op.arith_shift_right)
-        cp(r("offu", 0, 2), r("vi", 4, 6))
-        cp(r("offu", 2, 4), r("vi", 8, 10))
-        pick("pko", 0, "qx", 256, "offu", 0, 2)
-        pick("pkp", 0, c, P * t + P, "offu", 2, 4)
-        if t < R - 1:
-            my = "my%d" % (t + 1)
-            ts(r("vz", 3, 4), r("okv", 2, 3), float(P * rank + 7), Op.mult, -7.0, Op.add)
-            tt(r(my, 0, 1), r("vi", 6, 7), r("vz", 3, 4), Op.add)
+        for i in (0, 1):
+            ts(r("dx", 64 * i, 64 * i + 64), r("tb", 0, 64), cf(6 + i), Op.subtract)
+        for i in (0, 1):
+            red(r("pt", i, i + 1), r("dx", 64 * i, 64 * i + 64), Op.min, absolute=True)
+        spread("pt", 2)
+        for i in (0, 1):
+            red(r("vi", i, i + 1), r("pt", i, 8, st=2), Op.min)
+        more = t < R - 1
+        ts(r("vi", 2, 4), r("vi", 0, 2), 255, Op.bitwise_and)
+        if more:
+            ts(r("vz", 0, 2), r("vi", 0, 2), float(2 ** 18), Op.is_ge, -10000.0, Op.mult)
+        ts(r("vi", 4, 6), r("vi", 0, 2), 8, Op.arith_shift_right)
+        if more:
+            tt(r("vz", 2, 4), r("vi", 2, 4), r("vz", 0, 2), Op.add)
+        cp(r("offu", 0, 2), r("vi", 2, 4))
+        if more:
+            tt(r("vz", 4, 5), r("vz", 3, 4), r("vz", 2, 3), Op.subtract)
+        ts(r("offu", 2, 4), r("vi", 4, 6), float(P * t + P - 1), Op.min)
+        if more:
+            ts(r("my%d" % (t + 1), 0, 1), r("vz", 4, 5), cf(5), Op.mult, r("vz", 2, 3), Op.add)
             send_list(t + 1)
+        pick("pk", 0, "qx", 256, "offu", 0, 2)
+        pick("pk", 32, c, P * t + P, "offu", 2, 4)
         for b in range(4):
-            mm("dec", b, 128, "eq", 128 * b, "pko", 0, True, False)
-        for b in range(4):
-            mm("dec", b, 128, "eq", 128 * b, "pkp", 0, False, True)
-        ts(r("tk", 0, 2), r("rk", 0, 2), 31.5, Op.is_lt)
-        ts(r("w2", 0, 2), r("rk", 0, 2), float(P + S * t), Op.add)
-        tt(r("w3", 0, 2), r("w2", 0, 2), place2, Op.subtract)
-        tt(r("w2", 0, 2), r("w3", 0, 2), r("tk", 0, 2), Op.mult)
+            mm("dec", b, 128, "eq", 128 * b, "pk", 0)
+            act(r("od", 32 * b, 32 * b + 32), r("dec", 512 * b, 512 * b + 32), Fn.Copy)
+        tt(r("w2", 0, 2), r("rk", 0, 2), r("ib", 0, 2), Op.add)
+        ts(r("w3", 0, 2), r("rk", 0, 2), float(P + S * t), Op.add)
+        ts(r("tk", 0, 2), r("w2", 0, 2), 31.5, Op.is_lt)
+        tt(r("x2", 0, 2), r("w3", 0, 2), place2, Op.subtract)
+        tt(r("w2", 0, 2), r("x2", 0, 2), r("tk", 0, 2), Op.mult)
         tt(r("fl", 0, 2), r("fl", 0, 2), r("w2", 0, 2), Op.add)
-        if t == R - 1:
+        if not more:
             for h in (0, 1):
                 ts(r("rpd", 32 * h, 32 * h + 32), r("ones32", 0, 32), r("fl", h, h + 1), Op.mult)
             tr(r("flt", 0, 64), r("rpd", 0, 64))
             for a in range(4):
                 i_, o_ = r("flt", 0, 64, 32 * a, 32 * a + 1), r("flr", 64 * a, 64 * a + 64)
                 op("g", lambda: g.partition_broadcast(ap(o_), ap(i_), 128), [i_], [o_])
+        tt(r("x2", 0, 2), r("q2", 0, 2), r("qs", 0, 2), Op.subtract)
+        tt(r("y2", 0, 2), r("x2", 0, 2), r("tk", 0, 2), Op.mult)
+        tt(r("qs", 0, 2), r("qs", 0, 2), r("y2", 0, 2), Op.add)
         for b in range(4):
-            o_, i_ = r("ht", b, 128, st=4), r("dec", 512 * b, 512 * b + 32)
-            if b < 2:
-                ts(o_, i_, 0.5, Op.mult)
-            else:
-                act(o_, i_, Fn.Copy, scale=0.5)
-        if t < R - 1:
+            tt(r("ht", b, 128, st=4), r("dec", 512 * b + 32, 512 * b + 64), r("od", 32 * b, 32 * b + 32), Op.add)
+        if more:
             d, o = "comb%d" % (t + 1), P * (t + 1) + 224
             quant(d, d + "s", o, o + 128, "ht", 0, 512)
             send_cols(t + 1)
             f = P + S * t
             dmas("df%d" % t, [("y", T.finw[:, f:f + S].bitcast(dt.uint8), T[d][:, o:o + S].bitcast(dt.uint8), [r(d, o, o + S)], [r("finw", f, f + S)]),
                               ("y", T.finws[:, f:f + S], T[d + "s"][:, o:o + S], [r(d + "s", o, o + S)], [r("finws", f, f + S)])])
-        else:
-            quant("finw", "finws", 320, 448, "ht", 0, 512)
-        def parents():
-            for h in (0, 1):
-                ts(r("e8", 4 * h, 4 * h + 4), r("pl8", 4 * h, 4 * h + 4), r("q2", h, h + 1), Op.is_equal)
-            tt(r("u8", 0, 8), r("e8", 0, 8), nbo, Op.mult)
-            for h in (0, 1):
-                red(r("w2", h, h + 1), r("u8", 4 * h, 4 * h + 4), Op.add)
-            tt(r("w3", 0, 2), r("w2", 0, 2), r("pa2", 0, 2), Op.subtract)
-            tt(r("w2", 0, 2), r("w3", 0, 2), r("tk", 0, 2), Op.mult)
-            tt(r("pa2", 0, 2), r("pa2", 0, 2), r("w2", 0, 2), Op.add)
-        parents()
-        if t < R - 1:
             settle(False)
             masks(t + 1)
-            if t == 0:
-                late()
+            chip_scores(t + 1)
+        else:
+            quant("finw", "finws", 320, 448, "ht", 0, 512)
+            quant("qw", "qws", 0, 256, "wt", 0, 1024)
+            ts(r("m16", 0, 256), r("c16", 0, 256), cf(1), Op.is_equal)
 
-    dmas("dpa", [("y", T.pa[0:1, 128 * h:128 * h + 128], T.pa2[:, h:h + 1], [r("pa2", h, h + 1)], []) for h in (0, 1)])
     tt(r("flm", 0, 256), r("flr", 0, 256), r("m16", 0, 256), Op.mult)
     scan(r("fls", 0, 256), r("seg", 0, 256), r("flm", 0, 256), 0.0, Op.mult, Op.add)
     for h in (0, 1):
@@ -478,13 +501,15 @@ def rank_program(g, core, T, topo):
             cp(r("fo", 8 * h + u, 8 * h + 8, st=2), r("fls", (2 * h + u) * 16 + 15, 256, st=64))
     pick("fin", 0, "finw", 352, "fo", 0, 16)
     for o in (0, 1):
-        mm("yy", o, 256, "qw", 128 * o, "fin", 0, True, True)
+        mm("yy", o, 256, "qw", 128 * o, "fin", 0)
     lst = [("y", T.oc[:], T.fin[:].bitcast(dt.uint8), [r("fin", 0, 256)], [])]
     lst += [("y", T.osc[4 * k:4 * k + 4, :], T.fins[32 * k:32 * k + 4, :], [r("fins", 0, 256)], []) for k in range(4)]
     cp(r("sy", 0, 256), r("yy", 0, 256))
     act(r("sy", 256, 512), r("yy", 512, 768), Fn.Copy)
     lst += [("y", T.y[:, 0:256], T.sy[:, 0:256], [r("sy", 0, 256)], []), ("s", T.y[:, 256:512], T.sy[:, 256:512], [r("sy", 256, 512)], [])]
     dmas("dout", lst)
+    parents()
+    dmas("dpa", [("y", T.pa[0:1, 128 * h:128 * h + 128], T.pa2[:, h:h + 1], [r("pa2", h, h + 1)], []) for h in (0, 1)])
     for sem in cnt:
         if known["g"].get(sem, 0) < cnt[sem]:
             g.wait_ge(T.sem[sem], cnt[sem])

@@ -21,9 +21,9 @@ SCRATCH = {
     "nbof": ("sbuf", [128, 2], "uint16"), "nbo": ("sbuf", [128, 16], "float32"), "nbx": ("sbuf", [128, 8], "float32"),
     "pint": ("sbuf", [128, 1], "int32"), "pidx": ("sbuf", [128, 1], "float32"), "icol": ("sbuf", [128, 128], "float32"),
     "c16": ("sbuf", [128, 256], "float32"), "kk8": ("sbuf", [128, 8], "float32"), "plc": ("sbuf", [128, 8], "float32"),
-    "ic64": ("sbuf", [128, 64], "float32"), "ci": ("sbuf", [128, 16], "int32"), "cf": ("sbuf", [128, 32], "float32"),
+    "ic": ("sbuf", [128, 256], "float32"), "ci": ("sbuf", [128, 16], "int32"), "cf": ("sbuf", [128, 32], "float32"),
     "plm": ("sbuf", [128, 256], "float32"), "ste": ("sbuf", [128, 512], "bfloat16"),
-    "ones32": ("sbuf", [128, 32], "float32"), "c19": ("sbuf", [128, 32], "float32"), "ones": ("sbuf", [128, 2048], "bfloat16"),
+    "ones32": ("sbuf", [128, 32], "float32"), "c256": ("sbuf", [128, 32], "float32"), "ones": ("sbuf", [128, 256], "bfloat16"),
     "m16": ("sbuf", [128, 256], "float32"), "seg": ("sbuf", [128, 256], "float32"), "c8": ("sbuf", [128, 8], "float32"),
     "my0": ("sbuf", [128, 4], "float32"), "my1": ("sbuf", [128, 4], "float32"), "my2": ("sbuf", [128, 4], "float32"),
     "land0": ("sbuf", [128, 8], "float32"), "land1": ("sbuf", [128, 8], "float32"), "land2": ("sbuf", [128, 8], "float32"),
@@ -37,15 +37,17 @@ SCRATCH = {
     "ed": ("sbuf", [128, 1024], "bfloat16"), "cm": ("sbuf", [128, 1024], "bfloat16"), "sg": ("sbuf", [128, 512], "bfloat16"),
     "rs": ("sbuf", [128, 2], "float32"), "rk": ("sbuf", [128, 2], "float32"),
     "e8": ("sbuf", [128, 8], "float32"), "q2": ("sbuf", [128, 2], "float32"), "qi": ("sbuf", [128, 4], "int32"),
-    "qs": ("sbuf", [128, 2], "float32"), "x2": ("sbuf", [128, 2], "float32"), "y2": ("sbuf", [128, 2], "float32"),
+    "qf": ("sbuf", [128, 2], "float32"), "qs": ("sbuf", [128, 2], "float32"), "x2": ("sbuf", [128, 2], "float32"),
+    "y2": ("sbuf", [128, 2], "float32"), "z2": ("sbuf", [128, 2], "float32"),
     "pay": ("sbuf", [128, 2], "float32"), "rpb": ("sbuf", [128, 64], "float32"), "tb": ("sbuf", [128, 64], "float32"),
-    "pt": ("sbuf", [128, 8], "float32"), "dx": ("sbuf", [128, 128], "float32"),
-    "vz": ("sbuf", [128, 8], "float32"), "vi": ("sbuf", [128, 12], "int32"), "offu": ("sbuf", [128, 4], "uint16"),
-    "tk": ("sbuf", [128, 2], "float32"), "nf": ("sbuf", [128, 2], "float32"), "nfm": ("sbuf", [128, 2], "float32"),
-    "fx": ("sbuf", [128, 2], "float32"), "fl": ("sbuf", [128, 2], "float32"), "pa2": ("sbuf", [128, 2], "float32"),
-    "w2": ("sbuf", [128, 2], "float32"), "w3": ("sbuf", [128, 2], "float32"), "rpd": ("sbuf", [128, 64], "float32"),
-    "flt": ("sbuf", [128, 64], "float32"), "flr": ("sbuf", [128, 256], "float32"), "flm": ("sbuf", [128, 256], "float32"),
-    "fls": ("sbuf", [128, 256], "float32"), "fo": ("sbuf", [128, 16], "uint16"), "sy": ("sbuf", [128, 512], "float32"),
+    "pt": ("sbuf", [128, 12], "float32"), "dx": ("sbuf", [128, 192], "float32"),
+    "vz": ("sbuf", [128, 4], "float32"), "vi": ("sbuf", [128, 12], "int32"), "offu": ("sbuf", [128, 4], "uint16"),
+    "tk0": ("sbuf", [128, 2], "float32"), "tk": ("sbuf", [128, 2], "float32"), "nf": ("sbuf", [128, 2], "float32"),
+    "nfm": ("sbuf", [128, 2], "float32"), "fx": ("sbuf", [128, 2], "float32"), "fl": ("sbuf", [128, 2], "float32"),
+    "pa2": ("sbuf", [128, 2], "float32"), "w2": ("sbuf", [128, 2], "float32"), "w3": ("sbuf", [128, 2], "float32"),
+    "rpd": ("sbuf", [128, 64], "float32"), "flt": ("sbuf", [128, 64], "float32"), "flr": ("sbuf", [128, 256], "float32"),
+    "flm": ("sbuf", [128, 256], "float32"), "fls": ("sbuf", [128, 256], "float32"), "fo": ("sbuf", [128, 16], "uint16"),
+    "sy": ("sbuf", [128, 512], "float32"),
     "dec": ("psum", [128, 2048], "float32"), "zz": ("psum", [128, 1024], "float32"), "yy": ("psum", [128, 1024], "float32"),
 }
 SEMAPHORES = ["v", "s", "p", "gp", "dsd", "dx", "dnb", "dw", "arl0", "arl1", "arl2", "arc0", "arc1", "arc2",
@@ -195,7 +197,6 @@ def rank_program(g, core, T, topo):
     near = [q for q in range(n) if q != rank and topo.chip(cores[q]) == topo.chip(core)]
     mate = rank ^ 1
     assert near == [mate]
-    even = [q for q in far if (q ^ rank) % 2 == 0]
     fe = topo.engines(core, cores[far[0]])
     ne = [e for e in topo.engines(core, cores[mate]) if e not in fe]
     block = lambda q: n - 1 - (q ^ rank)
@@ -204,10 +205,10 @@ def rank_program(g, core, T, topo):
         a = topo.addr(cores[q])
         return DstId(rid=a[0], pnc=a[1])
 
-    def send(parts, reads):
+    def send(fsem, nsem, src, dst_of, reads):
         before("g", reads, [])
         out = []
-        for qs, es, sem, src, dst_of in parts:
+        for qs, es, sem in ((far, fe, fsem), (near, ne, nsem)):
             out.append(RemoteDMATransfer(dst_ids=[dest(q) for q in qs], dma_engine_mask=sum(1 << e for e in es), remote_sem=T.sem[sem],
                                          srcs=[src], dsts=[dst_of(q) for q in qs], alu_op=0))
             cnt["sent"] = cnt.get("sent", 0) + len(es)
@@ -220,20 +221,16 @@ def rank_program(g, core, T, topo):
             note("far", [], [a], (sem, total, {}, seq[0]))
 
     def send_list(t):
-        src, dst = T["my%d" % t][:, 0:1], lambda q: T["land%d" % t][:, block(q):block(q) + 1]
-        send([(far, fe, "arl%d" % t, src, dst), (near, ne, "arl%d" % t, src, dst)], [r("my%d" % t, 0, 1)])
+        send("arl%d" % t, "arl%d" % t, T["my%d" % t][:, 0:1], lambda q: T["land%d" % t][:, block(q):block(q) + 1], [r("my%d" % t, 0, 1)])
         landed("arl%d" % t, len(fe) * len(far) + len(ne), [r("land%d" % t, 0, 7)])
 
     def send_cols(t):
         c, b, fs, nr = "comb%d" % t, P * t, "arc%d" % t, "arn%d" % t
         o, w = b + 224, b + 192
-        src, dst = T[c][:, o:o + S].bitcast(dt.uint8), lambda q: T[c][:, b + S * block(q):b + S * block(q) + S].bitcast(dt.uint8)
-        send([(far, fe, fs, src, dst), (near, ne, nr, src, dst)], [r(c, o, o + S)])
-        send([(near, ne, nr, T[c + "s"][:, o:o + S], lambda q: T[c + "s"][:, w:w + S])], [r(c + "s", o, o + S)])
+        send(fs, nr, T[c][:, o:o + S].bitcast(dt.uint8), lambda q: T[c][:, b + S * block(q):b + S * block(q) + S].bitcast(dt.uint8), [r(c, o, o + S)])
+        send(fs, nr, T[c + "s"][:, o:o + S], lambda q: T[c + "s"][:, b + S * block(q):b + S * block(q) + S], [r(c + "s", o, o + S)])
         landed(nr, 2 * len(ne), [r(c, w, w + S), r(c + "s", w, w + S)])
-        send([(even, fe, fs, T[c + "s"][:, w:w + 2 * S], lambda q: T[c + "s"][:, b + S * (block(q) - 1):b + S * (block(q) + 1)])],
-             [r(c + "s", w, w + 2 * S)])
-        landed(fs, len(fe) * (len(far) + len(even)), [r(c, b, w), r(c + "s", b, w)])
+        landed(fs, 2 * len(fe) * len(far), [r(c, b, w), r(c + "s", b, w)])
 
     sdl = [(T.sdw[16 * a:16 * a + 16, :], r("sdw", 0, 2, 16 * a, 16 * a + 16)) for a in range(8)]
     dmas("dx", [("s", T.xt[:], T.x[:], [], [r("xt", 0, 1024)])])
@@ -245,35 +242,49 @@ def rank_program(g, core, T, topo):
     iota(pint, [[0, 1]], 0, 1, False)
     iota(pidx, [[0, 1]], 0, 1)
     iota(r("icol", 0, 128), [[1, 128]], 0, 0)
-    iota(r("ic64", 0, 64), [[128, 2], [1, 32]], 0, 0)
     iota(r("kk8", 0, 8), [[0, 2], [-1, 4]], 3, 0)
     iota(r("plc", 0, 8), [[128, 2], [0, 4]], 0, 1)
+    iota(r("ic", 0, 256), [[32, 4], [128, 2], [1, 32]], 0, 0)
     ci = lambda i: r("ci", i, i + 1)
     cf = lambda i: r("cf", i, i + 1)
+    fill(r("ste", 0, 512, st=2), 0.0)
+    fill(r("ste", 1, 512, st=2), 1.0)
+    for b in range(4):
+        act(r("et", 512 * b, 512 * b + 512), r("ste", 0, 512), Fn.Copy, scale=0.0)
+    act(r("ht", 0, 512), r("ste", 0, 512), Fn.Copy, scale=0.0)
     fill(r("ones32", 0, 32), 1.0)
-    fill(r("c19", 0, 32), float(2 ** 19))
-    fill(r("ones", 0, 2048), 1.0)
+    fill(r("c256", 0, 32), 256.0)
+    fill(r("ones", 0, 256), 1.0)
     ts(ci(0), pint, 31, Op.bitwise_and)
     ts(ci(1), pint, 15, Op.bitwise_and)
     ts(ci(2), pint, 96, Op.bitwise_and)
     ts(ci(3), pint, 32, Op.bitwise_and)
     ts(ci(4), pint, 64, Op.bitwise_and)
-    cp(r("cf", 0, 5), r("ci", 0, 5))
-    ts(cf(5), cf(0), 16.0, Op.is_ge)
-    ts(cf(6), cf(1), float(2 ** 19), Op.mult)
-    ts(cf(7), cf(6), float(2 ** 23), Op.add)
-    cp(cf(8), pidx)
-    ts(cf(9), pidx, 128.0, Op.add)
-    ts(r("cf", 10, 12), r("cf", 8, 10), -0.5, Op.add)
-    fill(r("ste", 0, 512, st=2), 0.0)
-    fill(r("ste", 1, 512, st=2), 1.0)
-    place = lambda h: r("cf", 8 + h, 9 + h)
-    place2 = r("cf", 8, 10)
+    ts(ci(5), pint, 3, Op.bitwise_and)
+    ts(ci(6), pint, 4, Op.bitwise_and)
+    ts(ci(7), pint, 4, Op.arith_shift_right)
+    cp(r("cf", 0, 8), r("ci", 0, 8))
+    cp(cf(10), pidx)
+    ts(cf(11), pidx, 128.0, Op.add)
+    ts(cf(8), cf(0), 16.0, Op.is_ge)
+    ts(cf(14), cf(1), 2.0, Op.mult)
+    ts(cf(15), cf(1), 2.0, Op.mult, 32.0, Op.add)
+    ts(cf(16), cf(0), 2.0, Op.mult)
+    ts(cf(17), cf(5), 16.0, Op.mult, cf(7), Op.add)
+    ts(cf(21), cf(3), -2.0, Op.mult, cf(2), Op.add)
+    ts(cf(22), cf(4), -2.0, Op.mult, cf(2), Op.add)
+    ts(cf(18), cf(6), 2.0, Op.mult, cf(17), Op.add)
+    ts(cf(23), cf(4), -2.0, Op.mult, cf(21), Op.add)
+    ts(r("cf", 12, 14), r("cf", 10, 12), -0.5, Op.add, -2.0 ** -120, Op.mult)
+    cp(r("nbof", 0, 1), cf(18))
+    cp(r("nbof", 1, 2), cf(18))
+    place = lambda h: r("cf", 10 + h, 11 + h)
+    place2 = r("cf", 10, 12)
 
-    cp(r("sdu", 0, 2), r("sdw", 0, 2))
     cp(r("sdf", 0, 2), r("sdw", 0, 2))
+    cp(r("sdu", 0, 2), r("sdw", 0, 2))
     tt(r("sdf", 2, 3), r("sdf", 1, 2), r("sdf", 0, 1), Op.subtract)
-    ts(r("my0", 0, 1), r("sdf", 2, 3), cf(5), Op.mult, r("sdf", 0, 1), Op.add)
+    ts(r("my0", 0, 1), r("sdf", 2, 3), cf(8), Op.mult, r("sdf", 0, 1), Op.add)
     send_list(0)
     quant("qx", "qxs", 0, 256, "xt", 0, 1024)
     quant("comb0", "comb0s", 224, 352, "xt", 0, 512)
@@ -283,40 +294,44 @@ def rank_program(g, core, T, topo):
                  ("y", T.finws[:, 0:P], T.qxs[:], [r("qxs", 0, P)], [r("finws", 0, P)])])
     iota(r("c16", 0, 256), [[0, 16], [1, 16]], 0, 0)
 
-    ts(ci(5), pint, 3, Op.bitwise_and)
-    ts(ci(6), pint, 4, Op.bitwise_and)
-    ts(ci(7), pint, 4, Op.arith_shift_right)
-    cp(r("cf", 16, 19), r("ci", 5, 8))
-    ts(cf(19), cf(16), 16.0, Op.mult, cf(18), Op.add)
-    ts(cf(20), cf(17), 2.0, Op.mult, cf(19), Op.add)
-    cp(r("nbof", 0, 1), cf(20))
-    cp(r("nbof", 1, 2), cf(20))
+    for d, b in enumerate((2, 21, 22, 23)):
+        act(r("plm", 64 * d, 64 * d + 64), r("ic", 64 * d, 64 * d + 64), Fn.Identity, bias=cf(b))
+    for h in (0, 1):
+        act(r("ed", 512 * h + 1, 512 * h + 512, st=2), r("plm", 0, 256), Fn.Identity, bias=r("cf", 12 + h, 13 + h), scale=2.0 ** -120)
+    act(r("seg", 0, 256), r("c16", 0, 256), Fn.Sign)
     op("v", lambda: g.vector.tensor_copy(T.nbo[:, 0:16], T.nbw[:, 0:64].indirect(T.nbof[:, 0:1])), [r("nbw", 0, 64), r("nbof", 0, 1)], [r("nbo", 0, 16)])
     nbo = r("nbo", 0, 8)
     ts(r("rpa", 0, 32), r("ones32", 0, 32), r("my0", 0, 1), Op.mult)
-    tr(r("tb", 0, 32), r("rpa", 0, 32))
-    for h in (0, 1):
-        ts(r("rpb", 32 * h, 32 * h + 32), r("tb", 0, 32), place(h), Op.is_equal)
-        red(r("tk", h, h + 1), r("rpb", 32 * h, 32 * h + 32), Op.add)
     fill(r("sb", 0, 16), -9e29)
     fill(r("pl8", 0, 8), float(-2 ** 22))
+    tr(r("tb", 0, 32), r("rpa", 0, 32))
     fill(r("qs", 0, 2), -1.0)
+    ts(r("m8", 0, 8), r("kk8", 0, 8), float(2 ** 18), Op.mult, float(-2 ** 22), Op.add)
+    for h in (0, 1):
+        ts(r("rpb", 32 * h, 32 * h + 32), r("tb", 0, 32), place(h), Op.is_equal)
+    tt(r("c8", 0, 8), r("m8", 0, 8), r("plc", 0, 8), Op.add)
+    for h in (0, 1):
+        red(r("tk0", h, h + 1), r("rpb", 32 * h, 32 * h + 32), Op.add)
+    cp(r("fl", 0, 2), place2)
 
     def settle(first):
         if first:
-            ts(r("nf", 0, 2), r("tk", 0, 2), -1.0, Op.mult, 1.0, Op.add)
+            ts(r("nf", 0, 2), r("tk0", 0, 2), -1.0, Op.mult, 1.0, Op.add)
         else:
             tt(r("nf", 0, 2), r("nf", 0, 2), r("tk", 0, 2), Op.subtract)
         ts(r("nfm", 0, 2), r("nf", 0, 2), -1.0, Op.add)
-        ts(r("fx", 0, 2), r("nfm", 0, 2), 9e29, Op.mult)
+        ts(r("fx", 0, 2), r("nf", 0, 2), -1.0, Op.add, 9e29, Op.mult)
         for h in (0, 1):
             ts(r("nbx", 4 * h, 4 * h + 4), r("nbo", 4 * h, 4 * h + 4), r("nf", h, h + 1), Op.mult, r("nfm", h, h + 1), Op.add)
         for h in (0, 1):
             ts(r("sb", 8 * h, 8 * h + 4), r("sb", 8 * h, 8 * h + 4), r("nf", h, h + 1), Op.mult, r("fx", h, h + 1), Op.add)
 
     settle(True)
-    ts(r("m8", 0, 8), r("kk8", 0, 8), float(2 ** 18), Op.mult, float(-2 ** 22), Op.add)
-    tt(r("c8", 0, 8), r("m8", 0, 8), r("plc", 0, 8), Op.add)
+    for b in range(4):
+        ts(r("et", 512 * b + b, 512 * b + 512, st=4), r("icol", 0, 128), pidx, Op.is_equal, 0.5, Op.mult)
+    for b in range(4):
+        quant("eq", "eqs", 128 * b, 128 * b + 128, "et", 512 * b, 512 * b + 512)
+    quant("pk", "pks", 0, 128, "xt", 0, 512)
 
     def masks(t):
         for m in range(8):
@@ -325,73 +340,47 @@ def rank_program(g, core, T, topo):
         tr(r("ff", 0, 256), r("rpf", 0, 256))
         for i in range(8):
             ts(r("eqx", 256 * i, 256 * i + 256), r("ff", 0, 256), r("nbx", i, i + 1), Op.is_equal, 256.0, Op.mult)
-        scan(r("sc", 0, 2048), r("eqx", 0, 2048), r("ones", 0, 2048), 0.0, Op.max, Op.subtract)
-        pos = r("sc", 255, 2048, st=256)
-        ts(r("pkc", 0, 8), pos, 192.0, Op.is_lt, -9e29 / 64, Op.mult)
-        ts(r("t8", 0, 8), pos, 0.0, Op.is_lt, -9e29 / 192, Op.mult)
-        ts(r("u8", 0, 8), pos, 192.0, Op.is_ge, -9e29 / 192, Op.mult)
-        tt(r("pkb", 0, 8), r("t8", 0, 8), r("u8", 0, 8), Op.add)
-
-    def chip_scores(t):
+        for i in range(8):
+            scan(r("sc", 256 * i, 256 * i + 256), r("eqx", 256 * i, 256 * i + 256), r("ones", 0, 256), 0.0, Op.max, Op.subtract)
         for h in (0, 1):
             mm("yy", h, 128, "qx", 128 * h, "comb%d" % t, P * t + 192)
-        for i in range(8):
+
+        def chip(i):
             x = r("prc", 64 * i, 64 * i + 64)
             tt(x, r("yy", 512 * (i // 4), 512 * (i // 4) + 64), r("eqx", 256 * i + 192, 256 * i + 256), Op.mult)
             act(x, x, Fn.Identity, bias=r("pkc", i, i + 1), scale=1.0 / 256, accum=r("sb1", i, i + 1))
+
         pos = r("sc", 255, 2048, st=256)
-        ts(r("m8", 0, 8), pos, 0.0, Op.is_ge, float(2 ** 22 + 65536 * t), Op.mult)
+        chip_bias = r("pkc", 0, 8)
+        ts(chip_bias, pos, 192.0, Op.is_lt, -9e29 / 64, Op.mult)
+        ts(r("t8", 0, 8), pos, 0.0, Op.is_lt, -9e29 / 192, Op.mult)
+        ts(r("u8", 0, 8), pos, 192.0, Op.is_ge, -9e29 / 192, Op.mult)
         ts(r("n8", 0, 8), pos, 256.0, Op.mult)
-        for h in (0, 1):
-            tt(r("sb", 8 * h, 8 * h + 4), r("sb", 8 * h, 8 * h + 4), r("sb1", 4 * h, 4 * h + 4), Op.max)
+        ts(r("m8", 0, 8), pos, 0.0, Op.is_ge, float(2 ** 22 + 65536 * t), Op.mult)
+        for i in range(3):
+            chip(i)
+        tt(r("pkb", 0, 8), r("t8", 0, 8), r("u8", 0, 8), Op.add)
         tt(r("o8", 0, 8), r("n8", 0, 8), r("c8", 0, 8), Op.add)
+        for i in range(3, 6):
+            chip(i)
         tt(r("n8", 0, 8), r("m8", 0, 8), r("o8", 0, 8), Op.add)
+        for i in range(6, 8):
+            chip(i)
         tt(r("pl8", 0, 8), r("pl8", 0, 8), r("n8", 0, 8), Op.max)
 
-    fill(r("et", 0, 2048), 0.0)
-    for b in range(4):
-        ts(r("et", 512 * b + b, 512 * b + 512, st=4), r("icol", 0, 128), pidx, Op.is_equal, 0.5, Op.mult)
-    for b in range(4):
-        quant("eq", "eqs", 128 * b, 128 * b + 128, "et", 512 * b, 512 * b + 512)
-    fill(r("ht", 0, 512), 0.0)
-    quant("pk", "pks", 0, 128, "xt", 0, 512)
-    ts(cf(21), cf(3), -2.0, Op.mult, cf(2), Op.add)
-    ts(cf(22), cf(4), -2.0, Op.mult, cf(2), Op.add)
-    ts(cf(23), cf(4), -2.0, Op.mult, cf(21), Op.add)
-    for d, b in enumerate((2, 21, 22, 23)):
-        ts(r("plm", 64 * d, 64 * d + 64), r("ic64", 0, 64), cf(b), Op.add, float(32 * d), Op.add)
-    for h in (0, 1):
-        ts(r("ed", 512 * h + 1, 512 * h + 512, st=2), r("plm", 0, 256), r("cf", 10 + h, 11 + h), Op.subtract, 2.0 ** -120, Op.mult)
-    cp(r("fl", 0, 2), place2)
-    ts(r("w2", 0, 2), place2, float(P * rank + 1), Op.add)
-    tt(r("w3", 0, 2), r("w2", 0, 2), r("tk", 0, 2), Op.mult)
-    ts(r("pa2", 0, 2), r("w3", 0, 2), -1.0, Op.add)
-    ts(r("seg", 0, 256), r("c16", 0, 256), 0.0, Op.not_equal)
     masks(0)
-    chip_scores(0)
 
-    def spread(buf, w):
+    def spread(buf, w, between=None):
         for b in range(4):
             cp(r(buf, w, 2 * w, 32 * b, 32 * b + 32), r(buf, 0, w, 32 * (b ^ 1), 32 * (b ^ 1) + 32))
+        if between is not None:
+            between()
         for b in (0, 1):
             cp(r(buf, 2 * w, 4 * w, 64 * b, 64 * b + 64), r(buf, 0, 2 * w, 64 * (1 - b), 64 * (1 - b) + 64))
 
-    def parents():
-        cp(r("qi", 0, 2), r("qs", 0, 2))
-        ts(r("qi", 2, 4), r("qi", 0, 2), 18, Op.arith_shift_right)
-        cp(r("w3", 0, 2), r("qi", 2, 4))
-        for h in (0, 1):
-            ts(r("e8", 4 * h, 4 * h + 4), r("kk8", 4 * h, 4 * h + 4), r("w3", h, h + 1), Op.is_equal)
-        tt(r("u8", 0, 8), r("e8", 0, 8), nbo, Op.mult)
-        for h in (0, 1):
-            red(r("w2", h, h + 1), r("u8", 4 * h, 4 * h + 4), Op.add)
-        ts(r("tk", 0, 2), r("qs", 0, 2), 0.0, Op.is_ge)
-        tt(r("x2", 0, 2), r("w2", 0, 2), r("pa2", 0, 2), Op.subtract)
-        tt(r("y2", 0, 2), r("x2", 0, 2), r("tk", 0, 2), Op.mult)
-        tt(r("pa2", 0, 2), r("pa2", 0, 2), r("y2", 0, 2), Op.add)
-
     for t in range(R):
         c = "comb%d" % t
+        more = t < R - 1
         for h in (0, 1):
             mm("zz", h, 192, "qx", 128 * h, c, P * t)
         for i in range(8):
@@ -399,7 +388,9 @@ def rank_program(g, core, T, topo):
             blk = r("prod", 256 * i, 256 * i + 192)
             tt(blk, r("zz", 512 * h, 512 * h + 192), r("eqx", 256 * i, 256 * i + 192), Op.mult)
             act(blk, blk, Fn.Identity, bias=r("pkb", i, i + 1), scale=1.0 / 256, accum=r("sb", 8 * h + 4 + k, 8 * h + 5 + k))
-        if t < R - 1:
+        for h in (0, 1):
+            tt(r("sb", 8 * h, 8 * h + 4), r("sb", 8 * h, 8 * h + 4), r("sb1", 4 * h, 4 * h + 4), Op.max)
+        if more:
             lst = []
             for t2 in range(t + 1, R):
                 d = "comb%d" % t2
@@ -412,71 +403,76 @@ def rank_program(g, core, T, topo):
             red(r("bst", h, h + 1), r("sb", 8 * h, 8 * h + 8), Op.max)
         for h in (0, 1):
             ts(r("rpa", 32 * h, 32 * h + 32), r("ones32", 0, 32), r("bst", h, h + 1), Op.mult)
+        ts(r("ib", 0, 2), r("bst", 0, 2), -5e29, Op.is_lt, 2048.0, Op.mult)
         tr(r("row", 0, 64), r("rpa", 0, 64))
-        spread("row", 64)
+        tt(r("sb", 0, 4), r("sb", 0, 4), r("sb", 4, 8), Op.max)
+        spread("row", 64, lambda: tt(r("sb", 8, 12), r("sb", 8, 12), r("sb", 12, 16), Op.max))
         for h in (0, 1):
             act(r("ed", 512 * h, 512 * h + 512, st=2), r("row", 0, 256), Fn.Identity, bias=r("bst", h, h + 1), scale=-1.0)
-        ts(r("ib", 0, 2), r("bst", 0, 2), -5e29, Op.is_lt, float(2 ** 29), Op.mult)
-        for h in (0, 1):
-            tt(r("sb", 8 * h, 8 * h + 4), r("sb", 8 * h, 8 * h + 4), r("sb", 8 * h + 4, 8 * h + 8), Op.max)
         for h in (0, 1):
             ts(r("e8", 4 * h, 4 * h + 4), r("sb", 8 * h, 8 * h + 4), r("bst", h, h + 1), Op.is_equal)
-        for h in (0, 1):
+        tt(r("t8", 0, 8), r("e8", 0, 8), r("pl8", 0, 8), Op.mult)
+
+        def ahead(h):
             x = 512 * h
             scan(r("cm", x, x + 512), r("ste", 0, 512), r("ed", x, x + 512), 0.0, Op.mult, Op.add)
             act(r("sg", 256 * h, 256 * h + 256), r("cm", x + 1, x + 512, st=2), Fn.Sign, accum=r("rs", h, h + 1))
-        tt(r("t8", 0, 8), r("e8", 0, 8), r("pl8", 0, 8), Op.mult)
+
+        ahead(0)
         for h in (0, 1):
             red(r("q2", h, h + 1), r("t8", 4 * h, 4 * h + 4), Op.max)
         cp(r("qi", 0, 2), r("q2", 0, 2))
+        ahead(1)
         ts(r("qi", 2, 4), r("qi", 0, 2), 2 ** 18 - 1, Op.bitwise_and)
-        tt(r("pay", 0, 2), r("qi", 2, 4), r("ib", 0, 2), Op.add)
-        ts(r("rk", 0, 2), r("rs", 0, 2), -0.5, Op.mult, 128.0, Op.add)
+        tt(r("x2", 0, 2), r("q2", 0, 2), r("qs", 0, 2), Op.subtract)
+        ts(r("qf", 0, 2), r("qi", 2, 4), 2.0 ** -18, Op.mult)
+        tt(r("pay", 0, 2), r("qf", 0, 2), r("ib", 0, 2), Op.add)
         for h in (0, 1):
-            ts(r("rpb", 32 * h, 32 * h + 32), r("c19", 0, 32), r("rk", h, h + 1), Op.mult, r("pay", h, h + 1), Op.add)
+            ts(r("rpb", 32 * h, 32 * h + 32), r("c256", 0, 32), r("rs", h, h + 1), Op.subtract, r("pay", h, h + 1), Op.add)
+        ts(r("rk", 0, 2), r("rs", 0, 2), -0.5, Op.mult, 128.0, Op.add)
         tr(r("tb", 0, 64), r("rpb", 0, 64))
-        for i in (0, 1):
-            ts(r("dx", 64 * i, 64 * i + 64), r("tb", 0, 64), cf(6 + i), Op.subtract)
-        for i in (0, 1):
+        tt(r("w2", 0, 2), r("rk", 0, 2), r("ib", 0, 2), Op.add)
+        for i in range(3):
+            ts(r("dx", 64 * i, 64 * i + 64), r("tb", 0, 64), cf(14 + i), Op.subtract, float(2 ** 18), Op.mult)
+        ts(r("tk", 0, 2), r("w2", 0, 2), 31.5, Op.is_lt)
+        for i in range(3):
             red(r("pt", i, i + 1), r("dx", 64 * i, 64 * i + 64), Op.min, absolute=True)
-        spread("pt", 2)
-        for i in (0, 1):
-            red(r("vi", i, i + 1), r("pt", i, 8, st=2), Op.min)
-        more = t < R - 1
-        ts(r("vi", 2, 4), r("vi", 0, 2), 255, Op.bitwise_and)
+        ts(r("w3", 0, 2), r("rk", 0, 2), float(P + S * t), Op.add)
+        spread("pt", 3, lambda: tt(r("z2", 0, 2), r("w3", 0, 2), r("tk", 0, 2), Op.mult))
         if more:
-            ts(r("vz", 0, 2), r("vi", 0, 2), float(2 ** 18), Op.is_ge, -10000.0, Op.mult)
-        ts(r("vi", 4, 6), r("vi", 0, 2), 8, Op.arith_shift_right)
+            tt(r("fl", 0, 2), r("fl", 0, 2), r("z2", 0, 2), Op.max)
+        else:
+            for h in (0, 1):
+                ts(r("rpd", 32 * h, 32 * h + 32), r("ones32", 0, 32), r("z2", h, h + 1), Op.mult, r("fl", h, h + 1), Op.max)
+        for i in range(3):
+            red(r("vi", i, i + 1), r("pt", i, 12, st=3), Op.min)
+        if not more:
+            tr(r("flt", 0, 64), r("rpd", 0, 64))
+            for a in range(4):
+                i_, o_ = r("flt", 0, 64, 32 * a, 32 * a + 1), r("flr", 64 * a, 64 * a + 64)
+                op("g", lambda: g.partition_broadcast(ap(o_), ap(i_), 128), [i_], [o_])
+        ts(r("vi", 4, 7), r("vi", 0, 3), 255, Op.bitwise_and)
         if more:
-            tt(r("vz", 2, 4), r("vi", 2, 4), r("vz", 0, 2), Op.add)
-        cp(r("offu", 0, 2), r("vi", 2, 4))
+            ts(r("vz", 0, 1), r("vi", 2, 3), float(2 ** 18), Op.is_ge, -10000.0, Op.mult)
+        ts(r("vi", 8, 10), r("vi", 0, 2), 8, Op.arith_shift_right)
+        cp(r("offu", 0, 2), r("vi", 4, 6))
         if more:
-            tt(r("vz", 4, 5), r("vz", 3, 4), r("vz", 2, 3), Op.subtract)
-        ts(r("offu", 2, 4), r("vi", 4, 6), float(P * t + P - 1), Op.min)
-        if more:
-            ts(r("my%d" % (t + 1), 0, 1), r("vz", 4, 5), cf(5), Op.mult, r("vz", 2, 3), Op.add)
+            tt(r("my%d" % (t + 1), 0, 1), r("vi", 6, 7), r("vz", 0, 1), Op.add)
             send_list(t + 1)
+        ts(r("offu", 2, 4), r("vi", 8, 10), float(P * t + P - 1), Op.min)
         pick("pk", 0, "qx", 256, "offu", 0, 2)
         pick("pk", 32, c, P * t + P, "offu", 2, 4)
         for b in range(4):
             mm("dec", b, 128, "eq", 128 * b, "pk", 0)
             act(r("od", 32 * b, 32 * b + 32), r("dec", 512 * b, 512 * b + 32), Fn.Copy)
-        tt(r("w2", 0, 2), r("rk", 0, 2), r("ib", 0, 2), Op.add)
-        ts(r("w3", 0, 2), r("rk", 0, 2), float(P + S * t), Op.add)
-        ts(r("tk", 0, 2), r("w2", 0, 2), 31.5, Op.is_lt)
-        tt(r("x2", 0, 2), r("w3", 0, 2), place2, Op.subtract)
-        tt(r("w2", 0, 2), r("x2", 0, 2), r("tk", 0, 2), Op.mult)
-        tt(r("fl", 0, 2), r("fl", 0, 2), r("w2", 0, 2), Op.add)
-        if not more:
-            for h in (0, 1):
-                ts(r("rpd", 32 * h, 32 * h + 32), r("ones32", 0, 32), r("fl", h, h + 1), Op.mult)
-            tr(r("flt", 0, 64), r("rpd", 0, 64))
-            for a in range(4):
-                i_, o_ = r("flt", 0, 64, 32 * a, 32 * a + 1), r("flr", 64 * a, 64 * a + 64)
-                op("g", lambda: g.partition_broadcast(ap(o_), ap(i_), 128), [i_], [o_])
-        tt(r("x2", 0, 2), r("q2", 0, 2), r("qs", 0, 2), Op.subtract)
         tt(r("y2", 0, 2), r("x2", 0, 2), r("tk", 0, 2), Op.mult)
+        if more:
+            settle(False)
+        else:
+            tt(r("flm", 0, 256), r("flr", 0, 256), r("m16", 0, 256), Op.mult)
         tt(r("qs", 0, 2), r("qs", 0, 2), r("y2", 0, 2), Op.add)
+        if not more:
+            scan(r("fls", 0, 256), r("seg", 0, 256), r("flm", 0, 256), 0.0, Op.mult, Op.add)
         for b in range(4):
             tt(r("ht", b, 128, st=4), r("dec", 512 * b + 32, 512 * b + 64), r("od", 32 * b, 32 * b + 32), Op.add)
         if more:
@@ -486,29 +482,41 @@ def rank_program(g, core, T, topo):
             f = P + S * t
             dmas("df%d" % t, [("y", T.finw[:, f:f + S].bitcast(dt.uint8), T[d][:, o:o + S].bitcast(dt.uint8), [r(d, o, o + S)], [r("finw", f, f + S)]),
                               ("y", T.finws[:, f:f + S], T[d + "s"][:, o:o + S], [r(d + "s", o, o + S)], [r("finws", f, f + S)])])
-            settle(False)
+            if t == 0:
+                quant("qw", "qws", 0, 256, "wt", 0, 1024)
+                ts(r("m16", 0, 256), r("c16", 0, 256), cf(1), Op.is_equal)
+            else:
+                ts(r("z2", 0, 2), place2, float(P * rank + 1), Op.add)
+                tt(r("w3", 0, 2), r("z2", 0, 2), r("tk0", 0, 2), Op.mult)
+                ts(r("pa2", 0, 2), r("w3", 0, 2), -1.0, Op.add)
             masks(t + 1)
-            chip_scores(t + 1)
         else:
             quant("finw", "finws", 320, 448, "ht", 0, 512)
-            quant("qw", "qws", 0, 256, "wt", 0, 1024)
-            ts(r("m16", 0, 256), r("c16", 0, 256), cf(1), Op.is_equal)
 
-    tt(r("flm", 0, 256), r("flr", 0, 256), r("m16", 0, 256), Op.mult)
-    scan(r("fls", 0, 256), r("seg", 0, 256), r("flm", 0, 256), 0.0, Op.mult, Op.add)
     for h in (0, 1):
         for u in (0, 1):
             cp(r("fo", 8 * h + u, 8 * h + 8, st=2), r("fls", (2 * h + u) * 16 + 15, 256, st=64))
+    cp(r("qi", 0, 2), r("qs", 0, 2))
     pick("fin", 0, "finw", 352, "fo", 0, 16)
     for o in (0, 1):
         mm("yy", o, 256, "qw", 128 * o, "fin", 0)
+    ts(r("qi", 2, 4), r("qi", 0, 2), 18, Op.arith_shift_right)
+    ts(r("tk", 0, 2), r("qs", 0, 2), 0.0, Op.is_ge)
+    cp(r("w3", 0, 2), r("qi", 2, 4))
+    for h in (0, 1):
+        ts(r("e8", 4 * h, 4 * h + 4), r("kk8", 4 * h, 4 * h + 4), r("w3", h, h + 1), Op.is_equal)
+    tt(r("u8", 0, 8), r("e8", 0, 8), nbo, Op.mult)
+    for h in (0, 1):
+        red(r("w2", h, h + 1), r("u8", 4 * h, 4 * h + 4), Op.add)
     lst = [("y", T.oc[:], T.fin[:].bitcast(dt.uint8), [r("fin", 0, 256)], [])]
     lst += [("y", T.osc[4 * k:4 * k + 4, :], T.fins[32 * k:32 * k + 4, :], [r("fins", 0, 256)], []) for k in range(4)]
     cp(r("sy", 0, 256), r("yy", 0, 256))
     act(r("sy", 256, 512), r("yy", 512, 768), Fn.Copy)
     lst += [("y", T.y[:, 0:256], T.sy[:, 0:256], [r("sy", 0, 256)], []), ("s", T.y[:, 256:512], T.sy[:, 256:512], [r("sy", 256, 512)], [])]
     dmas("dout", lst)
-    parents()
+    tt(r("x2", 0, 2), r("w2", 0, 2), r("pa2", 0, 2), Op.subtract)
+    tt(r("y2", 0, 2), r("x2", 0, 2), r("tk", 0, 2), Op.mult)
+    tt(r("pa2", 0, 2), r("pa2", 0, 2), r("y2", 0, 2), Op.add)
     dmas("dpa", [("y", T.pa[0:1, 128 * h:128 * h + 128], T.pa2[:, h:h + 1], [r("pa2", h, h + 1)], []) for h in (0, 1)])
     for sem in cnt:
         if known["g"].get(sem, 0) < cnt[sem]:

@@ -3,55 +3,60 @@ from concourse.bass import DstId, RemoteDMATransfer
 from concourse.mybir import dt, AluOpType as Op, AxisListType, ActivationFunctionType as Fn
 
 F8 = "float8_e4m3fn_x4"
-W0, W1, W2, WF = 352, 608, 864, 448
+XB = (256, 608, 864)
+WC = tuple(b + 256 for b in XB)
+WF = 448
+TAB, NONE, SPARE = 2312, 2048, 2056
+ZW = 769
+LOW = -9e29
+MAGIC = 1.5 * 2.0 ** 23
 SCRATCH = {
     "xt": ("sbuf", [128, 1024], "bfloat16"), "wt": ("sbuf", [128, 1024], "bfloat16"),
     "qx": ("sbuf", [128, 256], F8), "qxs": ("sbuf", [128, 256], "uint8"),
-    "qw": ("sbuf", [128, 256], F8), "qws": ("sbuf", [128, 256], "uint8"),
+    "qw": ("sbuf", [128, 256], F8), "qws": ("sbuf", [128, 256], "uint8"), "half": ("sbuf", [128, 128], "bfloat16"),
     "et": ("sbuf", [128, 2048], "bfloat16"), "eq": ("sbuf", [128, 512], F8), "eqs": ("sbuf", [128, 512], "uint8"),
-    "comb0": ("sbuf", [128, W0], F8), "comb0s": ("sbuf", [128, W0], "uint8"),
-    "comb1": ("sbuf", [128, W1], F8), "comb1s": ("sbuf", [128, W1], "uint8"),
-    "comb2": ("sbuf", [128, W2], F8), "comb2s": ("sbuf", [128, W2], "uint8"),
+    "comb0": ("sbuf", [128, WC[0]], F8), "comb0s": ("sbuf", [128, WC[0]], "uint8"),
+    "comb1": ("sbuf", [128, WC[1]], F8), "comb1s": ("sbuf", [128, WC[1]], "uint8"),
+    "comb2": ("sbuf", [128, WC[2]], F8), "comb2s": ("sbuf", [128, WC[2]], "uint8"),
     "finw": ("sbuf", [128, WF], F8), "finws": ("sbuf", [128, WF], "uint8"),
     "fin": ("sbuf", [128, 256], F8), "fins": ("sbuf", [128, 256], "uint8"),
     "pk": ("sbuf", [128, 128], F8), "pks": ("sbuf", [128, 128], "uint8"),
     "ht": ("sbuf", [128, 512], "bfloat16"), "od": ("sbuf", [128, 128], "float32"),
     "sdw": ("sbuf", [128, 2], "int32"), "nbw": ("sbuf", [128, 64], "int32"),
     "sdu": ("sbuf", [128, 2], "uint16"), "sdf": ("sbuf", [128, 4], "float32"),
-    "nbof": ("sbuf", [128, 2], "uint16"), "nbo": ("sbuf", [128, 16], "float32"), "nbx": ("sbuf", [128, 8], "float32"),
-    "pint": ("sbuf", [128, 1], "int32"), "pidx": ("sbuf", [128, 1], "float32"), "icol": ("sbuf", [128, 128], "float32"),
+    "nbof": ("sbuf", [128, 2], "uint16"), "nbo": ("sbuf", [128, 16], "float32"), "nbn": ("sbuf", [128, 8], "float32"),
+    "nb2": ("sbuf", [128, 8], "float32"), "nbu": ("sbuf", [128, 8], "uint16"),
+    "pint": ("sbuf", [128, 1], "int32"), "pidx": ("sbuf", [128, 1], "float32"),
     "c16": ("sbuf", [128, 256], "float32"), "kk8": ("sbuf", [128, 8], "float32"), "plc": ("sbuf", [128, 8], "float32"),
     "ic": ("sbuf", [128, 256], "float32"), "ci": ("sbuf", [128, 16], "int32"), "cf": ("sbuf", [128, 32], "float32"),
     "plm": ("sbuf", [128, 256], "float32"), "ste": ("sbuf", [128, 512], "bfloat16"),
-    "ones32": ("sbuf", [128, 32], "float32"), "c256": ("sbuf", [128, 32], "float32"), "ones": ("sbuf", [128, 256], "bfloat16"),
-    "m16": ("sbuf", [128, 256], "float32"), "seg": ("sbuf", [128, 256], "float32"), "c8": ("sbuf", [128, 8], "float32"),
-    "my0": ("sbuf", [128, 4], "float32"), "my1": ("sbuf", [128, 4], "float32"), "my2": ("sbuf", [128, 4], "float32"),
-    "land0": ("sbuf", [128, 8], "float32"), "land1": ("sbuf", [128, 8], "float32"), "land2": ("sbuf", [128, 8], "float32"),
-    "rpf": ("sbuf", [128, 256], "float16"), "ff": ("sbuf", [128, 256], "float16"),
-    "eqx": ("sbuf", [128, 2048], "bfloat16"), "sc": ("sbuf", [128, 2048], "bfloat16"), "prod": ("sbuf", [128, 2048], "float32"),
-    "m8": ("sbuf", [128, 8], "float32"), "n8": ("sbuf", [128, 8], "float32"), "o8": ("sbuf", [128, 8], "float32"),
-    "t8": ("sbuf", [128, 8], "float32"), "u8": ("sbuf", [128, 8], "float32"), "pl8": ("sbuf", [128, 8], "float32"),
-    "pkb": ("sbuf", [128, 8], "float32"), "pkc": ("sbuf", [128, 8], "float32"), "prc": ("sbuf", [128, 512], "float32"),
-    "sb": ("sbuf", [128, 16], "float32"), "sb1": ("sbuf", [128, 8], "float32"), "bst": ("sbuf", [128, 2], "float32"),
-    "ib": ("sbuf", [128, 2], "float32"), "rpa": ("sbuf", [128, 64], "float32"), "row": ("sbuf", [128, 256], "float32"),
+    "ones32": ("sbuf", [128, 32], "float32"), "c256": ("sbuf", [128, 32], "float32"),
+    "posc": ("sbuf", [128, 768], "float32"), "tab": ("sbuf", [128, TAB], "float32"), "loc": ("sbuf", [128, TAB], "float32"),
+    "hma": ("sbuf", [128, 256], "float32"), "hm": ("sbuf", [128, 256], "float32"),
+    "negm": ("sbuf", [128, 128], "float32"), "segm": ("sbuf", [128, 128], "float32"),
+    "my0": ("sbuf", [128, 2], "uint16"), "my1": ("sbuf", [128, 2], "uint16"), "my2": ("sbuf", [128, 2], "uint16"), "my3": ("sbuf", [128, 2], "uint16"),
+    "land0": ("sbuf", [128, 16], "uint16"), "land1": ("sbuf", [128, 16], "uint16"), "land2": ("sbuf", [128, 16], "uint16"),
+    "lk": ("sbuf", [128, 128], "float32"), "pv": ("sbuf", [128, 128], "float32"), "zo": ("sbuf", [128, 8], "uint16"),
+    "zsb": ("sbuf", [128, 2 * ZW], "float32"), "gs": ("sbuf", [128, 128], "float32"), "sbx": ("sbuf", [128, 128], "float32"),
+    "m8": ("sbuf", [128, 8], "float32"), "n8": ("sbuf", [128, 8], "float32"), "c8": ("sbuf", [128, 8], "float32"),
+    "kkh": ("sbuf", [128, 8], "float32"), "pls": ("sbuf", [128, 8], "float32"), "pl8": ("sbuf", [128, 8], "float32"),
+    "e8": ("sbuf", [128, 8], "float32"), "t8": ("sbuf", [128, 8], "float32"), "u8": ("sbuf", [128, 8], "float32"),
+    "bst": ("sbuf", [128, 2], "float32"), "ib": ("sbuf", [128, 2], "float32"), "ibh": ("sbuf", [128, 2], "float32"),
+    "rpa": ("sbuf", [128, 64], "float32"), "row": ("sbuf", [128, 256], "float32"),
     "ed": ("sbuf", [128, 1024], "bfloat16"), "cm": ("sbuf", [128, 1024], "bfloat16"), "sg": ("sbuf", [128, 512], "bfloat16"),
     "rs": ("sbuf", [128, 2], "float32"), "rk": ("sbuf", [128, 2], "float32"),
-    "e8": ("sbuf", [128, 8], "float32"), "q2": ("sbuf", [128, 2], "float32"), "qi": ("sbuf", [128, 4], "int32"),
-    "qf": ("sbuf", [128, 2], "float32"), "qs": ("sbuf", [128, 2], "float32"), "x2": ("sbuf", [128, 2], "float32"),
-    "y2": ("sbuf", [128, 2], "float32"), "z2": ("sbuf", [128, 2], "float32"),
+    "q2": ("sbuf", [128, 2], "float32"), "qk": ("sbuf", [128, 2], "float32"), "qf": ("sbuf", [128, 2], "float32"),
+    "qs": ("sbuf", [128, 2], "float32"), "x2": ("sbuf", [128, 2], "float32"), "y2": ("sbuf", [128, 2], "float32"), "z2": ("sbuf", [128, 2], "float32"),
     "pay": ("sbuf", [128, 2], "float32"), "rpb": ("sbuf", [128, 64], "float32"), "tb": ("sbuf", [128, 64], "float32"),
-    "pt": ("sbuf", [128, 12], "float32"), "dx": ("sbuf", [128, 192], "float32"),
+    "pt": ("sbuf", [128, 8], "float32"), "dx": ("sbuf", [128, 128], "float32"),
     "vz": ("sbuf", [128, 4], "float32"), "vi": ("sbuf", [128, 12], "int32"), "offu": ("sbuf", [128, 4], "uint16"),
     "tk0": ("sbuf", [128, 2], "float32"), "tk": ("sbuf", [128, 2], "float32"), "nf": ("sbuf", [128, 2], "float32"),
-    "nfm": ("sbuf", [128, 2], "float32"), "fx": ("sbuf", [128, 2], "float32"), "fl": ("sbuf", [128, 2], "float32"),
-    "pa2": ("sbuf", [128, 2], "float32"), "w2": ("sbuf", [128, 2], "float32"), "w3": ("sbuf", [128, 2], "float32"),
-    "rpd": ("sbuf", [128, 64], "float32"), "flt": ("sbuf", [128, 64], "float32"), "flr": ("sbuf", [128, 256], "float32"),
-    "flm": ("sbuf", [128, 256], "float32"), "fls": ("sbuf", [128, 256], "float32"), "fo": ("sbuf", [128, 16], "uint16"),
-    "sy": ("sbuf", [128, 512], "float32"),
+    "nfm": ("sbuf", [128, 2], "float32"), "pa2": ("sbuf", [128, 2], "float32"), "w2": ("sbuf", [128, 2], "float32"), "w3": ("sbuf", [128, 2], "float32"),
+    "flx": ("sbuf", [128, 256], "float32"), "fo": ("sbuf", [128, 16], "uint16"), "sy": ("sbuf", [128, 512], "float32"),
     "dec": ("psum", [128, 2048], "float32"), "zz": ("psum", [128, 1024], "float32"), "yy": ("psum", [128, 1024], "float32"),
 }
 SEMAPHORES = ["v", "s", "p", "gp", "dsd", "dx", "dnb", "dw", "arl0", "arl1", "arl2", "arc0", "arc1", "arc2",
-              "arn0", "arn1", "arn2", "dc0", "dc1", "df0", "df1", "dfx", "dout", "dpa", "sent"]
+              "arn0", "arn1", "arn2", "dc0", "dc1", "df0", "df1", "dout", "dpa", "sent"]
 
 
 def r(name, c0, c1, p0=0, p1=128, st=1):
@@ -179,6 +184,12 @@ def rank_program(g, core, T, topo):
     def quant(c, s, a, b, src, x0, x1):
         op("v", lambda: g.vector.quantize_mx(T[c][:, a:b], T[s][:, a:b], T[src][:, x0:x1]), [r(src, x0, x1)], [r(c, a, b), r(s, a, b)])
 
+    def gather(out, win, off):
+        op("v", lambda: g.vector.tensor_copy(ap(out), ap(win).indirect(ap(off))), [win, off], [out])
+
+    def scatter(win, off, a):
+        op("v", lambda: g.vector.tensor_copy(ap(win).indirect(ap(off)), ap(a)), [a, off], [win])
+
     def pick(c2, a2, c1, w, off, o0, o1):
         k = 16 * (o1 - o0)
         s2, s1 = c2 + "s", c1 + "s"
@@ -221,8 +232,8 @@ def rank_program(g, core, T, topo):
             note("far", [], [a], (sem, total, {}, seq[0]))
 
     def send_list(t):
-        send("arl%d" % t, "arl%d" % t, T["my%d" % t][:, 0:1], lambda q: T["land%d" % t][:, block(q):block(q) + 1], [r("my%d" % t, 0, 1)])
-        landed("arl%d" % t, len(fe) * len(far) + len(ne), [r("land%d" % t, 0, 7)])
+        send("arl%d" % t, "arl%d" % t, T["my%d" % t][:, 0:2], lambda q: T["land%d" % t][:, 2 * block(q):2 * block(q) + 2], [r("my%d" % t, 0, 2)])
+        landed("arl%d" % t, len(fe) * len(far) + len(ne), [r("land%d" % t, 0, 14)])
 
     def send_cols(t):
         c, b, fs, nr = "comb%d" % t, P * t, "arc%d" % t, "arn%d" % t
@@ -232,6 +243,10 @@ def rank_program(g, core, T, topo):
         landed(nr, 2 * len(ne), [r(c, w, w + S), r(c + "s", w, w + S)])
         landed(fs, 2 * len(fe) * len(far), [r(c, b, w), r(c + "s", b, w)])
 
+    def copies(src, s0, dst, d0, w):
+        return [("y", T[dst][:, d0:d0 + w].bitcast(dt.uint8), T[src][:, s0:s0 + w].bitcast(dt.uint8), [r(src, s0, s0 + w)], [r(dst, d0, d0 + w)]),
+                ("y", T[dst + "s"][:, d0:d0 + w], T[src + "s"][:, s0:s0 + w], [r(src + "s", s0, s0 + w)], [r(dst + "s", d0, d0 + w)])]
+
     sdl = [(T.sdw[16 * a:16 * a + 16, :], r("sdw", 0, 2, 16 * a, 16 * a + 16)) for a in range(8)]
     dmas("dx", [("s", T.xt[:], T.x[:], [], [r("xt", 0, 1024)])])
     dmas("dsd", [("y" if i % 2 == 0 else "s", o, T.sd[:], [], [w]) for i, (o, w) in enumerate(sdl)])
@@ -239,22 +254,32 @@ def rank_program(g, core, T, topo):
     dmas("dw", [("y", T.wt[:], T.w[:], [], [r("wt", 0, 1024)])])
 
     pint, pidx = r("pint", 0, 1), r("pidx", 0, 1)
+    iota(r("posc", 0, 256), [[1, 256]], 1, 0)
     iota(pint, [[0, 1]], 0, 1, False)
     iota(pidx, [[0, 1]], 0, 1)
-    iota(r("icol", 0, 128), [[1, 128]], 0, 0)
-    iota(r("kk8", 0, 8), [[0, 2], [-1, 4]], 3, 0)
+    iota(r("kk8", 0, 8), [[0, 2], [-1, 4]], 4, 0)
     iota(r("plc", 0, 8), [[128, 2], [0, 4]], 0, 1)
-    iota(r("ic", 0, 256), [[32, 4], [128, 2], [1, 32]], 0, 0)
     ci = lambda i: r("ci", i, i + 1)
     cf = lambda i: r("cf", i, i + 1)
     fill(r("ste", 0, 512, st=2), 0.0)
     fill(r("ste", 1, 512, st=2), 1.0)
-    for b in range(4):
-        act(r("et", 512 * b, 512 * b + 512), r("ste", 0, 512), Fn.Copy, scale=0.0)
-    act(r("ht", 0, 512), r("ste", 0, 512), Fn.Copy, scale=0.0)
-    fill(r("ones32", 0, 32), 1.0)
-    fill(r("c256", 0, 32), 256.0)
-    fill(r("ones", 0, 256), 1.0)
+    for b in range(3):
+        act(r("tab", 512 * b, 512 * b + 512), r("ste", 0, 512), Fn.Copy, scale=0.0)
+    fill(r("tab", 1536, TAB), 0.0)
+    fill(r("half", 0, 128), 0.5)
+    fill(r("ht", 0, 512), 0.0)
+    act(r("et", 0, 512), r("ste", 0, 512), Fn.Copy, scale=0.0)
+
+    ts(r("my0", 0, 2), r("sdw", 0, 2), float(P * rank), Op.add)
+    send_list(0)
+    cp(r("sdu", 0, 2), r("sdw", 0, 2))
+    quant("qx", "qxs", 0, 256, "xt", 0, 1024)
+    pick("comb0", 224, "qx", 256, "sdu", 0, 2)
+    send_cols(0)
+    iota(r("c16", 0, 256), [[0, 16], [1, 16]], 0, 0)
+    iota(r("ic", 0, 256), [[32, 4], [128, 2], [1, 32]], 0, 0)
+
+    ts(ci(7), pint, 4, Op.arith_shift_right)
     ts(ci(0), pint, 31, Op.bitwise_and)
     ts(ci(1), pint, 15, Op.bitwise_and)
     ts(ci(2), pint, 96, Op.bitwise_and)
@@ -262,113 +287,93 @@ def rank_program(g, core, T, topo):
     ts(ci(4), pint, 64, Op.bitwise_and)
     ts(ci(5), pint, 3, Op.bitwise_and)
     ts(ci(6), pint, 4, Op.bitwise_and)
-    ts(ci(7), pint, 4, Op.arith_shift_right)
-    cp(r("cf", 0, 8), r("ci", 0, 8))
     cp(cf(10), pidx)
+    cp(r("cf", 0, 8), r("ci", 0, 8))
     ts(cf(11), pidx, 128.0, Op.add)
-    ts(cf(8), cf(0), 16.0, Op.is_ge)
+    ts(cf(17), cf(5), 16.0, Op.mult, cf(7), Op.add)
+    ts(cf(9), cf(0), 16.0, Op.is_ge)
+    ts(r("nbof", 0, 1), cf(6), 2.0, Op.mult, cf(17), Op.add)
     ts(cf(14), cf(1), 2.0, Op.mult)
     ts(cf(15), cf(1), 2.0, Op.mult, 32.0, Op.add)
-    ts(cf(16), cf(0), 2.0, Op.mult)
-    ts(cf(17), cf(5), 16.0, Op.mult, cf(7), Op.add)
-    ts(cf(21), cf(3), -2.0, Op.mult, cf(2), Op.add)
-    ts(cf(22), cf(4), -2.0, Op.mult, cf(2), Op.add)
-    ts(cf(18), cf(6), 2.0, Op.mult, cf(17), Op.add)
-    ts(cf(23), cf(4), -2.0, Op.mult, cf(21), Op.add)
-    ts(r("cf", 12, 14), r("cf", 10, 12), -0.5, Op.add, -2.0 ** -120, Op.mult)
-    cp(r("nbof", 0, 1), cf(18))
-    cp(r("nbof", 1, 2), cf(18))
     place = lambda h: r("cf", 10 + h, 11 + h)
     place2 = r("cf", 10, 12)
-
+    tab = r("tab", 0, TAB)
+    for b in range(1, 4):
+        act(r("et", 512 * b, 512 * b + 512), r("ste", 0, 512), Fn.Copy, scale=0.0)
+    scatter(tab, r("my0", 0, 2), r("posc", 224, 256))
     cp(r("sdf", 0, 2), r("sdw", 0, 2))
-    cp(r("sdu", 0, 2), r("sdw", 0, 2))
-    tt(r("sdf", 2, 3), r("sdf", 1, 2), r("sdf", 0, 1), Op.subtract)
-    ts(r("my0", 0, 1), r("sdf", 2, 3), cf(8), Op.mult, r("sdf", 0, 1), Op.add)
-    send_list(0)
-    quant("qx", "qxs", 0, 256, "xt", 0, 1024)
-    quant("comb0", "comb0s", 224, 352, "xt", 0, 512)
-    pick("comb0", 224, "qx", 256, "sdu", 0, 2)
-    send_cols(0)
-    dmas("dfx", [("y", T.finw[:, 0:P].bitcast(dt.uint8), T.qx[:].bitcast(dt.uint8), [r("qx", 0, P)], [r("finw", 0, P)]),
-                 ("y", T.finws[:, 0:P], T.qxs[:], [r("qxs", 0, P)], [r("finws", 0, P)])])
-    iota(r("c16", 0, 256), [[0, 16], [1, 16]], 0, 0)
-
-    for d, b in enumerate((2, 21, 22, 23)):
-        act(r("plm", 64 * d, 64 * d + 64), r("ic", 64 * d, 64 * d + 64), Fn.Identity, bias=cf(b))
-    for h in (0, 1):
-        act(r("ed", 512 * h + 1, 512 * h + 512, st=2), r("plm", 0, 256), Fn.Identity, bias=r("cf", 12 + h, 13 + h), scale=2.0 ** -120)
-    act(r("seg", 0, 256), r("c16", 0, 256), Fn.Sign)
+    ts(cf(21), cf(3), -2.0, Op.mult, cf(2), Op.add)
     op("v", lambda: g.vector.tensor_copy(T.nbo[:, 0:16], T.nbw[:, 0:64].indirect(T.nbof[:, 0:1])), [r("nbw", 0, 64), r("nbof", 0, 1)], [r("nbo", 0, 16)])
-    nbo = r("nbo", 0, 8)
-    ts(r("rpa", 0, 32), r("ones32", 0, 32), r("my0", 0, 1), Op.mult)
-    fill(r("sb", 0, 16), -9e29)
-    fill(r("pl8", 0, 8), float(-2 ** 22))
+    nb2 = r("nb2", 0, 8)
+    tt(r("sdf", 2, 3), r("sdf", 1, 2), r("sdf", 0, 1), Op.subtract)
+    ts(r("nbn", 0, 8), r("nbo", 0, 8), 0.0, Op.is_lt, NONE + 1.0, Op.mult)
+    fill(r("ones32", 0, 32), 1.0)
+    ts(r("sdf", 3, 4), r("sdf", 2, 3), cf(9), Op.mult, r("sdf", 0, 1), Op.add)
+    tt(nb2, r("nbo", 0, 8), r("nbn", 0, 8), Op.add)
+    fill(r("c256", 0, 32), 256.0)
+    ts(r("rpa", 0, 32), r("ones32", 0, 32), r("sdf", 3, 4), Op.mult)
+    ts(cf(22), cf(4), -2.0, Op.mult, cf(2), Op.add)
+    ts(cf(19), cf(1), -1024.0, Op.mult, 15360.0, Op.add)
     tr(r("tb", 0, 32), r("rpa", 0, 32))
-    fill(r("qs", 0, 2), -1.0)
-    ts(r("m8", 0, 8), r("kk8", 0, 8), float(2 ** 18), Op.mult, float(-2 ** 22), Op.add)
+    ts(cf(23), cf(4), -2.0, Op.mult, cf(21), Op.add)
+    ts(cf(20), cf(19), -float(ZW), Op.add)
     for h in (0, 1):
         ts(r("rpb", 32 * h, 32 * h + 32), r("tb", 0, 32), place(h), Op.is_equal)
-    tt(r("c8", 0, 8), r("m8", 0, 8), r("plc", 0, 8), Op.add)
+    ts(r("cf", 12, 14), r("cf", 10, 12), -0.5, Op.add, -2.0 ** -120, Op.mult)
     for h in (0, 1):
         red(r("tk0", h, h + 1), r("rpb", 32 * h, 32 * h + 32), Op.add)
-    cp(r("fl", 0, 2), place2)
+    ts(r("hma", 0, 256), r("c16", 0, 256), cf(1), Op.is_equal)
+    act(r("hm", 0, 256), r("hma", 0, 256), Fn.Copy, bias=1024.0, scale=-66560.0)
 
     def settle(first):
         if first:
             ts(r("nf", 0, 2), r("tk0", 0, 2), -1.0, Op.mult, 1.0, Op.add)
         else:
             tt(r("nf", 0, 2), r("nf", 0, 2), r("tk", 0, 2), Op.subtract)
-        ts(r("nfm", 0, 2), r("nf", 0, 2), -1.0, Op.add)
-        ts(r("fx", 0, 2), r("nf", 0, 2), -1.0, Op.add, 9e29, Op.mult)
+        ts(r("nfm", 0, 2), r("nf", 0, 2), -float(NONE), Op.mult, float(NONE), Op.add)
         for h in (0, 1):
-            ts(r("nbx", 4 * h, 4 * h + 4), r("nbo", 4 * h, 4 * h + 4), r("nf", h, h + 1), Op.mult, r("nfm", h, h + 1), Op.add)
-        for h in (0, 1):
-            ts(r("sb", 8 * h, 8 * h + 4), r("sb", 8 * h, 8 * h + 4), r("nf", h, h + 1), Op.mult, r("fx", h, h + 1), Op.add)
+            ts(r("nbu", 4 * h, 4 * h + 4), r("nb2", 4 * h, 4 * h + 4), r("nf", h, h + 1), Op.mult, r("nfm", h, h + 1), Op.add)
 
     settle(True)
-    for b in range(4):
-        ts(r("et", 512 * b + b, 512 * b + 512, st=4), r("icol", 0, 128), pidx, Op.is_equal, 0.5, Op.mult)
-    for b in range(4):
-        quant("eq", "eqs", 128 * b, 128 * b + 128, "et", 512 * b, 512 * b + 512)
+    for d, b in enumerate((2, 21, 22, 23)):
+        act(r("plm", 64 * d, 64 * d + 64), r("ic", 64 * d, 64 * d + 64), Fn.Identity, bias=cf(b))
+    for h in (0, 1):
+        act(r("ed", 512 * h + 1, 512 * h + 512, st=2), r("plm", 0, 256), Fn.Identity, bias=r("cf", 12 + h, 13 + h), scale=2.0 ** -120)
+    for i in range(4):
+        z1 = min(512 * i + 512, 2 * ZW)
+        act(r("zsb", 512 * i, z1), r("ste", 0, z1 - 512 * i), Fn.Identity, bias=LOW, scale=0.0)
+    quant("comb0", "comb0s", XB[0], XB[0] + 256, "xt", 0, 1024)
+    ts(r("negm", 0, 128), r("c16", 0, 128), cf(1), Op.not_equal, LOW, Op.mult)
+    ts(r("segm", 0, 128), r("c16", 0, 128), 0.0, Op.is_equal, LOW, Op.mult)
+    ts(r("n8", 0, 8), r("plc", 0, 8), 1024.0, Op.mult, cf(19), Op.subtract)
+    fill(r("qs", 0, 2), -1.0)
+    ts(r("m8", 0, 8), r("n8", 0, 8), -0.5, Op.add, 2.0 ** -18, Op.mult)
+    for i in (0, 1):
+        ts(cf(24 + i), cf(1), float(SPARE - P * rank + S * rank + 16 * i), Op.add)
+    ts(r("kkh", 0, 8), r("kk8", 0, 8), -0.5, Op.add)
+    tt(r("c8", 0, 8), r("kkh", 0, 8), r("m8", 0, 8), Op.add)
     quant("pk", "pks", 0, 128, "xt", 0, 512)
+    for b in range(4):
+        e_, h_ = r("et", 512 * b + b, 512 * b + 512, st=4), r("half", 0, 128)
+        op("g", lambda: g.affine_select(ap(e_), ap(h_), [[-1, 128]], Op.is_equal, 0.0, 0, 1), [h_], [e_])
+    iota(r("posc", 256, 768), [[1, 512]], 257, 0)
+    iota(r("loc", P * rank, P * rank + P), [[1, P]], 0, 0)
+
+    def run_on(out, a, width):
+        scan(out, r("hm", 0, width), a, 0.0, Op.add, Op.max)
 
     def masks(t):
-        for m in range(8):
-            src = r("my%d" % t, 0, 1) if m == 7 else r("land%d" % t, m, m + 1)
-            ts(r("rpf", 32 * m, 32 * m + 32), r("ones32", 0, 32), src, Op.mult, float(P * (rank ^ (n - 1 - m))), Op.add)
-        tr(r("ff", 0, 256), r("rpf", 0, 256))
-        for i in range(8):
-            ts(r("eqx", 256 * i, 256 * i + 256), r("ff", 0, 256), r("nbx", i, i + 1), Op.is_equal, 256.0, Op.mult)
-        for i in range(8):
-            scan(r("sc", 256 * i, 256 * i + 256), r("eqx", 256 * i, 256 * i + 256), r("ones", 0, 256), 0.0, Op.max, Op.subtract)
-        for h in (0, 1):
-            mm("yy", h, 128, "qx", 128 * h, "comb%d" % t, P * t + 192)
-
-        def chip(i):
-            x = r("prc", 64 * i, 64 * i + 64)
-            tt(x, r("yy", 512 * (i // 4), 512 * (i // 4) + 64), r("eqx", 256 * i + 192, 256 * i + 256), Op.mult)
-            act(x, x, Fn.Identity, bias=r("pkc", i, i + 1), scale=1.0 / 256, accum=r("sb1", i, i + 1))
-
-        pos = r("sc", 255, 2048, st=256)
-        chip_bias = r("pkc", 0, 8)
-        ts(chip_bias, pos, 192.0, Op.is_lt, -9e29 / 64, Op.mult)
-        ts(r("t8", 0, 8), pos, 0.0, Op.is_lt, -9e29 / 192, Op.mult)
-        ts(r("u8", 0, 8), pos, 192.0, Op.is_ge, -9e29 / 192, Op.mult)
-        ts(r("n8", 0, 8), pos, 256.0, Op.mult)
-        ts(r("m8", 0, 8), pos, 0.0, Op.is_ge, float(2 ** 22 + 65536 * t), Op.mult)
-        for i in range(3):
-            chip(i)
-        tt(r("pkb", 0, 8), r("t8", 0, 8), r("u8", 0, 8), Op.add)
-        tt(r("o8", 0, 8), r("n8", 0, 8), r("c8", 0, 8), Op.add)
-        for i in range(3, 6):
-            chip(i)
-        tt(r("n8", 0, 8), r("m8", 0, 8), r("o8", 0, 8), Op.add)
-        for i in range(6, 8):
-            chip(i)
-        tt(r("pl8", 0, 8), r("pl8", 0, 8), r("n8", 0, 8), Op.max)
+        scatter(tab, r("land%d" % t, 0, 14), r("posc", P * t, P * t + 224))
+        gather(r("lk", 0, 128), r("tab", 0, SPARE), r("nbu", 0, 8))
+        run_on(r("pv", 0, 128), r("lk", 0, 128), 128)
+        ts(r("zo", 0, 4), r("pv", 15, 64, st=16), cf(19), Op.subtract)
+        ts(r("pls", 0, 8), r("pv", 15, 128, st=16), 2.0 ** -18, Op.mult)
+        ts(r("zo", 4, 8), r("pv", 79, 128, st=16), cf(20), Op.subtract)
+        tt(r("pl8", 0, 8), r("c8", 0, 8), r("pls", 0, 8), Op.add)
 
     masks(0)
+    for b in range(4):
+        quant("eq", "eqs", 128 * b, 128 * b + 128, "et", 512 * b, 512 * b + 512)
 
     def spread(buf, w, between=None):
         for b in range(4):
@@ -382,36 +387,31 @@ def rank_program(g, core, T, topo):
         c = "comb%d" % t
         more = t < R - 1
         for h in (0, 1):
-            mm("zz", h, 192, "qx", 128 * h, c, P * t)
-        for i in range(8):
-            h, k = i // 4, i % 4
-            blk = r("prod", 256 * i, 256 * i + 192)
-            tt(blk, r("zz", 512 * h, 512 * h + 192), r("eqx", 256 * i, 256 * i + 192), Op.mult)
-            act(blk, blk, Fn.Identity, bias=r("pkb", i, i + 1), scale=1.0 / 256, accum=r("sb", 8 * h + 4 + k, 8 * h + 5 + k))
-        for h in (0, 1):
-            tt(r("sb", 8 * h, 8 * h + 4), r("sb", 8 * h, 8 * h + 4), r("sb1", 4 * h, 4 * h + 4), Op.max)
+            mm("zz", h, P, "qx", 128 * h, c, P * t)
+        act(r("zsb", 1 + P * t, 1 + P * t + P), r("zz", 0, P), Fn.Copy)
+        cp(r("zsb", ZW + 1 + P * t, ZW + 1 + P * t + P), r("zz", 512, 512 + P))
+        op("v", lambda: g.vector.tensor_tensor(T.gs[:, 0:128], T.zsb[:, 0:2 * ZW].indirect(T.zo[:, 0:8]), T.negm[:, 0:128], Op.add),
+           [r("zsb", 0, 2 * ZW), r("zo", 0, 8), r("negm", 0, 128)], [r("gs", 0, 128)])
         if more:
             lst = []
             for t2 in range(t + 1, R):
-                d = "comb%d" % t2
-                for s, cast in (("", True), ("s", False)):
-                    i_, o_ = T[c + s][:, P * t:P * t + P], T[d + s][:, P * t:P * t + P]
-                    lst.append(("y", o_.bitcast(dt.uint8) if cast else o_, i_.bitcast(dt.uint8) if cast else i_,
-                                [r(c + s, P * t, P * t + P)], [r(d + s, P * t, P * t + P)]))
+                lst += copies(c, P * t, "comb%d" % t2, P * t, P)
+                if t == 0:
+                    lst += copies("qx", 0, "comb%d" % t2, XB[t2], P)
+            if t == 0:
+                lst += copies("qx", 0, "finw", 0, P)
             dmas("dc%d" % t, lst)
         for h in (0, 1):
-            red(r("bst", h, h + 1), r("sb", 8 * h, 8 * h + 8), Op.max)
+            red(r("bst", h, h + 1), r("gs", 64 * h, 64 * h + 64), Op.max)
         for h in (0, 1):
             ts(r("rpa", 32 * h, 32 * h + 32), r("ones32", 0, 32), r("bst", h, h + 1), Op.mult)
         ts(r("ib", 0, 2), r("bst", 0, 2), -5e29, Op.is_lt, 2048.0, Op.mult)
         tr(r("row", 0, 64), r("rpa", 0, 64))
-        tt(r("sb", 0, 4), r("sb", 0, 4), r("sb", 4, 8), Op.max)
-        spread("row", 64, lambda: tt(r("sb", 8, 12), r("sb", 8, 12), r("sb", 12, 16), Op.max))
-        for h in (0, 1):
-            act(r("ed", 512 * h, 512 * h + 512, st=2), r("row", 0, 256), Fn.Identity, bias=r("bst", h, h + 1), scale=-1.0)
-        for h in (0, 1):
-            ts(r("e8", 4 * h, 4 * h + 4), r("sb", 8 * h, 8 * h + 4), r("bst", h, h + 1), Op.is_equal)
-        tt(r("t8", 0, 8), r("e8", 0, 8), r("pl8", 0, 8), Op.mult)
+        scan(r("sbx", 0, 128), r("segm", 0, 128), r("gs", 0, 128), LOW, Op.add, Op.max)
+        spread("row", 64, lambda: ts(r("e8", 0, 4), r("sbx", 15, 64, st=16), r("bst", 0, 1), Op.is_equal))
+        ts(r("ed", 0, 512, st=2), r("row", 0, 256), -1.0, Op.mult, r("bst", 0, 1), Op.add)
+        act(r("ed", 512, 1024, st=2), r("row", 0, 256), Fn.Identity, bias=r("bst", 1, 2), scale=-1.0)
+        ts(r("e8", 4, 8), r("sbx", 79, 128, st=16), r("bst", 1, 2), Op.is_equal)
 
         def ahead(h):
             x = 512 * h
@@ -419,72 +419,66 @@ def rank_program(g, core, T, topo):
             act(r("sg", 256 * h, 256 * h + 256), r("cm", x + 1, x + 512, st=2), Fn.Sign, accum=r("rs", h, h + 1))
 
         ahead(0)
+        tt(r("t8", 0, 8), r("e8", 0, 8), r("pl8", 0, 8), Op.mult)
+        ahead(1)
         for h in (0, 1):
             red(r("q2", h, h + 1), r("t8", 4 * h, 4 * h + 4), Op.max)
-        cp(r("qi", 0, 2), r("q2", 0, 2))
-        ahead(1)
-        ts(r("qi", 2, 4), r("qi", 0, 2), 2 ** 18 - 1, Op.bitwise_and)
+        ts(r("ibh", 0, 2), r("ib", 0, 2), 0.5 - 2.0 ** -19, Op.add)
+        ts(r("qk", 0, 2), r("q2", 0, 2), MAGIC, Op.add, -MAGIC, Op.add)
         tt(r("x2", 0, 2), r("q2", 0, 2), r("qs", 0, 2), Op.subtract)
-        ts(r("qf", 0, 2), r("qi", 2, 4), 2.0 ** -18, Op.mult)
-        tt(r("pay", 0, 2), r("qf", 0, 2), r("ib", 0, 2), Op.add)
+        tt(r("qf", 0, 2), r("q2", 0, 2), r("qk", 0, 2), Op.subtract)
+        tt(r("pay", 0, 2), r("qf", 0, 2), r("ibh", 0, 2), Op.add)
         for h in (0, 1):
             ts(r("rpb", 32 * h, 32 * h + 32), r("c256", 0, 32), r("rs", h, h + 1), Op.subtract, r("pay", h, h + 1), Op.add)
         ts(r("rk", 0, 2), r("rs", 0, 2), -0.5, Op.mult, 128.0, Op.add)
         tr(r("tb", 0, 64), r("rpb", 0, 64))
         tt(r("w2", 0, 2), r("rk", 0, 2), r("ib", 0, 2), Op.add)
-        for i in range(3):
+        for i in range(2):
             ts(r("dx", 64 * i, 64 * i + 64), r("tb", 0, 64), cf(14 + i), Op.subtract, float(2 ** 18), Op.mult)
-        ts(r("tk", 0, 2), r("w2", 0, 2), 31.5, Op.is_lt)
-        for i in range(3):
+        for i in range(2):
             red(r("pt", i, i + 1), r("dx", 64 * i, 64 * i + 64), Op.min, absolute=True)
-        ts(r("w3", 0, 2), r("rk", 0, 2), float(P + S * t), Op.add)
-        spread("pt", 3, lambda: tt(r("z2", 0, 2), r("w3", 0, 2), r("tk", 0, 2), Op.mult))
-        if more:
-            tt(r("fl", 0, 2), r("fl", 0, 2), r("z2", 0, 2), Op.max)
-        else:
-            for h in (0, 1):
-                ts(r("rpd", 32 * h, 32 * h + 32), r("ones32", 0, 32), r("z2", h, h + 1), Op.mult, r("fl", h, h + 1), Op.max)
-        for i in range(3):
-            red(r("vi", i, i + 1), r("pt", i, 12, st=3), Op.min)
-        if not more:
-            tr(r("flt", 0, 64), r("rpd", 0, 64))
-            for a in range(4):
-                i_, o_ = r("flt", 0, 64, 32 * a, 32 * a + 1), r("flr", 64 * a, 64 * a + 64)
-                op("g", lambda: g.partition_broadcast(ap(o_), ap(i_), 128), [i_], [o_])
-        ts(r("vi", 4, 7), r("vi", 0, 3), 255, Op.bitwise_and)
-        if more:
-            ts(r("vz", 0, 1), r("vi", 2, 3), float(2 ** 18), Op.is_ge, -10000.0, Op.mult)
-        ts(r("vi", 8, 10), r("vi", 0, 2), 8, Op.arith_shift_right)
-        cp(r("offu", 0, 2), r("vi", 4, 6))
-        if more:
-            tt(r("my%d" % (t + 1), 0, 1), r("vi", 6, 7), r("vz", 0, 1), Op.add)
-            send_list(t + 1)
+        ts(r("tk", 0, 2), r("w2", 0, 2), 31.5, Op.is_lt)
+        spread("pt", 2, lambda: tt(r("y2", 0, 2), r("x2", 0, 2), r("tk", 0, 2), Op.mult))
+        for i in range(2):
+            red(r("vi", i, i + 1), r("pt", i, 8, st=2), Op.min)
+        ts(r("vi", 4, 6), r("vi", 0, 2), 10, Op.arith_shift_right)
+        ts(r("vi", 8, 10), r("vi", 0, 2), 1023, Op.bitwise_and)
+        ts(r("vz", 0, 2), r("vi", 0, 2), float(2 ** 18), Op.is_ge, 8192.0, Op.mult)
+        ts(r("offu", 0, 2), r("vi", 4, 6), P - 1.0, Op.min, float(XB[t]), Op.add)
         ts(r("offu", 2, 4), r("vi", 8, 10), float(P * t + P - 1), Op.min)
-        pick("pk", 0, "qx", 256, "offu", 0, 2)
-        pick("pk", 32, c, P * t + P, "offu", 2, 4)
+        tt(r("vz", 2, 4), r("vi", 4, 6), r("vz", 0, 2), Op.add)
+        pick("pk", 0, c, WC[t], "offu", 0, 4)
+        my = "my%d" % (t + 1)
+        for i in range(2):
+            ts(r(my, i, i + 1), r("vz", 2 + i, 3 + i), cf(24 + i), Op.min, float(P * rank), Op.add)
+        if more:
+            send_list(t + 1)
         for b in range(4):
             mm("dec", b, 128, "eq", 128 * b, "pk", 0)
             act(r("od", 32 * b, 32 * b + 32), r("dec", 512 * b, 512 * b + 32), Fn.Copy)
-        tt(r("y2", 0, 2), r("x2", 0, 2), r("tk", 0, 2), Op.mult)
-        if more:
-            settle(False)
-        else:
-            tt(r("flm", 0, 256), r("flr", 0, 256), r("m16", 0, 256), Op.mult)
         tt(r("qs", 0, 2), r("qs", 0, 2), r("y2", 0, 2), Op.add)
+        lv = P - 1 + S * t
+        scatter(r("loc", 0, TAB), r(my, 0, 2), r("posc", lv, lv + S))
+        fills = []
         if not more:
-            scan(r("fls", 0, 256), r("seg", 0, 256), r("flm", 0, 256), 0.0, Op.mult, Op.add)
+            run_on(r("flx", 0, 256), r("loc", P * rank, P * rank + P), 256)
+            ts(r("w3", 0, 2), r("qs", 0, 2), MAGIC, Op.add, -MAGIC, Op.add)
+            fills = [lambda: ts(r("fo", 0, 16), r("flx", 15, 256, st=16), cf(19), Op.subtract)]
+            fills += [lambda h=h: ts(r("e8", 4 * h, 4 * h + 4), r("kk8", 4 * h, 4 * h + 4), r("w3", h, h + 1), Op.is_equal) for h in (0, 1)]
+            fills += [lambda: ts(r("tk", 0, 2), r("qs", 0, 2), -0.75, Op.is_ge)]
         for b in range(4):
             tt(r("ht", b, 128, st=4), r("dec", 512 * b + 32, 512 * b + 64), r("od", 32 * b, 32 * b + 32), Op.add)
+            if fills:
+                fills[b]()
         if more:
             d, o = "comb%d" % (t + 1), P * (t + 1) + 224
             quant(d, d + "s", o, o + 128, "ht", 0, 512)
             send_cols(t + 1)
-            f = P + S * t
-            dmas("df%d" % t, [("y", T.finw[:, f:f + S].bitcast(dt.uint8), T[d][:, o:o + S].bitcast(dt.uint8), [r(d, o, o + S)], [r("finw", f, f + S)]),
-                              ("y", T.finws[:, f:f + S], T[d + "s"][:, o:o + S], [r(d + "s", o, o + S)], [r("finws", f, f + S)])])
+            dmas("df%d" % t, copies(d, o, "finw", P + S * t, S))
+            scatter(tab, r(my, 0, 2), r("posc", P * (t + 1) + 224, P * (t + 1) + 256))
+            settle(False)
             if t == 0:
                 quant("qw", "qws", 0, 256, "wt", 0, 1024)
-                ts(r("m16", 0, 256), r("c16", 0, 256), cf(1), Op.is_equal)
             else:
                 ts(r("z2", 0, 2), place2, float(P * rank + 1), Op.add)
                 tt(r("w3", 0, 2), r("z2", 0, 2), r("tk0", 0, 2), Op.mult)
@@ -492,28 +486,22 @@ def rank_program(g, core, T, topo):
             masks(t + 1)
         else:
             quant("finw", "finws", 320, 448, "ht", 0, 512)
+            tt(r("u8", 0, 8), r("e8", 0, 8), nb2, Op.mult)
 
-    for h in (0, 1):
-        for u in (0, 1):
-            cp(r("fo", 8 * h + u, 8 * h + 8, st=2), r("fls", (2 * h + u) * 16 + 15, 256, st=64))
-    cp(r("qi", 0, 2), r("qs", 0, 2))
-    pick("fin", 0, "finw", 352, "fo", 0, 16)
-    for o in (0, 1):
-        mm("yy", o, 256, "qw", 128 * o, "fin", 0)
-    ts(r("qi", 2, 4), r("qi", 0, 2), 18, Op.arith_shift_right)
-    ts(r("tk", 0, 2), r("qs", 0, 2), 0.0, Op.is_ge)
-    cp(r("w3", 0, 2), r("qi", 2, 4))
-    for h in (0, 1):
-        ts(r("e8", 4 * h, 4 * h + 4), r("kk8", 4 * h, 4 * h + 4), r("w3", h, h + 1), Op.is_equal)
-    tt(r("u8", 0, 8), r("e8", 0, 8), nbo, Op.mult)
+    bank = ("yy", "zz")
+    for m in (0, 1):
+        pick("fin", 128 * m, "finw", 352, "fo", 8 * m, 8 * m + 8)
+        for o in (0, 1):
+            mm(bank[m], o, 128, "qw", 128 * o, "fin", 128 * m)
     for h in (0, 1):
         red(r("w2", h, h + 1), r("u8", 4 * h, 4 * h + 4), Op.add)
-    lst = [("y", T.oc[:], T.fin[:].bitcast(dt.uint8), [r("fin", 0, 256)], [])]
-    lst += [("y", T.osc[4 * k:4 * k + 4, :], T.fins[32 * k:32 * k + 4, :], [r("fins", 0, 256)], []) for k in range(4)]
-    cp(r("sy", 0, 256), r("yy", 0, 256))
-    act(r("sy", 256, 512), r("yy", 512, 768), Fn.Copy)
-    lst += [("y", T.y[:, 0:256], T.sy[:, 0:256], [r("sy", 0, 256)], []), ("s", T.y[:, 256:512], T.sy[:, 256:512], [r("sy", 256, 512)], [])]
-    dmas("dout", lst)
+    cp(r("sy", 0, 128), r("yy", 0, 128))
+    act(r("sy", 256, 384), r("yy", 512, 640), Fn.Copy)
+    cp(r("sy", 128, 256), r("zz", 0, 128))
+    act(r("sy", 384, 512), r("zz", 512, 640), Fn.Copy)
+    dmas("dout", [("y", T.oc[:], T.fin[:].bitcast(dt.uint8), [r("fin", 0, 256)], [])] +
+         [("y", T.osc[4 * k:4 * k + 4, :], T.fins[32 * k:32 * k + 4, :], [r("fins", 0, 256)], []) for k in range(4)] +
+         [("y", T.y[:, 0:256], T.sy[:, 0:256], [r("sy", 0, 256)], []), ("s", T.y[:, 256:512], T.sy[:, 256:512], [r("sy", 256, 512)], [])])
     tt(r("x2", 0, 2), r("w2", 0, 2), r("pa2", 0, 2), Op.subtract)
     tt(r("y2", 0, 2), r("x2", 0, 2), r("tk", 0, 2), Op.mult)
     tt(r("pa2", 0, 2), r("pa2", 0, 2), r("y2", 0, 2), Op.add)

@@ -3,13 +3,12 @@ from concourse.bass import DstId, RemoteDMATransfer
 from concourse.mybir import dt, AluOpType as Op, AxisListType, ActivationFunctionType as Fn
 
 F8 = "float8_e4m3fn_x4"
-XB = (256, 608, 864)
-WC = tuple(b + 256 for b in XB)
+WC = (384, 608, 864)
 WF = 448
 TAB, NONE, SPARE = 2312, 2048, 2056
-ZW = 769
+ZW = 776
 LOW = -9e29
-MAGIC = 1.5 * 2.0 ** 23
+UNIT = 2.0 ** 19
 SCRATCH = {
     "xt": ("sbuf", [128, 1024], "bfloat16"), "wt": ("sbuf", [128, 1024], "bfloat16"),
     "qx": ("sbuf", [128, 256], F8), "qxs": ("sbuf", [128, 256], "uint8"),
@@ -21,39 +20,37 @@ SCRATCH = {
     "finw": ("sbuf", [128, WF], F8), "finws": ("sbuf", [128, WF], "uint8"),
     "fin": ("sbuf", [128, 256], F8), "fins": ("sbuf", [128, 256], "uint8"),
     "pk": ("sbuf", [128, 128], F8), "pks": ("sbuf", [128, 128], "uint8"),
-    "ht": ("sbuf", [128, 512], "bfloat16"), "od": ("sbuf", [128, 128], "float32"),
+    "ht": ("sbuf", [128, 512], "bfloat16"), "od": ("sbuf", [128, 128], "float32"), "own": ("sbuf", [128, 1024], "bfloat16"),
     "sdw": ("sbuf", [128, 2], "int32"), "nbw": ("sbuf", [128, 64], "int32"),
     "sdu": ("sbuf", [128, 2], "uint16"), "sdf": ("sbuf", [128, 4], "float32"),
     "nbof": ("sbuf", [128, 2], "uint16"), "nbo": ("sbuf", [128, 16], "float32"), "nbn": ("sbuf", [128, 8], "float32"),
-    "nb2": ("sbuf", [128, 8], "float32"), "nbu": ("sbuf", [128, 8], "uint16"),
+    "nb2": ("sbuf", [128, 8], "float32"), "nb3": ("sbuf", [128, 8], "float32"), "nbu": ("sbuf", [128, 8], "uint16"),
     "pint": ("sbuf", [128, 1], "int32"), "pidx": ("sbuf", [128, 1], "float32"),
-    "c16": ("sbuf", [128, 256], "float32"), "kk8": ("sbuf", [128, 8], "float32"), "plc": ("sbuf", [128, 8], "float32"),
+    "c16": ("sbuf", [128, 64], "float32"),
     "ic": ("sbuf", [128, 256], "float32"), "ci": ("sbuf", [128, 16], "int32"), "cf": ("sbuf", [128, 32], "float32"),
     "plm": ("sbuf", [128, 256], "float32"), "ste": ("sbuf", [128, 512], "bfloat16"),
-    "ones32": ("sbuf", [128, 32], "float32"), "c256": ("sbuf", [128, 32], "float32"),
+    "ones32": ("sbuf", [128, 32], "float32"),
     "posc": ("sbuf", [128, 768], "float32"), "tab": ("sbuf", [128, TAB], "float32"), "loc": ("sbuf", [128, TAB], "float32"),
-    "hma": ("sbuf", [128, 256], "float32"), "hm": ("sbuf", [128, 256], "float32"),
-    "negm": ("sbuf", [128, 128], "float32"), "segm": ("sbuf", [128, 128], "float32"),
+    "hma": ("sbuf", [128, 64], "float32"), "hm": ("sbuf", [128, 128], "float32"),
+    "negm": ("sbuf", [128, 64], "float32"), "segm": ("sbuf", [128, 64], "float32"),
     "my0": ("sbuf", [128, 2], "uint16"), "my1": ("sbuf", [128, 2], "uint16"), "my2": ("sbuf", [128, 2], "uint16"), "my3": ("sbuf", [128, 2], "uint16"),
     "land0": ("sbuf", [128, 16], "uint16"), "land1": ("sbuf", [128, 16], "uint16"), "land2": ("sbuf", [128, 16], "uint16"),
     "lk": ("sbuf", [128, 128], "float32"), "pv": ("sbuf", [128, 128], "float32"), "zo": ("sbuf", [128, 8], "uint16"),
     "zsb": ("sbuf", [128, 2 * ZW], "float32"), "gs": ("sbuf", [128, 128], "float32"), "sbx": ("sbuf", [128, 128], "float32"),
-    "m8": ("sbuf", [128, 8], "float32"), "n8": ("sbuf", [128, 8], "float32"), "c8": ("sbuf", [128, 8], "float32"),
-    "kkh": ("sbuf", [128, 8], "float32"), "pls": ("sbuf", [128, 8], "float32"), "pl8": ("sbuf", [128, 8], "float32"),
-    "e8": ("sbuf", [128, 8], "float32"), "t8": ("sbuf", [128, 8], "float32"), "u8": ("sbuf", [128, 8], "float32"),
-    "bst": ("sbuf", [128, 2], "float32"), "ib": ("sbuf", [128, 2], "float32"), "ibh": ("sbuf", [128, 2], "float32"),
+    "pl8": ("sbuf", [128, 8], "float32"), "e8": ("sbuf", [128, 8], "float32"), "ne8": ("sbuf", [128, 8], "float32"),
+    "t8": ("sbuf", [128, 8], "float32"), "u8": ("sbuf", [128, 8], "float32"),
+    "sf": ("sbuf", [128, 8], "float32"), "sn": ("sbuf", [128, 8], "float32"),
+    "bst": ("sbuf", [128, 2], "float32"), "cib": ("sbuf", [128, 64], "float32"),
     "rpa": ("sbuf", [128, 64], "float32"), "row": ("sbuf", [128, 256], "float32"),
     "ed": ("sbuf", [128, 1024], "bfloat16"), "cm": ("sbuf", [128, 1024], "bfloat16"), "sg": ("sbuf", [128, 512], "bfloat16"),
-    "rs": ("sbuf", [128, 2], "float32"), "rk": ("sbuf", [128, 2], "float32"),
-    "q2": ("sbuf", [128, 2], "float32"), "qk": ("sbuf", [128, 2], "float32"), "qf": ("sbuf", [128, 2], "float32"),
-    "qs": ("sbuf", [128, 2], "float32"), "x2": ("sbuf", [128, 2], "float32"), "y2": ("sbuf", [128, 2], "float32"), "z2": ("sbuf", [128, 2], "float32"),
-    "pay": ("sbuf", [128, 2], "float32"), "rpb": ("sbuf", [128, 64], "float32"), "tb": ("sbuf", [128, 64], "float32"),
+    "rs": ("sbuf", [128, 2], "float32"), "y2": ("sbuf", [128, 2], "float32"), "z2": ("sbuf", [128, 2], "float32"),
+    "rpb": ("sbuf", [128, 64], "float32"), "tb": ("sbuf", [128, 64], "float32"),
     "pt": ("sbuf", [128, 8], "float32"), "dx": ("sbuf", [128, 128], "float32"),
-    "vz": ("sbuf", [128, 4], "float32"), "vi": ("sbuf", [128, 12], "int32"), "offu": ("sbuf", [128, 4], "uint16"),
+    "vi": ("sbuf", [128, 8], "int32"), "offp": ("sbuf", [128, 2], "uint16"), "offo": ("sbuf", [128, 2], "uint16"),
     "tk0": ("sbuf", [128, 2], "float32"), "tk": ("sbuf", [128, 2], "float32"), "nf": ("sbuf", [128, 2], "float32"),
-    "nfm": ("sbuf", [128, 2], "float32"), "pa2": ("sbuf", [128, 2], "float32"), "w2": ("sbuf", [128, 2], "float32"), "w3": ("sbuf", [128, 2], "float32"),
+    "nfm": ("sbuf", [128, 2], "float32"), "pa2": ("sbuf", [128, 2], "float32"), "w3": ("sbuf", [128, 2], "float32"),
     "flx": ("sbuf", [128, 256], "float32"), "fo": ("sbuf", [128, 16], "uint16"), "sy": ("sbuf", [128, 512], "float32"),
-    "dec": ("psum", [128, 2048], "float32"), "zz": ("psum", [128, 1024], "float32"), "yy": ("psum", [128, 1024], "float32"),
+    "dec": ("psum", [128, 2048], "float32"), "zz": ("psum", [128, 2048], "float32"),
 }
 SEMAPHORES = ["v", "s", "p", "gp", "dsd", "dx", "dnb", "dw", "arl0", "arl1", "arl2", "arc0", "arc1", "arc2",
               "arn0", "arn1", "arn2", "dc0", "dc1", "df0", "df1", "dout", "dpa", "sent"]
@@ -187,6 +184,9 @@ def rank_program(g, core, T, topo):
     def gather(out, win, off):
         op("v", lambda: g.vector.tensor_copy(ap(out), ap(win).indirect(ap(off))), [win, off], [out])
 
+    def gather_s(out, win, off):
+        op("s", lambda: g.scalar.activation(ap(out), ap(win).indirect(ap(off)), Fn.Copy), [win, off], [out])
+
     def scatter(win, off, a):
         op("v", lambda: g.vector.tensor_copy(ap(win).indirect(ap(off)), ap(a)), [a, off], [win])
 
@@ -209,7 +209,7 @@ def rank_program(g, core, T, topo):
     mate = rank ^ 1
     assert near == [mate]
     fe = topo.engines(core, cores[far[0]])
-    ne = [e for e in topo.engines(core, cores[mate]) if e not in fe]
+    ne = [e for e in topo.engines(core, cores[mate]) if e not in fe][::2]
     block = lambda q: n - 1 - (q ^ rank)
 
     def dest(q):
@@ -247,38 +247,32 @@ def rank_program(g, core, T, topo):
         return [("y", T[dst][:, d0:d0 + w].bitcast(dt.uint8), T[src][:, s0:s0 + w].bitcast(dt.uint8), [r(src, s0, s0 + w)], [r(dst, d0, d0 + w)]),
                 ("y", T[dst + "s"][:, d0:d0 + w], T[src + "s"][:, s0:s0 + w], [r(src + "s", s0, s0 + w)], [r(dst + "s", d0, d0 + w)])]
 
-    sdl = [(T.sdw[16 * a:16 * a + 16, :], r("sdw", 0, 2, 16 * a, 16 * a + 16)) for a in range(8)]
-    dmas("dx", [("s", T.xt[:], T.x[:], [], [r("xt", 0, 1024)])])
-    dmas("dsd", [("y" if i % 2 == 0 else "s", o, T.sd[:], [], [w]) for i, (o, w) in enumerate(sdl)])
+    dmas("dsd", [(q, T.sdw[16 * a:16 * a + 16, :], T.sd[:], [], [r("sdw", 0, 2, 16 * a, 16 * a + 16)]) for a, q in enumerate("ys")])
+    dmas("dx", [("y", T.xt[:], T.x[:], [], [r("xt", 0, 1024)])])
     dmas("dnb", [("y", T.nbw[16 * a:16 * a + 16, :], T.nb[:], [], [r("nbw", 0, 64, 16 * a, 16 * a + 16)]) for a in range(8)])
     dmas("dw", [("y", T.wt[:], T.w[:], [], [r("wt", 0, 1024)])])
 
     pint, pidx = r("pint", 0, 1), r("pidx", 0, 1)
-    iota(r("posc", 0, 256), [[1, 256]], 1, 0)
     iota(pint, [[0, 1]], 0, 1, False)
     iota(pidx, [[0, 1]], 0, 1)
-    iota(r("kk8", 0, 8), [[0, 2], [-1, 4]], 4, 0)
-    iota(r("plc", 0, 8), [[128, 2], [0, 4]], 0, 1)
+    iota(r("posc", 0, 256), [[1, 256]], 1, 0)
     ci = lambda i: r("ci", i, i + 1)
     cf = lambda i: r("cf", i, i + 1)
+    fill(r("half", 0, 128), 0.5)
+    fill(r("et", 0, 512), 0.0)
     fill(r("ste", 0, 512, st=2), 0.0)
     fill(r("ste", 1, 512, st=2), 1.0)
-    for b in range(3):
-        act(r("tab", 512 * b, 512 * b + 512), r("ste", 0, 512), Fn.Copy, scale=0.0)
-    fill(r("tab", 1536, TAB), 0.0)
-    fill(r("half", 0, 128), 0.5)
     fill(r("ht", 0, 512), 0.0)
-    act(r("et", 0, 512), r("ste", 0, 512), Fn.Copy, scale=0.0)
+    for b in range(5):
+        act(r("tab", 512 * b, min(512 * b + 512, TAB)), r("ste", 0, min(512, TAB - 512 * b)), Fn.Copy, scale=0.0)
+    for h in (0, 1):
+        fill(r("zsb", ZW * h, ZW * h + 1), LOW)
 
-    ts(r("my0", 0, 2), r("sdw", 0, 2), float(P * rank), Op.add)
-    send_list(0)
-    cp(r("sdu", 0, 2), r("sdw", 0, 2))
-    quant("qx", "qxs", 0, 256, "xt", 0, 1024)
-    pick("comb0", 224, "qx", 256, "sdu", 0, 2)
-    send_cols(0)
-    iota(r("c16", 0, 256), [[0, 16], [1, 16]], 0, 0)
-    iota(r("ic", 0, 256), [[32, 4], [128, 2], [1, 32]], 0, 0)
+    def unpacker(b):
+        e_, h_ = r("et", 512 * b + b, 512 * b + 512, st=4), r("half", 0, 128)
+        op("g", lambda: g.affine_select(ap(e_), ap(h_), [[-1, 128]], Op.is_equal, 0.0, 0, 1), [h_], [e_])
 
+    unpacker(0)
     ts(ci(7), pint, 4, Op.arith_shift_right)
     ts(ci(0), pint, 31, Op.bitwise_and)
     ts(ci(1), pint, 15, Op.bitwise_and)
@@ -290,40 +284,55 @@ def rank_program(g, core, T, topo):
     cp(cf(10), pidx)
     cp(r("cf", 0, 8), r("ci", 0, 8))
     ts(cf(11), pidx, 128.0, Op.add)
-    ts(cf(17), cf(5), 16.0, Op.mult, cf(7), Op.add)
+    ts(cf(17), cf(5), -16.0, Op.mult, cf(7), Op.add)
+
+    for b in range(4):
+        ts(r("my0", 0, 2, 32 * b, 32 * b + 32), r("sdw", 0, 2, 0, 32), float(P * rank), Op.add)
+    send_list(0)
+    for b in range(4):
+        cp(r("sdu", 0, 2, 32 * b, 32 * b + 32), r("sdw", 0, 2, 0, 32))
     ts(cf(9), cf(0), 16.0, Op.is_ge)
-    ts(r("nbof", 0, 1), cf(6), 2.0, Op.mult, cf(17), Op.add)
-    ts(cf(14), cf(1), 2.0, Op.mult)
-    ts(cf(15), cf(1), 2.0, Op.mult, 32.0, Op.add)
+    ts(cf(18), cf(6), 2.0, Op.mult, 48.0, Op.add)
+    ts(cf(14), cf(1), 2.0, Op.mult, -32.0, Op.add)
+    tt(r("nbof", 0, 1), cf(17), cf(18), Op.add)
+    ts(cf(15), cf(1), 2.0, Op.mult)
+    ts(cf(19), cf(1), -1024.0, Op.mult, 15360.0, Op.add)
+    quant("qx", "qxs", 0, 256, "xt", 0, 1024)
+    pick("comb0", 224, "qx", 256, "sdu", 0, 2)
+    send_cols(0)
+    iota(r("c16", 0, 64), [[0, 4], [1, 16]], 0, 0)
+    iota(r("ic", 0, 256), [[32, 4], [128, 2], [1, 32]], 0, 0)
+
     place = lambda h: r("cf", 10 + h, 11 + h)
     place2 = r("cf", 10, 12)
     tab = r("tab", 0, TAB)
-    for b in range(1, 4):
+    for b in (1, 2, 3):
         act(r("et", 512 * b, 512 * b + 512), r("ste", 0, 512), Fn.Copy, scale=0.0)
     scatter(tab, r("my0", 0, 2), r("posc", 224, 256))
-    cp(r("sdf", 0, 2), r("sdw", 0, 2))
+    cp(r("sdf", 0, 2), r("sdu", 0, 2))
     ts(cf(21), cf(3), -2.0, Op.mult, cf(2), Op.add)
     op("v", lambda: g.vector.tensor_copy(T.nbo[:, 0:16], T.nbw[:, 0:64].indirect(T.nbof[:, 0:1])), [r("nbw", 0, 64), r("nbof", 0, 1)], [r("nbo", 0, 16)])
-    nb2 = r("nb2", 0, 8)
+    nb2, nb3 = r("nb2", 0, 8), r("nb3", 0, 8)
     tt(r("sdf", 2, 3), r("sdf", 1, 2), r("sdf", 0, 1), Op.subtract)
     ts(r("nbn", 0, 8), r("nbo", 0, 8), 0.0, Op.is_lt, NONE + 1.0, Op.mult)
     fill(r("ones32", 0, 32), 1.0)
     ts(r("sdf", 3, 4), r("sdf", 2, 3), cf(9), Op.mult, r("sdf", 0, 1), Op.add)
     tt(nb2, r("nbo", 0, 8), r("nbn", 0, 8), Op.add)
-    fill(r("c256", 0, 32), 256.0)
+    ts(nb3, r("nbo", 0, 8), 1.0, Op.add)
     ts(r("rpa", 0, 32), r("ones32", 0, 32), r("sdf", 3, 4), Op.mult)
     ts(cf(22), cf(4), -2.0, Op.mult, cf(2), Op.add)
-    ts(cf(19), cf(1), -1024.0, Op.mult, 15360.0, Op.add)
     tr(r("tb", 0, 32), r("rpa", 0, 32))
     ts(cf(23), cf(4), -2.0, Op.mult, cf(21), Op.add)
-    ts(cf(20), cf(19), -float(ZW), Op.add)
+    ts(cf(20), cf(19), 512.0, Op.mult, 512.0, Op.add)
     for h in (0, 1):
         ts(r("rpb", 32 * h, 32 * h + 32), r("tb", 0, 32), place(h), Op.is_equal)
     ts(r("cf", 12, 14), r("cf", 10, 12), -0.5, Op.add, -2.0 ** -120, Op.mult)
     for h in (0, 1):
         red(r("tk0", h, h + 1), r("rpb", 32 * h, 32 * h + 32), Op.add)
-    ts(r("hma", 0, 256), r("c16", 0, 256), cf(1), Op.is_equal)
-    act(r("hm", 0, 256), r("hma", 0, 256), Fn.Copy, bias=1024.0, scale=-66560.0)
+    ts(r("cf", 26, 28), place2, cf(20), Op.subtract, 1.0 / UNIT, Op.mult)
+    ts(r("hma", 0, 64), r("c16", 0, 64), cf(1), Op.is_equal)
+    for b in range(2):
+        act(r("hm", 64 * b, 64 * b + 64), r("hma", 0, 64), Fn.Copy, bias=1024.0, scale=-66560.0)
 
     def settle(first):
         if first:
@@ -339,23 +348,22 @@ def rank_program(g, core, T, topo):
         act(r("plm", 64 * d, 64 * d + 64), r("ic", 64 * d, 64 * d + 64), Fn.Identity, bias=cf(b))
     for h in (0, 1):
         act(r("ed", 512 * h + 1, 512 * h + 512, st=2), r("plm", 0, 256), Fn.Identity, bias=r("cf", 12 + h, 13 + h), scale=2.0 ** -120)
-    for i in range(4):
-        z1 = min(512 * i + 512, 2 * ZW)
-        act(r("zsb", 512 * i, z1), r("ste", 0, z1 - 512 * i), Fn.Identity, bias=LOW, scale=0.0)
-    quant("comb0", "comb0s", XB[0], XB[0] + 256, "xt", 0, 1024)
-    ts(r("negm", 0, 128), r("c16", 0, 128), cf(1), Op.not_equal, LOW, Op.mult)
-    ts(r("segm", 0, 128), r("c16", 0, 128), 0.0, Op.is_equal, LOW, Op.mult)
-    ts(r("n8", 0, 8), r("plc", 0, 8), 1024.0, Op.mult, cf(19), Op.subtract)
-    fill(r("qs", 0, 2), -1.0)
-    ts(r("m8", 0, 8), r("n8", 0, 8), -0.5, Op.add, 2.0 ** -18, Op.mult)
+    for b in range(1, 4):
+        unpacker(b)
+    ts(r("negm", 0, 64), r("c16", 0, 64), cf(1), Op.not_equal, LOW, Op.mult)
+    ts(r("segm", 0, 64), r("c16", 0, 64), 0.0, Op.is_equal, LOW, Op.mult)
     for i in (0, 1):
         ts(cf(24 + i), cf(1), float(SPARE - P * rank + S * rank + 16 * i), Op.add)
-    ts(r("kkh", 0, 8), r("kk8", 0, 8), -0.5, Op.add)
-    tt(r("c8", 0, 8), r("kkh", 0, 8), r("m8", 0, 8), Op.add)
+    ts(r("z2", 0, 2), place2, float(P * rank + 1), Op.add)
     quant("pk", "pks", 0, 128, "xt", 0, 512)
+    quant("comb0", "comb0s", 256, 384, "xt", 0, 512)
+    tt(r("w3", 0, 2), r("z2", 0, 2), r("tk0", 0, 2), Op.mult)
     for b in range(4):
-        e_, h_ = r("et", 512 * b + b, 512 * b + 512, st=4), r("half", 0, 128)
-        op("g", lambda: g.affine_select(ap(e_), ap(h_), [[-1, 128]], Op.is_equal, 0.0, 0, 1), [h_], [e_])
+        quant("eq", "eqs", 128 * b, 128 * b + 128, "et", 512 * b, 512 * b + 512)
+    ts(r("pa2", 0, 2), r("w3", 0, 2), -1.0, Op.add)
+    for b in range(4):
+        mm("dec", b, 256, "eq", 128 * b, "qx", 0)
+        act(r("own", 256 * b, 256 * b + 256), r("dec", 512 * b, 512 * b + 256), Fn.Copy)
     iota(r("posc", 256, 768), [[1, 512]], 257, 0)
     iota(r("loc", P * rank, P * rank + P), [[1, P]], 0, 0)
 
@@ -366,110 +374,124 @@ def rank_program(g, core, T, topo):
         scatter(tab, r("land%d" % t, 0, 14), r("posc", P * t, P * t + 224))
         gather(r("lk", 0, 128), r("tab", 0, SPARE), r("nbu", 0, 8))
         run_on(r("pv", 0, 128), r("lk", 0, 128), 128)
-        ts(r("zo", 0, 4), r("pv", 15, 64, st=16), cf(19), Op.subtract)
-        ts(r("pls", 0, 8), r("pv", 15, 128, st=16), 2.0 ** -18, Op.mult)
-        ts(r("zo", 4, 8), r("pv", 79, 128, st=16), cf(20), Op.subtract)
-        tt(r("pl8", 0, 8), r("c8", 0, 8), r("pls", 0, 8), Op.add)
+        ts(r("zo", 0, 8), r("pv", 15, 128, st=16), cf(19), Op.subtract)
+        for h in (0, 1):
+            ts(r("pl8", 4 * h, 4 * h + 4), r("pv", 15 + 64 * h, 64 + 64 * h, st=16), 512.0 / UNIT, Op.mult, r("cf", 26 + h, 27 + h), Op.add)
 
     masks(0)
-    for b in range(4):
-        quant("eq", "eqs", 128 * b, 128 * b + 128, "et", 512 * b, 512 * b + 512)
 
     def spread(buf, w, between=None):
+        def move(e, out, a):
+            if e == "v":
+                cp(out, a)
+            else:
+                act(out, a, Fn.Copy)
         for b in range(4):
-            cp(r(buf, w, 2 * w, 32 * b, 32 * b + 32), r(buf, 0, w, 32 * (b ^ 1), 32 * (b ^ 1) + 32))
+            move("v" if b < 2 else "s", r(buf, w, 2 * w, 32 * b, 32 * b + 32), r(buf, 0, w, 32 * (b ^ 1), 32 * (b ^ 1) + 32))
         if between is not None:
             between()
         for b in (0, 1):
-            cp(r(buf, 2 * w, 4 * w, 64 * b, 64 * b + 64), r(buf, 0, 2 * w, 64 * (1 - b), 64 * (1 - b) + 64))
+            move("v" if b < 1 else "s", r(buf, 2 * w, 4 * w, 64 * b, 64 * b + 64), r(buf, 0, 2 * w, 64 * (1 - b), 64 * (1 - b) + 64))
 
     for t in range(R):
         c = "comb%d" % t
         more = t < R - 1
+        zs = lambda h, a, w: r("zsb", ZW * h + 1 + P * t + a, ZW * h + 1 + P * t + a + w)
         for h in (0, 1):
-            mm("zz", h, P, "qx", 128 * h, c, P * t)
-        act(r("zsb", 1 + P * t, 1 + P * t + P), r("zz", 0, P), Fn.Copy)
-        cp(r("zsb", ZW + 1 + P * t, ZW + 1 + P * t + P), r("zz", 512, 512 + P))
-        op("v", lambda: g.vector.tensor_tensor(T.gs[:, 0:128], T.zsb[:, 0:2 * ZW].indirect(T.zo[:, 0:8]), T.negm[:, 0:128], Op.add),
-           [r("zsb", 0, 2 * ZW), r("zo", 0, 8), r("negm", 0, 128)], [r("gs", 0, 128)])
+            mm("zz", 2 + h, 128, "qx", 128 * h, c, P * t + 192)
+            act(zs(h, 192, 64), r("zz", 1024 + 512 * h, 1088 + 512 * h), Fn.Copy)
+        for h in (0, 1):
+            mm("zz", h, 192, "qx", 128 * h, c, P * t)
+            act(zs(h, 0, 192), r("zz", 512 * h, 512 * h + 192), Fn.Copy)
+
+        def scores(h):
+            w, o, q = r("zsb", ZW * h, ZW * h + 1 + P * t + P), r("zo", 4 * h, 4 * h + 4), r("gs", 64 * h, 64 * h + 64)
+            op("v", lambda: g.vector.tensor_tensor(ap(q), ap(w).indirect(ap(o)), T.negm[:, 0:64], Op.add), [w, o, r("negm", 0, 64)], [q])
+
+        def own_scores(h):
+            scan(r("sbx", 64 * h, 64 * h + 64), r("segm", 0, 64), r("gs", 64 * h, 64 * h + 64), LOW, Op.add, Op.max)
+
+        sb = lambda h: r("sbx", 15 + 64 * h, 64 + 64 * h, st=16)
+        bst = lambda h: r("bst", h, h + 1)
+        k4 = lambda name, h: r(name, 4 * h, 4 * h + 4)
+        best = lambda h: red(bst(h), r("gs", 64 * h, 64 * h + 64), Op.max)
+        wide = lambda h: ts(r("rpa", 32 * h, 32 * h + 32), r("ones32", 0, 32), bst(h), Op.mult)
+        scores(0)
+        best(0)
+        scores(1)
+        wide(0)
+        best(1)
+        own_scores(0)
+        wide(1)
+        own_scores(1)
         if more:
             lst = []
             for t2 in range(t + 1, R):
                 lst += copies(c, P * t, "comb%d" % t2, P * t, P)
-                if t == 0:
-                    lst += copies("qx", 0, "comb%d" % t2, XB[t2], P)
             if t == 0:
                 lst += copies("qx", 0, "finw", 0, P)
             dmas("dc%d" % t, lst)
-        for h in (0, 1):
-            red(r("bst", h, h + 1), r("gs", 64 * h, 64 * h + 64), Op.max)
-        for h in (0, 1):
-            ts(r("rpa", 32 * h, 32 * h + 32), r("ones32", 0, 32), r("bst", h, h + 1), Op.mult)
-        ts(r("ib", 0, 2), r("bst", 0, 2), -5e29, Op.is_lt, 2048.0, Op.mult)
         tr(r("row", 0, 64), r("rpa", 0, 64))
-        scan(r("sbx", 0, 128), r("segm", 0, 128), r("gs", 0, 128), LOW, Op.add, Op.max)
-        spread("row", 64, lambda: ts(r("e8", 0, 4), r("sbx", 15, 64, st=16), r("bst", 0, 1), Op.is_equal))
-        ts(r("ed", 0, 512, st=2), r("row", 0, 256), -1.0, Op.mult, r("bst", 0, 1), Op.add)
-        act(r("ed", 512, 1024, st=2), r("row", 0, 256), Fn.Identity, bias=r("bst", 1, 2), scale=-1.0)
-        ts(r("e8", 4, 8), r("sbx", 79, 128, st=16), r("bst", 1, 2), Op.is_equal)
+        ts(k4("e8", 0), sb(0), bst(0), Op.is_equal)
+        spread("row", 64, lambda: ts(k4("e8", 1), sb(1), bst(1), Op.is_equal))
+        for i in (0, 1):
+            a = r("row", 128 * i, 128 * i + 128)
+            ts(r("ed", 256 * i, 256 * i + 256, st=2), a, -1.0, Op.mult, bst(0), Op.add)
+            act(r("ed", 512 + 256 * i, 768 + 256 * i, st=2), a, Fn.Identity, bias=bst(1), scale=-1.0)
+        for h in (0, 1):
+            act(k4("ne8", h), sb(h), Fn.Sign, bias=bst(h), scale=-1.0)
 
-        def ahead(h):
-            x = 512 * h
-            scan(r("cm", x, x + 512), r("ste", 0, 512), r("ed", x, x + 512), 0.0, Op.mult, Op.add)
-            act(r("sg", 256 * h, 256 * h + 256), r("cm", x + 1, x + 512, st=2), Fn.Sign, accum=r("rs", h, h + 1))
+        def ahead(x, w):
+            scan(r("cm", x, x + w), r("ste", 0, w), r("ed", x, x + w), 0.0, Op.mult, Op.add)
 
-        ahead(0)
+        def count(h):
+            act(r("sg", 256 * h, 256 * h + 256), r("cm", 512 * h + 1, 512 * h + 512, st=2), Fn.Sign, accum=r("rs", h, h + 1))
+
+        ahead(0, 256)
+        ahead(256, 256)
+        count(0)
+        ahead(512, 512)
+        count(1)
         tt(r("t8", 0, 8), r("e8", 0, 8), r("pl8", 0, 8), Op.mult)
-        ahead(1)
-        for h in (0, 1):
-            red(r("q2", h, h + 1), r("t8", 4 * h, 4 * h + 4), Op.max)
-        ts(r("ibh", 0, 2), r("ib", 0, 2), 0.5 - 2.0 ** -19, Op.add)
-        ts(r("qk", 0, 2), r("q2", 0, 2), MAGIC, Op.add, -MAGIC, Op.add)
-        tt(r("x2", 0, 2), r("q2", 0, 2), r("qs", 0, 2), Op.subtract)
-        tt(r("qf", 0, 2), r("q2", 0, 2), r("qk", 0, 2), Op.subtract)
-        tt(r("pay", 0, 2), r("qf", 0, 2), r("ibh", 0, 2), Op.add)
-        for h in (0, 1):
-            ts(r("rpb", 32 * h, 32 * h + 32), r("c256", 0, 32), r("rs", h, h + 1), Op.subtract, r("pay", h, h + 1), Op.add)
-        ts(r("rk", 0, 2), r("rs", 0, 2), -0.5, Op.mult, 128.0, Op.add)
+        tt(r("u8", 0, 8), r("e8", 0, 8), nb3, Op.mult)
+        scan(r("sf", 0, 8), r("ne8", 0, 8), r("t8", 0, 8), 0.0, Op.mult, Op.add)
+        ts(r("cib", 0, 64), r("rpa", 0, 64), -1e-27, Op.mult, 224.0, Op.max)
+        number = lambda h: ts(r("rpb", 32 * h, 32 * h + 32), r("cib", 32 * h, 32 * h + 32), r("rs", h, h + 1), Op.subtract, r("sf", 4 * h + 3, 4 * h + 4), Op.add)
+        number(0)
+        scan(r("sn", 0, 8), r("ne8", 0, 8), r("u8", 0, 8), 0.0, Op.mult, Op.add)
+        number(1)
         tr(r("tb", 0, 64), r("rpb", 0, 64))
-        tt(r("w2", 0, 2), r("rk", 0, 2), r("ib", 0, 2), Op.add)
+        ts(r("tk", 0, 2), r("rpb", 0, 64, st=32), 32.0, Op.is_lt)
         for i in range(2):
-            ts(r("dx", 64 * i, 64 * i + 64), r("tb", 0, 64), cf(14 + i), Op.subtract, float(2 ** 18), Op.mult)
+            ts(r("dx", 64 * i, 64 * i + 64), r("tb", 0, 64), cf(14 + i), Op.subtract, UNIT, Op.mult)
         for i in range(2):
             red(r("pt", i, i + 1), r("dx", 64 * i, 64 * i + 64), Op.min, absolute=True)
-        ts(r("tk", 0, 2), r("w2", 0, 2), 31.5, Op.is_lt)
-        spread("pt", 2, lambda: tt(r("y2", 0, 2), r("x2", 0, 2), r("tk", 0, 2), Op.mult))
+        tt(r("y2", 0, 2), r("sn", 3, 8, st=4), r("tk", 0, 2), Op.mult)
+        spread("pt", 2, lambda: tt(r("pa2", 0, 2), r("pa2", 0, 2), r("y2", 0, 2), Op.add))
         for i in range(2):
             red(r("vi", i, i + 1), r("pt", i, 8, st=2), Op.min)
-        ts(r("vi", 4, 6), r("vi", 0, 2), 10, Op.arith_shift_right)
-        ts(r("vi", 8, 10), r("vi", 0, 2), 1023, Op.bitwise_and)
-        ts(r("vz", 0, 2), r("vi", 0, 2), float(2 ** 18), Op.is_ge, 8192.0, Op.mult)
-        ts(r("offu", 0, 2), r("vi", 4, 6), P - 1.0, Op.min, float(XB[t]), Op.add)
-        ts(r("offu", 2, 4), r("vi", 8, 10), float(P * t + P - 1), Op.min)
-        tt(r("vz", 2, 4), r("vi", 4, 6), r("vz", 0, 2), Op.add)
-        pick("pk", 0, c, WC[t], "offu", 0, 4)
+        ts(r("offp", 0, 2), r("vi", 0, 2), 2.0 ** -9, Op.mult, float(P * t + P - 1), Op.min)
+        ts(r("vi", 4, 6), r("vi", 0, 2), 511 - 2 ** 19, Op.bitwise_and)
+        pick("pk", 0, c, P * t + P, "offp", 0, 2)
+        ts(r("offo", 0, 2), r("vi", 4, 6), P - 1.0, Op.min)
+        for b in range(4):
+            gather_s(r("od", 32 * b, 32 * b + 32), r("own", 256 * b, 256 * b + 256), r("offo", 0, 2))
         my = "my%d" % (t + 1)
         for i in range(2):
-            ts(r(my, i, i + 1), r("vz", 2 + i, 3 + i), cf(24 + i), Op.min, float(P * rank), Op.add)
+            ts(r(my, i, i + 1), r("vi", 4 + i, 5 + i), cf(24 + i), Op.min, float(P * rank), Op.add)
         if more:
             send_list(t + 1)
+        else:
+            dmas("dpa", [("y", T.pa[0:1, 128 * h:128 * h + 128], T.pa2[:, h:h + 1], [r("pa2", h, h + 1)], []) for h in (0, 1)])
         for b in range(4):
             mm("dec", b, 128, "eq", 128 * b, "pk", 0)
-            act(r("od", 32 * b, 32 * b + 32), r("dec", 512 * b, 512 * b + 32), Fn.Copy)
-        tt(r("qs", 0, 2), r("qs", 0, 2), r("y2", 0, 2), Op.add)
         lv = P - 1 + S * t
         scatter(r("loc", 0, TAB), r(my, 0, 2), r("posc", lv, lv + S))
-        fills = []
-        if not more:
-            run_on(r("flx", 0, 256), r("loc", P * rank, P * rank + P), 256)
-            ts(r("w3", 0, 2), r("qs", 0, 2), MAGIC, Op.add, -MAGIC, Op.add)
-            fills = [lambda: ts(r("fo", 0, 16), r("flx", 15, 256, st=16), cf(19), Op.subtract)]
-            fills += [lambda h=h: ts(r("e8", 4 * h, 4 * h + 4), r("kk8", 4 * h, 4 * h + 4), r("w3", h, h + 1), Op.is_equal) for h in (0, 1)]
-            fills += [lambda: ts(r("tk", 0, 2), r("qs", 0, 2), -0.75, Op.is_ge)]
+        half_row = lambda m: run_on(r("flx", 128 * m, 128 * m + 128), r("loc", P * rank + 128 * m, P * rank + 128 * m + 128), 128)
         for b in range(4):
-            tt(r("ht", b, 128, st=4), r("dec", 512 * b + 32, 512 * b + 64), r("od", 32 * b, 32 * b + 32), Op.add)
-            if fills:
-                fills[b]()
+            tt(r("ht", b, 128, st=4), r("dec", 512 * b, 512 * b + 32), r("od", 32 * b, 32 * b + 32), Op.add)
+            if not more and b == 1:
+                half_row(0)
         if more:
             d, o = "comb%d" % (t + 1), P * (t + 1) + 224
             quant(d, d + "s", o, o + 128, "ht", 0, 512)
@@ -479,33 +501,23 @@ def rank_program(g, core, T, topo):
             settle(False)
             if t == 0:
                 quant("qw", "qws", 0, 256, "wt", 0, 1024)
-            else:
-                ts(r("z2", 0, 2), place2, float(P * rank + 1), Op.add)
-                tt(r("w3", 0, 2), r("z2", 0, 2), r("tk0", 0, 2), Op.mult)
-                ts(r("pa2", 0, 2), r("w3", 0, 2), -1.0, Op.add)
             masks(t + 1)
         else:
             quant("finw", "finws", 320, 448, "ht", 0, 512)
-            tt(r("u8", 0, 8), r("e8", 0, 8), nb2, Op.mult)
+            half_row(1)
 
-    bank = ("yy", "zz")
+    for m in (0, 1):
+        ts(r("fo", 8 * m, 8 * m + 8), r("flx", 128 * m + 15, 128 * m + 128, st=16), cf(19), Op.subtract)
     for m in (0, 1):
         pick("fin", 128 * m, "finw", 352, "fo", 8 * m, 8 * m + 8)
         for o in (0, 1):
-            mm(bank[m], o, 128, "qw", 128 * o, "fin", 128 * m)
-    for h in (0, 1):
-        red(r("w2", h, h + 1), r("u8", 4 * h, 4 * h + 4), Op.add)
-    cp(r("sy", 0, 128), r("yy", 0, 128))
-    act(r("sy", 256, 384), r("yy", 512, 640), Fn.Copy)
-    cp(r("sy", 128, 256), r("zz", 0, 128))
-    act(r("sy", 384, 512), r("zz", 512, 640), Fn.Copy)
+            mm("zz", 2 * m + o, 128, "qw", 128 * o, "fin", 128 * m)
+    for m in (0, 1):
+        cp(r("sy", 128 * m, 128 * m + 128), r("zz", 1024 * m, 1024 * m + 128))
+        act(r("sy", 256 + 128 * m, 384 + 128 * m), r("zz", 1024 * m + 512, 1024 * m + 640), Fn.Copy)
     dmas("dout", [("y", T.oc[:], T.fin[:].bitcast(dt.uint8), [r("fin", 0, 256)], [])] +
          [("y", T.osc[4 * k:4 * k + 4, :], T.fins[32 * k:32 * k + 4, :], [r("fins", 0, 256)], []) for k in range(4)] +
-         [("y", T.y[:, 0:256], T.sy[:, 0:256], [r("sy", 0, 256)], []), ("s", T.y[:, 256:512], T.sy[:, 256:512], [r("sy", 256, 512)], [])])
-    tt(r("x2", 0, 2), r("w2", 0, 2), r("pa2", 0, 2), Op.subtract)
-    tt(r("y2", 0, 2), r("x2", 0, 2), r("tk", 0, 2), Op.mult)
-    tt(r("pa2", 0, 2), r("pa2", 0, 2), r("y2", 0, 2), Op.add)
-    dmas("dpa", [("y", T.pa[0:1, 128 * h:128 * h + 128], T.pa2[:, h:h + 1], [r("pa2", h, h + 1)], []) for h in (0, 1)])
+         [("s", T.y[:], T.sy[:], [r("sy", 0, 512)], [])])
     for sem in cnt:
         if known["g"].get(sem, 0) < cnt[sem]:
             g.wait_ge(T.sem[sem], cnt[sem])

@@ -5,15 +5,15 @@ from concourse.mybir import dt, AluOpType as Op, AxisListType, ActivationFunctio
 F8 = "float8_e4m3fn_x4"
 WC = (384, 608, 864)
 WF = 448
-TAB, NONE, SPARE = 2312, 2048, 2056
+STR, OFF = 304, 48
+TAB, NONE = 2440, 2432
 ZW = 776
 LOW = -9e29
-UNIT = 2.0 ** 19
 SCRATCH = {
     "xt": ("sbuf", [128, 1024], "bfloat16"), "wt": ("sbuf", [128, 1024], "bfloat16"),
     "qx": ("sbuf", [128, 256], F8), "qxs": ("sbuf", [128, 256], "uint8"),
     "qw": ("sbuf", [128, 256], F8), "qws": ("sbuf", [128, 256], "uint8"), "half": ("sbuf", [128, 128], "bfloat16"),
-    "et": ("sbuf", [128, 2048], "bfloat16"), "eq": ("sbuf", [128, 512], F8), "eqs": ("sbuf", [128, 512], "uint8"),
+    "et": ("sbuf", [128, 528], "bfloat16"), "eq": ("sbuf", [128, 512], F8), "eqs": ("sbuf", [128, 512], "uint8"),
     "comb0": ("sbuf", [128, WC[0]], F8), "comb0s": ("sbuf", [128, WC[0]], "uint8"),
     "comb1": ("sbuf", [128, WC[1]], F8), "comb1s": ("sbuf", [128, WC[1]], "uint8"),
     "comb2": ("sbuf", [128, WC[2]], F8), "comb2s": ("sbuf", [128, WC[2]], "uint8"),
@@ -21,39 +21,42 @@ SCRATCH = {
     "fin": ("sbuf", [128, 256], F8), "fins": ("sbuf", [128, 256], "uint8"),
     "pk": ("sbuf", [128, 128], F8), "pks": ("sbuf", [128, 128], "uint8"),
     "ht": ("sbuf", [128, 512], "bfloat16"), "od": ("sbuf", [128, 128], "float32"), "own": ("sbuf", [128, 1024], "bfloat16"),
-    "sdw": ("sbuf", [128, 2], "int32"), "nbw": ("sbuf", [128, 64], "int32"),
-    "sdu": ("sbuf", [128, 2], "uint16"), "sdf": ("sbuf", [128, 4], "float32"),
-    "nbof": ("sbuf", [128, 2], "uint16"), "nbo": ("sbuf", [128, 16], "float32"), "nbn": ("sbuf", [128, 8], "float32"),
-    "nb2": ("sbuf", [128, 8], "float32"), "nb3": ("sbuf", [128, 8], "float32"), "nbu": ("sbuf", [128, 8], "uint16"),
+    "sdw": ("sbuf", [128, 2], "int32"), "nbw": ("sbuf", [128, 64], "int32"), "sdu": ("sbuf", [128, 2], "uint16"),
+    "nbof": ("sbuf", [128, 2], "uint16"), "nboi": ("sbuf", [128, 16], "int32"), "nbsh": ("sbuf", [128, 8], "int32"),
+    "nbo": ("sbuf", [128, 8], "float32"), "nba": ("sbuf", [128, 8], "float32"), "nbn": ("sbuf", [128, 8], "float32"),
+    "nbm": ("sbuf", [128, 8], "float32"), "nb3": ("sbuf", [128, 8], "float32"), "nbu": ("sbuf", [128, 8], "uint16"),
+    "oix": ("sbuf", [128, 2], "uint16"), "olk": ("sbuf", [128, 32], "float32"), "ofl": ("sbuf", [128, 32], "float32"),
     "pint": ("sbuf", [128, 1], "int32"), "pidx": ("sbuf", [128, 1], "float32"),
     "c16": ("sbuf", [128, 64], "float32"),
     "ic": ("sbuf", [128, 256], "float32"), "ci": ("sbuf", [128, 16], "int32"), "cf": ("sbuf", [128, 32], "float32"),
     "plm": ("sbuf", [128, 256], "float32"), "ste": ("sbuf", [128, 512], "bfloat16"),
-    "ones32": ("sbuf", [128, 32], "float32"),
+    "ones": ("sbuf", [128, 2], "float32"),
     "posc": ("sbuf", [128, 768], "float32"), "tab": ("sbuf", [128, TAB], "float32"), "loc": ("sbuf", [128, TAB], "float32"),
     "hma": ("sbuf", [128, 64], "float32"), "hm": ("sbuf", [128, 128], "float32"),
     "negm": ("sbuf", [128, 64], "float32"), "segm": ("sbuf", [128, 64], "float32"),
     "my0": ("sbuf", [128, 2], "uint16"), "my1": ("sbuf", [128, 2], "uint16"), "my2": ("sbuf", [128, 2], "uint16"), "my3": ("sbuf", [128, 2], "uint16"),
     "land0": ("sbuf", [128, 16], "uint16"), "land1": ("sbuf", [128, 16], "uint16"), "land2": ("sbuf", [128, 16], "uint16"),
     "lk": ("sbuf", [128, 128], "float32"), "pv": ("sbuf", [128, 128], "float32"), "zo": ("sbuf", [128, 8], "uint16"),
-    "zsb": ("sbuf", [128, 2 * ZW], "float32"), "gs": ("sbuf", [128, 128], "float32"), "sbx": ("sbuf", [128, 128], "float32"),
-    "pl8": ("sbuf", [128, 8], "float32"), "e8": ("sbuf", [128, 8], "float32"), "ne8": ("sbuf", [128, 8], "float32"),
+    "zf": ("sbuf", [128, 8], "float32"),
+    "zsb": ("sbuf", [128, 2 * ZW], "float32"), "gs": ("sbuf", [128, 192], "float32"), "sc": ("sbuf", [128, 192], "float32"),
+    "sbx": ("sbuf", [128, 128], "float32"), "row": ("sbuf", [128, 256], "float32"),
+    "e8": ("sbuf", [128, 8], "float32"), "ne8": ("sbuf", [128, 8], "float32"),
     "t8": ("sbuf", [128, 8], "float32"), "u8": ("sbuf", [128, 8], "float32"),
-    "sf": ("sbuf", [128, 8], "float32"), "sn": ("sbuf", [128, 8], "float32"),
-    "bst": ("sbuf", [128, 2], "float32"), "cib": ("sbuf", [128, 64], "float32"),
-    "rpa": ("sbuf", [128, 64], "float32"), "row": ("sbuf", [128, 256], "float32"),
+    "sf": ("sbuf", [128, 8], "float32"), "sn": ("sbuf", [128, 8], "float32"), "val": ("sbuf", [128, 2], "float32"),
     "ed": ("sbuf", [128, 1024], "bfloat16"), "cm": ("sbuf", [128, 1024], "bfloat16"), "sg": ("sbuf", [128, 512], "bfloat16"),
     "rs": ("sbuf", [128, 2], "float32"), "y2": ("sbuf", [128, 2], "float32"), "z2": ("sbuf", [128, 2], "float32"),
-    "rpb": ("sbuf", [128, 64], "float32"), "tb": ("sbuf", [128, 64], "float32"),
-    "pt": ("sbuf", [128, 8], "float32"), "dx": ("sbuf", [128, 128], "float32"),
-    "vi": ("sbuf", [128, 8], "int32"), "offp": ("sbuf", [128, 2], "uint16"), "offo": ("sbuf", [128, 2], "uint16"),
+    "hi": ("sbuf", [128, 2], "int32"), "hf": ("sbuf", [128, 2], "float32"), "pat": ("sbuf", [128, 256], "bfloat16"),
+    "oh": ("sbuf", [128, 512], "bfloat16"), "ohq": ("sbuf", [128, 128], F8), "ohqs": ("sbuf", [128, 128], "uint8"),
+    "dg": ("sbuf", [128, 512], "bfloat16"), "dgq": ("sbuf", [128, 128], F8), "dgqs": ("sbuf", [128, 128], "uint8"),
+    "pl": ("sbuf", [128, 2], "float32"),
+    "offp": ("sbuf", [128, 2], "uint16"), "offo": ("sbuf", [128, 2], "uint16"),
     "tk0": ("sbuf", [128, 2], "float32"), "tk": ("sbuf", [128, 2], "float32"), "nf": ("sbuf", [128, 2], "float32"),
-    "nfm": ("sbuf", [128, 2], "float32"), "pa2": ("sbuf", [128, 2], "float32"), "w3": ("sbuf", [128, 2], "float32"),
+    "pa2": ("sbuf", [128, 2], "float32"), "w3": ("sbuf", [128, 2], "float32"),
     "flx": ("sbuf", [128, 256], "float32"), "fo": ("sbuf", [128, 16], "uint16"), "sy": ("sbuf", [128, 512], "float32"),
     "dec": ("psum", [128, 2048], "float32"), "zz": ("psum", [128, 2048], "float32"),
 }
 SEMAPHORES = ["v", "s", "p", "gp", "dsd", "dx", "dnb", "dw", "arl0", "arl1", "arl2", "arc0", "arc1", "arc2",
-              "arn0", "arn1", "arn2", "dc0", "dc1", "df0", "df1", "dout", "dpa", "sent"]
+              "arn0", "arn1", "arn2", "dc0", "dc1", "df0", "df1", "di", "dout", "dpa", "sent"]
 
 
 def r(name, c0, c1, p0=0, p1=128, st=1):
@@ -148,12 +151,6 @@ def rank_program(g, core, T, topo):
 
     def tt(out, a, b, o):
         op("v", lambda: g.vector.tensor_tensor(ap(out), ap(a), ap(b), o), [a, b], [out])
-
-    def red(out, a, o, absolute=False):
-        if absolute:
-            op("v", lambda: g.vector.tensor_reduce(ap(out), ap(a), AxisListType.X, o, apply_absolute_value=True), [a], [out])
-        else:
-            op("v", lambda: g.vector.tensor_reduce(ap(out), ap(a), AxisListType.X, o), [a], [out])
 
     def cp(out, a):
         op("v", lambda: g.vector.tensor_copy(ap(out), ap(a)), [a], [out])
@@ -252,27 +249,22 @@ def rank_program(g, core, T, topo):
     dmas("dnb", [("y", T.nbw[16 * a:16 * a + 16, :], T.nb[:], [], [r("nbw", 0, 64, 16 * a, 16 * a + 16)]) for a in range(8)])
     dmas("dw", [("y", T.wt[:], T.w[:], [], [r("wt", 0, 1024)])])
 
+    base = STR * rank + OFF
     pint, pidx = r("pint", 0, 1), r("pidx", 0, 1)
     iota(pint, [[0, 1]], 0, 1, False)
     iota(pidx, [[0, 1]], 0, 1)
     iota(r("posc", 0, 256), [[1, 256]], 1, 0)
     ci = lambda i: r("ci", i, i + 1)
     cf = lambda i: r("cf", i, i + 1)
-    fill(r("half", 0, 128), 0.5)
-    fill(r("et", 0, 512), 0.0)
     fill(r("ste", 0, 512, st=2), 0.0)
     fill(r("ste", 1, 512, st=2), 1.0)
-    fill(r("ht", 0, 512), 0.0)
     for b in range(5):
         act(r("tab", 512 * b, min(512 * b + 512, TAB)), r("ste", 0, min(512, TAB - 512 * b)), Fn.Copy, scale=0.0)
-    for h in (0, 1):
-        fill(r("zsb", ZW * h, ZW * h + 1), LOW)
-
-    def unpacker(b):
-        e_, h_ = r("et", 512 * b + b, 512 * b + 512, st=4), r("half", 0, 128)
-        op("g", lambda: g.affine_select(ap(e_), ap(h_), [[-1, 128]], Op.is_equal, 0.0, 0, 1), [h_], [e_])
-
-    unpacker(0)
+    fill(r("half", 0, 128), 0.5)
+    fill(r("et", 0, 528), 0.0)
+    e_, h_ = r("et", 3, 515, st=4), r("half", 0, 128)
+    op("g", lambda: g.affine_select(ap(e_), ap(h_), [[-1, 128]], Op.is_equal, 0.0, 0, 1), [h_], [e_])
+    iota(r("c16", 0, 64), [[0, 4], [1, 16]], 0, 0)
     ts(ci(7), pint, 4, Op.arith_shift_right)
     ts(ci(0), pint, 31, Op.bitwise_and)
     ts(ci(1), pint, 15, Op.bitwise_and)
@@ -287,111 +279,97 @@ def rank_program(g, core, T, topo):
     ts(cf(17), cf(5), -16.0, Op.mult, cf(7), Op.add)
 
     for b in range(4):
-        ts(r("my0", 0, 2, 32 * b, 32 * b + 32), r("sdw", 0, 2, 0, 32), float(P * rank), Op.add)
+        ts(r("my0", 0, 2, 32 * b, 32 * b + 32), r("sdw", 0, 2, 0, 32), float(base), Op.add)
     send_list(0)
     for b in range(4):
         cp(r("sdu", 0, 2, 32 * b, 32 * b + 32), r("sdw", 0, 2, 0, 32))
-    ts(cf(9), cf(0), 16.0, Op.is_ge)
-    ts(cf(18), cf(6), 2.0, Op.mult, 48.0, Op.add)
-    ts(cf(14), cf(1), 2.0, Op.mult, -32.0, Op.add)
-    tt(r("nbof", 0, 1), cf(17), cf(18), Op.add)
-    ts(cf(15), cf(1), 2.0, Op.mult)
-    ts(cf(19), cf(1), -1024.0, Op.mult, 15360.0, Op.add)
+    place2 = r("cf", 10, 12)
     quant("qx", "qxs", 0, 256, "xt", 0, 1024)
     pick("comb0", 224, "qx", 256, "sdu", 0, 2)
     send_cols(0)
-    iota(r("c16", 0, 64), [[0, 4], [1, 16]], 0, 0)
-    iota(r("ic", 0, 256), [[32, 4], [128, 2], [1, 32]], 0, 0)
+    dmas("di", copies("qx", 0, "comb0", 256, 128) + copies("qx", 32, "pk", 32, 96))
 
-    place = lambda h: r("cf", 10 + h, 11 + h)
-    place2 = r("cf", 10, 12)
+    iota(r("ic", 0, 256), [[32, 4], [128, 2], [1, 32]], 0, 0)
+    iota(r("dg", 0, 512), [[0, 512]], 0, 0)
+    iota(r("pat", 0, 256), [[0, 8], [-2, 16], [-32, 2]], 256, 0)
+    iota(r("posc", 256, 768), [[1, 512]], 257, 0)
+    iota(r("loc", base, base + P), [[1, P]], 0, 0)
+    iota(r("ht", 0, 512), [[0, 512]], 0, 0)
+
     tab = r("tab", 0, TAB)
-    for b in (1, 2, 3):
-        act(r("et", 512 * b, 512 * b + 512), r("ste", 0, 512), Fn.Copy, scale=0.0)
-    scatter(tab, r("my0", 0, 2), r("posc", 224, 256))
-    cp(r("sdf", 0, 2), r("sdu", 0, 2))
-    ts(cf(21), cf(3), -2.0, Op.mult, cf(2), Op.add)
-    op("v", lambda: g.vector.tensor_copy(T.nbo[:, 0:16], T.nbw[:, 0:64].indirect(T.nbof[:, 0:1])), [r("nbw", 0, 64), r("nbof", 0, 1)], [r("nbo", 0, 16)])
-    nb2, nb3 = r("nb2", 0, 8), r("nb3", 0, 8)
-    tt(r("sdf", 2, 3), r("sdf", 1, 2), r("sdf", 0, 1), Op.subtract)
-    ts(r("nbn", 0, 8), r("nbo", 0, 8), 0.0, Op.is_lt, NONE + 1.0, Op.mult)
-    fill(r("ones32", 0, 32), 1.0)
-    ts(r("sdf", 3, 4), r("sdf", 2, 3), cf(9), Op.mult, r("sdf", 0, 1), Op.add)
-    tt(nb2, r("nbo", 0, 8), r("nbn", 0, 8), Op.add)
-    ts(nb3, r("nbo", 0, 8), 1.0, Op.add)
-    ts(r("rpa", 0, 32), r("ones32", 0, 32), r("sdf", 3, 4), Op.mult)
-    ts(cf(22), cf(4), -2.0, Op.mult, cf(2), Op.add)
-    tr(r("tb", 0, 32), r("rpa", 0, 32))
-    ts(cf(23), cf(4), -2.0, Op.mult, cf(21), Op.add)
-    ts(cf(20), cf(19), 512.0, Op.mult, 512.0, Op.add)
-    for h in (0, 1):
-        ts(r("rpb", 32 * h, 32 * h + 32), r("tb", 0, 32), place(h), Op.is_equal)
-    ts(r("cf", 12, 14), r("cf", 10, 12), -0.5, Op.add, -2.0 ** -120, Op.mult)
-    for h in (0, 1):
-        red(r("tk0", h, h + 1), r("rpb", 32 * h, 32 * h + 32), Op.add)
-    ts(r("cf", 26, 28), place2, cf(20), Op.subtract, 1.0 / UNIT, Op.mult)
+    for b in range(4):
+        quant("eq", "eqs", 128 * b, 128 * b + 128, "et", 3 - b, 515 - b)
+    ts(cf(18), cf(6), 2.0, Op.mult, 48.0, Op.add)
+    ts(cf(19), cf(1), -1024.0, Op.mult, 15360.0, Op.add)
+    ts(cf(25), cf(1), 16.0, Op.add)
+    tt(r("nbof", 0, 1), cf(17), cf(18), Op.add)
+    ts(r("oix", 0, 2), place2, float(base), Op.add)
     ts(r("hma", 0, 64), r("c16", 0, 64), cf(1), Op.is_equal)
     for b in range(2):
         act(r("hm", 64 * b, 64 * b + 64), r("hma", 0, 64), Fn.Copy, bias=1024.0, scale=-66560.0)
+    for b in range(4):
+        mm("dec", b, 256, "eq", 128 * b, "qx", 0)
+        act(r("own", 256 * b, 256 * b + 256), r("dec", 512 * b, 512 * b + 256), Fn.Copy)
+    op("v", lambda: g.vector.tensor_copy(T.nboi[:, 0:16], T.nbw[:, 0:64].indirect(T.nbof[:, 0:1])), [r("nbw", 0, 64), r("nbof", 0, 1)], [r("nboi", 0, 16)])
+    scatter(tab, r("my0", 0, 2), r("posc", 224, 256))
+    nbi, nbo, nb3 = r("nboi", 0, 8), r("nbo", 0, 8), r("nb3", 0, 8)
+    ts(r("nbsh", 0, 8), nbi, 8, Op.arith_shift_right)
+    cp(nbo, nbi)
+    gather(r("olk", 0, 32), tab, r("oix", 0, 2))
+    ts(r("nba", 0, 8), r("nbsh", 0, 8), float(STR - P), Op.mult, float(OFF - NONE), Op.add)
+    ts(r("nbn", 0, 8), nbo, 0.0, Op.is_lt, float(NONE + 1 + STR - P - OFF), Op.mult)
+
+    def run_on(out, a, width):
+        scan(out, r("hm", 0, width), a, 0.0, Op.add, Op.max)
+
+    run_on(r("ofl", 0, 32), r("olk", 0, 32), 32)
+    tt(r("nba", 0, 8), r("nba", 0, 8), nbo, Op.add)
+    ts(cf(21), cf(3), -2.0, Op.mult, cf(2), Op.add)
+    ts(r("tk0", 0, 2), r("ofl", 15, 32, st=16), cf(19), Op.subtract, 0.0, Op.is_gt)
+    tt(r("nbm", 0, 8), r("nba", 0, 8), r("nbn", 0, 8), Op.add)
+    ts(cf(22), cf(4), -2.0, Op.mult, cf(2), Op.add)
+    ts(cf(23), cf(4), -2.0, Op.mult, cf(21), Op.add)
 
     def settle(first):
         if first:
             ts(r("nf", 0, 2), r("tk0", 0, 2), -1.0, Op.mult, 1.0, Op.add)
+            ts(r("cf", 12, 14), place2, -0.5, Op.add, -2.0 ** -120, Op.mult)
         else:
             tt(r("nf", 0, 2), r("nf", 0, 2), r("tk", 0, 2), Op.subtract)
-        ts(r("nfm", 0, 2), r("nf", 0, 2), -float(NONE), Op.mult, float(NONE), Op.add)
         for h in (0, 1):
-            ts(r("nbu", 4 * h, 4 * h + 4), r("nb2", 4 * h, 4 * h + 4), r("nf", h, h + 1), Op.mult, r("nfm", h, h + 1), Op.add)
+            ts(r("nbu", 4 * h, 4 * h + 4), r("nbm", 4 * h, 4 * h + 4), r("nf", h, h + 1), Op.mult, float(NONE), Op.add)
+
+    def masks(t):
+        scatter(tab, r("land%d" % t, 0, 14), r("posc", P * t, P * t + 224))
+        gather(r("lk", 0, 128), tab, r("nbu", 0, 8))
+        run_on(r("pv", 0, 128), r("lk", 0, 128), 128)
+        ts(r("zo", 0, 8), r("pv", 15, 128, st=16), cf(19), Op.subtract)
+        ts(r("zf", 0, 8), r("pv", 15, 128, st=16), cf(19), Op.subtract, -1.0, Op.add)
 
     settle(True)
     for d, b in enumerate((2, 21, 22, 23)):
         act(r("plm", 64 * d, 64 * d + 64), r("ic", 64 * d, 64 * d + 64), Fn.Identity, bias=cf(b))
     for h in (0, 1):
         act(r("ed", 512 * h + 1, 512 * h + 512, st=2), r("plm", 0, 256), Fn.Identity, bias=r("cf", 12 + h, 13 + h), scale=2.0 ** -120)
-    for b in range(1, 4):
-        unpacker(b)
+    masks(0)
+    fill(r("ones", 0, 2), 1.0)
+    for h in (0, 1):
+        fill(r("zsb", ZW * h, ZW * h + 1), LOW)
+        fill(r("gs", 96 * h + 64, 96 * h + 96), LOW)
     ts(r("negm", 0, 64), r("c16", 0, 64), cf(1), Op.not_equal, LOW, Op.mult)
     ts(r("segm", 0, 64), r("c16", 0, 64), 0.0, Op.is_equal, LOW, Op.mult)
-    for i in (0, 1):
-        ts(cf(24 + i), cf(1), float(SPARE - P * rank + S * rank + 16 * i), Op.add)
-    ts(r("z2", 0, 2), place2, float(P * rank + 1), Op.add)
-    quant("pk", "pks", 0, 128, "xt", 0, 512)
-    quant("comb0", "comb0s", 256, 384, "xt", 0, 512)
-    tt(r("w3", 0, 2), r("z2", 0, 2), r("tk0", 0, 2), Op.mult)
-    for b in range(4):
-        quant("eq", "eqs", 128 * b, 128 * b + 128, "et", 512 * b, 512 * b + 512)
-    ts(r("pa2", 0, 2), r("w3", 0, 2), -1.0, Op.add)
-    for b in range(4):
-        mm("dec", b, 256, "eq", 128 * b, "qx", 0)
-        act(r("own", 256 * b, 256 * b + 256), r("dec", 512 * b, 512 * b + 256), Fn.Copy)
-    iota(r("posc", 256, 768), [[1, 512]], 257, 0)
-    iota(r("loc", P * rank, P * rank + P), [[1, P]], 0, 0)
 
-    def run_on(out, a, width):
-        scan(out, r("hm", 0, width), a, 0.0, Op.add, Op.max)
+    def digits(h):
+        ts(r("dg", 16 + h, 23 + h, st=6), r("ones", 0, 2), cf(2), Op.mult, float(OFF + 16 + 128 * h), Op.add)
+        ts(r("dg", 48 + 6 * h, 50 + 6 * h), r("ones", 0, 2), cf(0), Op.mult, -16.0, Op.add)
 
-    def masks(t):
-        scatter(tab, r("land%d" % t, 0, 14), r("posc", P * t, P * t + 224))
-        gather(r("lk", 0, 128), r("tab", 0, SPARE), r("nbu", 0, 8))
-        run_on(r("pv", 0, 128), r("lk", 0, 128), 128)
-        ts(r("zo", 0, 8), r("pv", 15, 128, st=16), cf(19), Op.subtract)
-        for h in (0, 1):
-            ts(r("pl8", 4 * h, 4 * h + 4), r("pv", 15 + 64 * h, 64 + 64 * h, st=16), 512.0 / UNIT, Op.mult, r("cf", 26 + h, 27 + h), Op.add)
+    digits(0)
 
-    masks(0)
-
-    def spread(buf, w, between=None):
-        def move(e, out, a):
-            if e == "v":
-                cp(out, a)
-            else:
-                act(out, a, Fn.Copy)
-        for b in range(4):
-            move("v" if b < 2 else "s", r(buf, w, 2 * w, 32 * b, 32 * b + 32), r(buf, 0, w, 32 * (b ^ 1), 32 * (b ^ 1) + 32))
-        if between is not None:
-            between()
-        for b in (0, 1):
-            move("v" if b < 1 else "s", r(buf, 2 * w, 4 * w, 64 * b, 64 * b + 64), r(buf, 0, 2 * w, 64 * (1 - b), 64 * (1 - b) + 64))
+    def move(e, out, a):
+        if e == "v":
+            cp(out, a)
+        else:
+            act(out, a, Fn.Copy)
 
     for t in range(R):
         c = "comb%d" % t
@@ -405,25 +383,25 @@ def rank_program(g, core, T, topo):
             act(zs(h, 0, 192), r("zz", 512 * h, 512 * h + 192), Fn.Copy)
 
         def scores(h):
-            w, o, q = r("zsb", ZW * h, ZW * h + 1 + P * t + P), r("zo", 4 * h, 4 * h + 4), r("gs", 64 * h, 64 * h + 64)
+            w, o, q = r("zsb", ZW * h, ZW * h + 1 + P * t + P), r("zo", 4 * h, 4 * h + 4), r("gs", 96 * h, 96 * h + 64)
             op("v", lambda: g.vector.tensor_tensor(ap(q), ap(w).indirect(ap(o)), T.negm[:, 0:64], Op.add), [w, o, r("negm", 0, 64)], [q])
 
         def own_scores(h):
-            scan(r("sbx", 64 * h, 64 * h + 64), r("segm", 0, 64), r("gs", 64 * h, 64 * h + 64), LOW, Op.add, Op.max)
+            scan(r("sbx", 64 * h, 64 * h + 64), r("segm", 0, 64), r("gs", 96 * h, 96 * h + 64), LOW, Op.add, Op.max)
 
         sb = lambda h: r("sbx", 15 + 64 * h, 64 + 64 * h, st=16)
-        bst = lambda h: r("bst", h, h + 1)
+        bst = lambda h: r("sc", 96 * h + 95, 96 * h + 96)
         k4 = lambda name, h: r(name, 4 * h, 4 * h + 4)
-        best = lambda h: red(bst(h), r("gs", 64 * h, 64 * h + 64), Op.max)
-        wide = lambda h: ts(r("rpa", 32 * h, 32 * h + 32), r("ones32", 0, 32), bst(h), Op.mult)
+        isbest = lambda h: ts(k4("e8", h), sb(h), bst(h), Op.is_equal)
         scores(0)
-        best(0)
+        if t == 0:
+            digits(1)
         scores(1)
-        wide(0)
-        best(1)
-        own_scores(0)
-        wide(1)
-        own_scores(1)
+        for h in (0, 1):
+            a = r("gs", 96 * h, 96 * h + 96)
+            scan(r("sc", 96 * h, 96 * h + 96), a, a, LOW, Op.max, Op.max)
+        for h in (0, 1):
+            tr(r("row", 32 * h, 32 * h + 32), r("sc", 96 * h + 64, 96 * h + 96))
         if more:
             lst = []
             for t2 in range(t + 1, R):
@@ -431,13 +409,27 @@ def rank_program(g, core, T, topo):
             if t == 0:
                 lst += copies("qx", 0, "finw", 0, P)
             dmas("dc%d" % t, lst)
-        tr(r("row", 0, 64), r("rpa", 0, 64))
-        ts(k4("e8", 0), sb(0), bst(0), Op.is_equal)
-        spread("row", 64, lambda: ts(k4("e8", 1), sb(1), bst(1), Op.is_equal))
-        for i in (0, 1):
-            a = r("row", 128 * i, 128 * i + 128)
-            ts(r("ed", 256 * i, 256 * i + 256, st=2), a, -1.0, Op.mult, bst(0), Op.add)
-            act(r("ed", 512 + 256 * i, 768 + 256 * i, st=2), a, Fn.Identity, bias=bst(1), scale=-1.0)
+        own_scores(0)
+        for b in range(4):
+            move("v" if b < 2 else "s", r("row", 64, 128, 32 * b, 32 * b + 32), r("row", 0, 64, 32 * (b ^ 1), 32 * (b ^ 1) + 32))
+        own_scores(1)
+        for b in (0, 1):
+            move("v" if b < 1 else "s", r("row", 128, 256, 64 * b, 64 * b + 64), r("row", 0, 128, 64 * (1 - b), 64 * (1 - b) + 64))
+        isbest(0)
+        isbest(1)
+
+        def differ(e, h, i):
+            a, o = r("row", 128 * i, 128 * i + 128), r("ed", 512 * h + 256 * i, 512 * h + 256 * i + 256, st=2)
+            if e == "v":
+                ts(o, a, -1.0, Op.mult, bst(h), Op.add)
+            else:
+                act(o, a, Fn.Identity, bias=bst(h), scale=-1.0)
+
+        differ("v", 0, 0)
+        tt(r("t8", 0, 8), r("e8", 0, 8), r("zf", 0, 8), Op.mult)
+        differ("s", 0, 1)
+        differ("s", 1, 0)
+        differ("s", 1, 1)
         for h in (0, 1):
             act(k4("ne8", h), sb(h), Fn.Sign, bias=bst(h), scale=-1.0)
 
@@ -452,46 +444,67 @@ def rank_program(g, core, T, topo):
         count(0)
         ahead(512, 512)
         count(1)
-        tt(r("t8", 0, 8), r("e8", 0, 8), r("pl8", 0, 8), Op.mult)
-        tt(r("u8", 0, 8), r("e8", 0, 8), nb3, Op.mult)
         scan(r("sf", 0, 8), r("ne8", 0, 8), r("t8", 0, 8), 0.0, Op.mult, Op.add)
-        ts(r("cib", 0, 64), r("rpa", 0, 64), -1e-27, Op.mult, 224.0, Op.max)
-        number = lambda h: ts(r("rpb", 32 * h, 32 * h + 32), r("cib", 32 * h, 32 * h + 32), r("rs", h, h + 1), Op.subtract, r("sf", 4 * h + 3, 4 * h + 4), Op.add)
-        number(0)
+        ts(r("val", 0, 2), r("sc", 95, 192, st=96), -1e29, Op.is_gt)
+        loc2 = r("sf", 3, 8, st=4)
+        top = 8 if t == 2 else 0
+        ts(r("hi", 0, 2), loc2, 1.0 / 32, Op.mult)
+
+        def slots(h):
+            ts(r("oh", h, 512, st=2), r("pat", 0, 256), r("rs", h, h + 1), Op.is_equal, r("val", h, h + 1), Op.mult)
+
+        slots(0)
+        ts(r("hf", 0, 2), r("hi", 0, 2), 32.0, Op.mult)
+        for u in (0, 1):
+            act(r("dg", 6 * u, 6 * u + 2), r("hf", 0, 2), Fn.Copy, bias=-32.0 * top)
+            tt(r("dg", 32 + 6 * u, 34 + 6 * u), loc2, r("hf", 0, 2), Op.subtract)
+        slots(1)
+        quant("dgq", "dgqs", 0, 128, "dg", 0, 512)
+        quant("ohq", "ohqs", 0, 128, "oh", 0, 512)
+        mm("zz", 2, 128, "ohq", 0, "dgq", 0)
+        if t == 0:
+            ts(nb3, nbo, 1.0, Op.add)
+        ts(r("tk", 0, 1), r("rs", 0, 1), 193.0, Op.is_gt, r("val", 0, 1), Op.mult)
+        ts(r("tk", 1, 2), r("rs", 1, 2), 193.0, Op.is_gt, r("val", 1, 2), Op.mult)
+        tt(r("u8", 0, 8), r("e8", 0, 8), nb3, Op.mult)
         scan(r("sn", 0, 8), r("ne8", 0, 8), r("u8", 0, 8), 0.0, Op.mult, Op.add)
-        number(1)
-        tr(r("tb", 0, 64), r("rpb", 0, 64))
-        ts(r("tk", 0, 2), r("rpb", 0, 64, st=32), 32.0, Op.is_lt)
-        for i in range(2):
-            ts(r("dx", 64 * i, 64 * i + 64), r("tb", 0, 64), cf(14 + i), Op.subtract, UNIT, Op.mult)
-        for i in range(2):
-            red(r("pt", i, i + 1), r("dx", 64 * i, 64 * i + 64), Op.min, absolute=True)
-        tt(r("y2", 0, 2), r("sn", 3, 8, st=4), r("tk", 0, 2), Op.mult)
-        spread("pt", 2, lambda: tt(r("pa2", 0, 2), r("pa2", 0, 2), r("y2", 0, 2), Op.add))
-        for i in range(2):
-            red(r("vi", i, i + 1), r("pt", i, 8, st=2), Op.min)
-        ts(r("offp", 0, 2), r("vi", 0, 2), 2.0 ** -9, Op.mult, float(P * t + P - 1), Op.min)
-        ts(r("vi", 4, 6), r("vi", 0, 2), 511 - 2 ** 19, Op.bitwise_and)
+        out = lambda i: r("zz", 1024 + i, 1025 + i)
+        for u in (0, 1):
+            ts(r("offp", u, u + 1), out(u), out(8 + u), Op.add, 32.0 * top, Op.add)
+        for u, k in enumerate((1, 25)):
+            ts(r("pl", u, u + 1), out(4 + u), out(12 + u), Op.add, cf(k), Op.max)
         pick("pk", 0, c, P * t + P, "offp", 0, 2)
-        ts(r("offo", 0, 2), r("vi", 4, 6), P - 1.0, Op.min)
+        ts(r("offo", 0, 2), r("pl", 0, 2), -float(OFF), Op.add, 0.0, Op.max)
         for b in range(4):
             gather_s(r("od", 32 * b, 32 * b + 32), r("own", 256 * b, 256 * b + 256), r("offo", 0, 2))
         my = "my%d" % (t + 1)
-        for i in range(2):
-            ts(r(my, i, i + 1), r("vi", 4 + i, 5 + i), cf(24 + i), Op.min, float(P * rank), Op.add)
+        ts(r(my, 0, 2), r("pl", 0, 2), float(STR * rank), Op.add)
         if more:
             send_list(t + 1)
-        else:
-            dmas("dpa", [("y", T.pa[0:1, 128 * h:128 * h + 128], T.pa2[:, h:h + 1], [r("pa2", h, h + 1)], []) for h in (0, 1)])
+
+        def parents():
+            if t == 0:
+                ts(r("z2", 0, 2), place2, float(P * rank + 1), Op.add)
+                tt(r("w3", 0, 2), r("z2", 0, 2), r("tk0", 0, 2), Op.mult)
+                ts(r("pa2", 0, 2), r("w3", 0, 2), -1.0, Op.add)
+            tt(r("y2", 0, 2), r("sn", 3, 8, st=4), r("tk", 0, 2), Op.mult)
+            tt(r("pa2", 0, 2), r("pa2", 0, 2), r("y2", 0, 2), Op.add)
+
         for b in range(4):
             mm("dec", b, 128, "eq", 128 * b, "pk", 0)
         lv = P - 1 + S * t
         scatter(r("loc", 0, TAB), r(my, 0, 2), r("posc", lv, lv + S))
-        half_row = lambda m: run_on(r("flx", 128 * m, 128 * m + 128), r("loc", P * rank + 128 * m, P * rank + 128 * m + 128), 128)
+        if not more:
+            parents()
+            dmas("dpa", [("y", T.pa[0:1, 128 * h:128 * h + 128], T.pa2[:, h:h + 1], [r("pa2", h, h + 1)], []) for h in (0, 1)])
+        half_row = lambda m: run_on(r("flx", 128 * m, 128 * m + 128), r("loc", base + 128 * m, base + 128 * m + 128), 128)
+        half_list = lambda m: ts(r("fo", 8 * m, 8 * m + 8), r("flx", 128 * m + 15, 128 * m + 128, st=16), cf(19), Op.subtract)
         for b in range(4):
             tt(r("ht", b, 128, st=4), r("dec", 512 * b, 512 * b + 32), r("od", 32 * b, 32 * b + 32), Op.add)
-            if not more and b == 1:
-                half_row(0)
+            if not more and b < 2:
+                half_row(b)
+            elif not more:
+                half_list(b - 2)
         if more:
             d, o = "comb%d" % (t + 1), P * (t + 1) + 224
             quant(d, d + "s", o, o + 128, "ht", 0, 512)
@@ -499,15 +512,13 @@ def rank_program(g, core, T, topo):
             dmas("df%d" % t, copies(d, o, "finw", P + S * t, S))
             scatter(tab, r(my, 0, 2), r("posc", P * (t + 1) + 224, P * (t + 1) + 256))
             settle(False)
+            masks(t + 1)
+            parents()
             if t == 0:
                 quant("qw", "qws", 0, 256, "wt", 0, 1024)
-            masks(t + 1)
         else:
             quant("finw", "finws", 320, 448, "ht", 0, 512)
-            half_row(1)
 
-    for m in (0, 1):
-        ts(r("fo", 8 * m, 8 * m + 8), r("flx", 128 * m + 15, 128 * m + 128, st=16), cf(19), Op.subtract)
     for m in (0, 1):
         pick("fin", 128 * m, "finw", 352, "fo", 8 * m, 8 * m + 8)
         for o in (0, 1):
@@ -517,7 +528,7 @@ def rank_program(g, core, T, topo):
         act(r("sy", 256 + 128 * m, 384 + 128 * m), r("zz", 1024 * m + 512, 1024 * m + 640), Fn.Copy)
     dmas("dout", [("y", T.oc[:], T.fin[:].bitcast(dt.uint8), [r("fin", 0, 256)], [])] +
          [("y", T.osc[4 * k:4 * k + 4, :], T.fins[32 * k:32 * k + 4, :], [r("fins", 0, 256)], []) for k in range(4)] +
-         [("s", T.y[:], T.sy[:], [r("sy", 0, 512)], [])])
+         [(q, T.y[:, 256 * o:256 * o + 256], T.sy[:, 256 * o:256 * o + 256], [r("sy", 256 * o, 256 * o + 256)], []) for o, q in enumerate("ys")])
     for sem in cnt:
         if known["g"].get(sem, 0) < cnt[sem]:
             g.wait_ge(T.sem[sem], cnt[sem])

import numpy as np
from concourse.bass import DstId, RemoteDMATransfer
from concourse.mybir import dt, AluOpType as Op, AxisListType, ActivationFunctionType as Fn

F8 = "float8_e4m3fn_x4"
WC = (384, 608, 864)
WF = 448
STR, OFF = 304, 48
TAB, NONE = 2440, 2432
ZW = 776
LOW = -9e29
SCRATCH = {
    "xt": ("sbuf", [128, 1024], "bfloat16"), "wt": ("sbuf", [128, 1024], "bfloat16"),
    "qx": ("sbuf", [128, 256], F8), "qxs": ("sbuf", [128, 256], "uint8"),
    "qw": ("sbuf", [128, 256], F8), "qws": ("sbuf", [128, 256], "uint8"), "half": ("sbuf", [128, 128], "bfloat16"),
    "et": ("sbuf", [128, 528], "bfloat16"), "eq": ("sbuf", [128, 512], F8), "eqs": ("sbuf", [128, 512], "uint8"),
    "comb0": ("sbuf", [128, WC[0]], F8), "comb0s": ("sbuf", [128, WC[0]], "uint8"),
    "comb1": ("sbuf", [128, WC[1]], F8), "comb1s": ("sbuf", [128, WC[1]], "uint8"),
    "comb2": ("sbuf", [128, WC[2]], F8), "comb2s": ("sbuf", [128, WC[2]], "uint8"),
    "finw": ("sbuf", [128, WF], F8), "finws": ("sbuf", [128, WF], "uint8"),
    "fin": ("sbuf", [128, 256], F8), "fins": ("sbuf", [128, 256], "uint8"),
    "pk": ("sbuf", [128, 128], F8), "pks": ("sbuf", [128, 128], "uint8"),
    "ht": ("sbuf", [128, 512], "bfloat16"), "od": ("sbuf", [128, 128], "float32"), "own": ("sbuf", [128, 1024], "bfloat16"),
    "sdw": ("sbuf", [128, 2], "int32"), "nbw": ("sbuf", [128, 64], "int32"), "sdu": ("sbuf", [128, 2], "uint16"),
    "nbof": ("sbuf", [128, 2], "uint16"), "nboi": ("sbuf", [128, 16], "int32"), "nbsh": ("sbuf", [128, 8], "int32"),
    "nbo": ("sbuf", [128, 8], "float32"), "nba": ("sbuf", [128, 8], "float32"), "nbn": ("sbuf", [128, 8], "float32"),
    "nbm": ("sbuf", [128, 8], "float32"), "nb3": ("sbuf", [128, 8], "float32"), "nbu": ("sbuf", [128, 8], "uint16"),
    "oix": ("sbuf", [128, 2], "uint16"), "olk": ("sbuf", [128, 32], "float32"), "ofl": ("sbuf", [128, 32], "float32"),
    "pint": ("sbuf", [128, 1], "int32"), "pidx": ("sbuf", [128, 1], "float32"),
    "c16": ("sbuf", [128, 64], "float32"),
    "ic": ("sbuf", [128, 256], "float32"), "ci": ("sbuf", [128, 16], "int32"), "cf": ("sbuf", [128, 32], "float32"),
    "plm": ("sbuf", [128, 256], "float32"), "ste": ("sbuf", [128, 512], "bfloat16"),
    "ones": ("sbuf", [128, 2], "float32"),
    "posc": ("sbuf", [128, 768], "float32"), "tab": ("sbuf", [128, TAB], "float32"), "loc": ("sbuf", [128, TAB], "float32"),
    "hma": ("sbuf", [128, 64], "float32"), "hm": ("sbuf", [128, 128], "float32"),
    "negm": ("sbuf", [128, 64], "float32"), "segm": ("sbuf", [128, 64], "float32"),
    "my0": ("sbuf", [128, 2], "uint16"), "my1": ("sbuf", [128, 2], "uint16"), "my2": ("sbuf", [128, 2], "uint16"), "my3": ("sbuf", [128, 2], "uint16"),
    "land0": ("sbuf", [128, 16], "uint16"), "land1": ("sbuf", [128, 16], "uint16"), "land2": ("sbuf", [128, 16], "uint16"),
    "lk": ("sbuf", [128, 128], "float32"), "pv": ("sbuf", [128, 128], "float32"), "zo": ("sbuf", [128, 8], "uint16"),
    "zf": ("sbuf", [128, 8], "float32"),
    "zsb": ("sbuf", [128, 2 * ZW], "float32"), "gs": ("sbuf", [128, 192], "float32"), "sc": ("sbuf", [128, 192], "float32"),
    "sbx": ("sbuf", [128, 128], "float32"), "row": ("sbuf", [128, 256], "float32"),
    "e8": ("sbuf", [128, 8], "float32"), "ne8": ("sbuf", [128, 8], "float32"),
    "t8": ("sbuf", [128, 8], "float32"), "u8": ("sbuf", [128, 8], "float32"),
    "sf": ("sbuf", [128, 8], "float32"), "sn": ("sbuf", [128, 8], "float32"), "val": ("sbuf", [128, 2], "float32"),
    "ed": ("sbuf", [128, 1024], "bfloat16"), "cm": ("sbuf", [128, 1024], "bfloat16"), "sg": ("sbuf", [128, 512], "bfloat16"),
    "rs": ("sbuf", [128, 2], "float32"), "y2": ("sbuf", [128, 2], "float32"), "z2": ("sbuf", [128, 2], "float32"),
    "hi": ("sbuf", [128, 2], "int32"), "hf": ("sbuf", [128, 2], "float32"), "pat": ("sbuf", [128, 256], "bfloat16"),
    "oh": ("sbuf", [128, 512], "bfloat16"), "ohq": ("sbuf", [128, 128], F8), "ohqs": ("sbuf", [128, 128], "uint8"),
    "dg": ("sbuf", [128, 512], "bfloat16"), "dgq": ("sbuf", [128, 128], F8), "dgqs": ("sbuf", [128, 128], "uint8"),
    "pl": ("sbuf", [128, 2], "float32"),
    "offp": ("sbuf", [128, 2], "uint16"), "offo": ("sbuf", [128, 2], "uint16"),
    "tk0": ("sbuf", [128, 2], "float32"), "tk": ("sbuf", [128, 2], "float32"), "nf": ("sbuf", [128, 2], "float32"),
    "pa2": ("sbuf", [128, 2], "float32"), "w3": ("sbuf", [128, 2], "float32"),
    "flx": ("sbuf", [128, 256], "float32"), "fo": ("sbuf", [128, 16], "uint16"), "sy": ("sbuf", [128, 512], "float32"),
    "dec": ("psum", [128, 2048], "float32"), "zz": ("psum", [128, 2048], "float32"),
}
SEMAPHORES = ["v", "s", "p", "gp", "dsd", "dx", "dnb", "dw", "arl0", "arl1", "arl2", "arc0", "arc1", "arc2",
              "arn0", "arn1", "arn2", "dc0", "dc1", "df0", "df1", "di", "dout", "dpa", "sent"]


def r(name, c0, c1, p0=0, p1=128, st=1):
    return (name, c0, c1, p0, p1, st)


def meet(a, b):
    if a[0] != b[0] or a[1] >= b[2] or b[1] >= a[2] or a[3] >= b[4] or b[3] >= a[4]:
        return False
    return not (a[5] == b[5] and a[5] > 1 and (a[1] - b[1]) % a[5])


def inside(a, b):
    return a[1] >= b[1] and a[2] <= b[2] and a[3] >= b[3] and a[4] <= b[4] and b[5] == 1


def rank_program(g, core, T, topo):
    rank = T.rank_of(core)
    if rank is None:
        return
    cores = list(T.cores)
    n = len(cores)
    S, P, R = 32, 256, 3

    eng = {"v": g.vector, "s": g.scalar, "p": g.tensor, "y": g.sync, "g": g}
    own = {"v": "v", "s": "s", "p": "p", "g": "gp"}
    known = {e: {} for e in eng}
    cnt = {}
    hist = {}
    seq = [0]

    def need(e, toks):
        for sem, val, clock, q in sorted(toks, key=lambda t: -t[3]):
            if known[e].get(sem, 0) < val:
                eng[e].wait_ge(T.sem[sem], val)
                known[e][sem] = val
                for k, c in clock.items():
                    known[e][k] = max(known[e].get(k, 0), c)

    def before(e, reads, writes):
        toks = []
        for a in reads:
            for b, kind, tok, f in hist.get(a[0], []):
                if kind == "w" and meet(a, b):
                    toks.append(tok)
        for a in writes:
            for b, kind, tok, f in hist.get(a[0], []):
                if meet(a, b):
                    toks.append(tok)
        need(e, toks)

    def note(e, reads, writes, tok):
        for a in writes:
            hist[a[0]] = [h for h in hist.get(a[0], []) if not inside(h[0], a)] + [(a, "w", tok, e)]
        for a in reads:
            hist[a[0]] = [h for h in hist.get(a[0], []) if not (h[1] == "r" and h[3] == e and inside(h[0], a))] + [(a, "r", tok, e)]

    def token(sem, clock):
        seq[0] += 1
        return (sem, cnt[sem], dict(clock), seq[0])

    def op(e, fn, reads, writes):
        before(e, reads, writes)
        sem = own[e]
        cnt[sem] = cnt.get(sem, 0) + 1
        fn().then_inc(T.sem[sem], 1)
        note(e, reads, writes, token(sem, known[e]))

    def dmas(sem, lst):
        for e, out, in_, reads, writes in lst:
            before(e, reads, writes)
            cnt[sem] = cnt.get(sem, 0) + 16
            eng[e].dma_start(out, in_).then_inc(T.sem[sem], 16)
        for e, out, in_, reads, writes in lst:
            note(sem, reads, writes, token(sem, {}))

    def ap(q):
        name, c0, c1, p0, p1, st = q
        return T[name][p0:p1, c0:c1] if st == 1 else T[name][p0:p1, c0:c1:st]

    def tup(*xs):
        return [x for x in xs if isinstance(x, tuple)]

    def sv(x):
        return ap(x) if isinstance(x, tuple) else x

    def ts(out, a, s1, op0, s2=None, op1=None):
        if op1 is None:
            op("v", lambda: g.vector.tensor_scalar(ap(out), ap(a), sv(s1), None, op0), [a] + tup(s1), [out])
        else:
            op("v", lambda: g.vector.tensor_scalar(ap(out), ap(a), sv(s1), sv(s2), op0, op1), [a] + tup(s1, s2), [out])

    def tt(out, a, b, o):
        op("v", lambda: g.vector.tensor_tensor(ap(out), ap(a), ap(b), o), [a, b], [out])

    def cp(out, a):
        op("v", lambda: g.vector.tensor_copy(ap(out), ap(a)), [a], [out])

    def tr(out, a):
        op("v", lambda: g.vector.transpose(ap(out), ap(a)), [a], [out])

    def scan(out, a, b, init, o0, o1):
        op("v", lambda: g.vector.tensor_tensor_scan(ap(out), ap(a), ap(b), init, o0, o1), [a, b], [out])

    def fill(out, c):
        op("v", lambda: g.vector.memset(ap(out), c), [], [out])

    def iota(out, pattern, base, cm, flag=True):
        if flag:
            op("g", lambda: g.iota(ap(out), pattern, base, cm, allow_small_or_imprecise_dtypes=True), [], [out])
        else:
            op("g", lambda: g.iota(ap(out), pattern, base, cm), [], [out])

    def act(out, a, func, bias=0.0, scale=1.0, accum=None):
        w = [out] + tup(accum)
        op("s", lambda: g.scalar.activation(ap(out), ap(a), func, bias=sv(bias), scale=sv(scale), accum_out=None if accum is None else ap(accum)),
           [a] + tup(bias, scale), w)

    def quant(c, s, a, b, src, x0, x1):
        op("v", lambda: g.vector.quantize_mx(T[c][:, a:b], T[s][:, a:b], T[src][:, x0:x1]), [r(src, x0, x1)], [r(c, a, b), r(s, a, b)])

    def gather(out, win, off):
        op("v", lambda: g.vector.tensor_copy(ap(out), ap(win).indirect(ap(off))), [win, off], [out])

    def gather_s(out, win, off):
        op("s", lambda: g.scalar.activation(ap(out), ap(win).indirect(ap(off)), Fn.Copy), [win, off], [out])

    def scatter(win, off, a):
        op("v", lambda: g.vector.tensor_copy(ap(win).indirect(ap(off)), ap(a)), [a, off], [win])

    def pick(c2, a2, c1, w, off, o0, o1):
        k = 16 * (o1 - o0)
        s2, s1 = c2 + "s", c1 + "s"
        op("v", lambda: g.vector.tensor_copy(T[c2][:, a2:a2 + k].bitcast(dt.uint32), T[c1][:, 0:w].bitcast(dt.uint32).indirect(T[off][:, o0:o1])),
           [r(c1, 0, w), r(off, o0, o1)], [r(c2, a2, a2 + k)])
        op("s", lambda: g.scalar.activation(T[s2][:, a2:a2 + k], T[s1][:, 0:w].indirect(T[off][:, o0:o1]), Fn.Copy),
           [r(s1, 0, w), r(off, o0, o1)], [r(s2, a2, a2 + k)])

    def mm(out, bank, width, c1, a1, c2, a2):
        op("p", lambda: g.tensor.matmul_mx(T[out][:, 512 * bank:512 * bank + width], T[c1][:, a1:a1 + 128], T[c1 + "s"][:, a1:a1 + 128],
                                           T[c2][:, a2:a2 + width], T[c2 + "s"][:, a2:a2 + width], True, True),
           [r(c1, a1, a1 + 128), r(c1 + "s", a1, a1 + 128), r(c2, a2, a2 + width), r(c2 + "s", a2, a2 + width)],
           [r(out, 512 * bank, 512 * bank + 512)])

    far = [q for q in range(n) if topo.chip(cores[q]) != topo.chip(core)]
    near = [q for q in range(n) if q != rank and topo.chip(cores[q]) == topo.chip(core)]
    mate = rank ^ 1
    assert near == [mate]
    fe = topo.engines(core, cores[far[0]])
    ne = [e for e in topo.engines(core, cores[mate]) if e not in fe][::2]
    block = lambda q: n - 1 - (q ^ rank)

    def dest(q):
        a = topo.addr(cores[q])
        return DstId(rid=a[0], pnc=a[1])

    def send(fsem, nsem, src, dst_of, reads):
        before("g", reads, [])
        out = []
        for qs, es, sem in ((far, fe, fsem), (near, ne, nsem)):
            out.append(RemoteDMATransfer(dst_ids=[dest(q) for q in qs], dma_engine_mask=sum(1 << e for e in es), remote_sem=T.sem[sem],
                                         srcs=[src], dsts=[dst_of(q) for q in qs], alu_op=0))
            cnt["sent"] = cnt.get("sent", 0) + len(es)
        g.remote_dma_fused(out, local_sem=T.sem["sent"])

    def landed(sem, total, regions):
        cnt[sem] = total
        seq[0] += 1
        for a in regions:
            note("far", [], [a], (sem, total, {}, seq[0]))

    def send_list(t):
        send("arl%d" % t, "arl%d" % t, T["my%d" % t][:, 0:2], lambda q: T["land%d" % t][:, 2 * block(q):2 * block(q) + 2], [r("my%d" % t, 0, 2)])
        landed("arl%d" % t, len(fe) * len(far) + len(ne), [r("land%d" % t, 0, 14)])

    def send_cols(t):
        c, b, fs, nr = "comb%d" % t, P * t, "arc%d" % t, "arn%d" % t
        o, w = b + 224, b + 192
        send(fs, nr, T[c][:, o:o + S].bitcast(dt.uint8), lambda q: T[c][:, b + S * block(q):b + S * block(q) + S].bitcast(dt.uint8), [r(c, o, o + S)])
        send(fs, nr, T[c + "s"][:, o:o + S], lambda q: T[c + "s"][:, b + S * block(q):b + S * block(q) + S], [r(c + "s", o, o + S)])
        landed(nr, 2 * len(ne), [r(c, w, w + S), r(c + "s", w, w + S)])
        landed(fs, 2 * len(fe) * len(far), [r(c, b, w), r(c + "s", b, w)])

    def copies(src, s0, dst, d0, w):
        return [("y", T[dst][:, d0:d0 + w].bitcast(dt.uint8), T[src][:, s0:s0 + w].bitcast(dt.uint8), [r(src, s0, s0 + w)], [r(dst, d0, d0 + w)]),
                ("y", T[dst + "s"][:, d0:d0 + w], T[src + "s"][:, s0:s0 + w], [r(src + "s", s0, s0 + w)], [r(dst + "s", d0, d0 + w)])]

    dmas("dsd", [(q, T.sdw[16 * a:16 * a + 16, :], T.sd[:], [], [r("sdw", 0, 2, 16 * a, 16 * a + 16)]) for a, q in enumerate("ys")])
    dmas("dx", [("y", T.xt[:], T.x[:], [], [r("xt", 0, 1024)])])
    dmas("dnb", [("y", T.nbw[16 * a:16 * a + 16, :], T.nb[:], [], [r("nbw", 0, 64, 16 * a, 16 * a + 16)]) for a in range(8)])
    dmas("dw", [("y", T.wt[:], T.w[:], [], [r("wt", 0, 1024)])])

    base = STR * rank + OFF
    pint, pidx = r("pint", 0, 1), r("pidx", 0, 1)
    iota(pint, [[0, 1]], 0, 1, False)
    iota(pidx, [[0, 1]], 0, 1)
    iota(r("posc", 0, 256), [[1, 256]], 1, 0)
    ci = lambda i: r("ci", i, i + 1)
    cf = lambda i: r("cf", i, i + 1)
    fill(r("ste", 0, 512, st=2), 0.0)
    fill(r("ste", 1, 512, st=2), 1.0)
    for b in range(5):
        act(r("tab", 512 * b, min(512 * b + 512, TAB)), r("ste", 0, min(512, TAB - 512 * b)), Fn.Copy, scale=0.0)
    fill(r("half", 0, 128), 0.5)
    fill(r("et", 0, 528), 0.0)
    e_, h_ = r("et", 3, 515, st=4), r("half", 0, 128)
    op("g", lambda: g.affine_select(ap(e_), ap(h_), [[-1, 128]], Op.is_equal, 0.0, 0, 1), [h_], [e_])
    iota(r("c16", 0, 64), [[0, 4], [1, 16]], 0, 0)
    ts(ci(7), pint, 4, Op.arith_shift_right)
    ts(ci(0), pint, 31, Op.bitwise_and)
    ts(ci(1), pint, 15, Op.bitwise_and)
    ts(ci(2), pint, 96, Op.bitwise_and)
    ts(ci(3), pint, 32, Op.bitwise_and)
    ts(ci(4), pint, 64, Op.bitwise_and)
    ts(ci(5), pint, 3, Op.bitwise_and)
    ts(ci(6), pint, 4, Op.bitwise_and)
    cp(cf(10), pidx)
    cp(r("cf", 0, 8), r("ci", 0, 8))
    ts(cf(11), pidx, 128.0, Op.add)
    ts(cf(17), cf(5), -16.0, Op.mult, cf(7), Op.add)

    for b in range(4):
        ts(r("my0", 0, 2, 32 * b, 32 * b + 32), r("sdw", 0, 2, 0, 32), float(base), Op.add)
    send_list(0)
    for b in range(4):
        cp(r("sdu", 0, 2, 32 * b, 32 * b + 32), r("sdw", 0, 2, 0, 32))
    place2 = r("cf", 10, 12)
    quant("qx", "qxs", 0, 256, "xt", 0, 1024)
    pick("comb0", 224, "qx", 256, "sdu", 0, 2)
    send_cols(0)
    dmas("di", copies("qx", 0, "comb0", 256, 128) + copies("qx", 32, "pk", 32, 96))

    iota(r("ic", 0, 256), [[32, 4], [128, 2], [1, 32]], 0, 0)
    iota(r("dg", 0, 512), [[0, 512]], 0, 0)
    iota(r("pat", 0, 256), [[0, 8], [-2, 16], [-32, 2]], 256, 0)
    iota(r("posc", 256, 768), [[1, 512]], 257, 0)
    iota(r("loc", base, base + P), [[1, P]], 0, 0)
    iota(r("ht", 0, 512), [[0, 512]], 0, 0)

    tab = r("tab", 0, TAB)
    for b in range(4):
        quant("eq", "eqs", 128 * b, 128 * b + 128, "et", 3 - b, 515 - b)
    ts(cf(18), cf(6), 2.0, Op.mult, 48.0, Op.add)
    ts(cf(19), cf(1), -1024.0, Op.mult, 15360.0, Op.add)
    ts(cf(25), cf(1), 16.0, Op.add)
    tt(r("nbof", 0, 1), cf(17), cf(18), Op.add)
    ts(r("oix", 0, 2), place2, float(base), Op.add)
    ts(r("hma", 0, 64), r("c16", 0, 64), cf(1), Op.is_equal)
    for b in range(2):
        act(r("hm", 64 * b, 64 * b + 64), r("hma", 0, 64), Fn.Copy, bias=1024.0, scale=-66560.0)
    for b in range(4):
        mm("dec", b, 256, "eq", 128 * b, "qx", 0)
        act(r("own", 256 * b, 256 * b + 256), r("dec", 512 * b, 512 * b + 256), Fn.Copy)
    op("v", lambda: g.vector.tensor_copy(T.nboi[:, 0:16], T.nbw[:, 0:64].indirect(T.nbof[:, 0:1])), [r("nbw", 0, 64), r("nbof", 0, 1)], [r("nboi", 0, 16)])
    scatter(tab, r("my0", 0, 2), r("posc", 224, 256))
    nbi, nbo, nb3 = r("nboi", 0, 8), r("nbo", 0, 8), r("nb3", 0, 8)
    ts(r("nbsh", 0, 8), nbi, 8, Op.arith_shift_right)
    cp(nbo, nbi)
    gather(r("olk", 0, 32), tab, r("oix", 0, 2))
    ts(r("nba", 0, 8), r("nbsh", 0, 8), float(STR - P), Op.mult, float(OFF - NONE), Op.add)
    ts(r("nbn", 0, 8), nbo, 0.0, Op.is_lt, float(NONE + 1 + STR - P - OFF), Op.mult)

    def run_on(out, a, width):
        scan(out, r("hm", 0, width), a, 0.0, Op.add, Op.max)

    run_on(r("ofl", 0, 32), r("olk", 0, 32), 32)
    tt(r("nba", 0, 8), r("nba", 0, 8), nbo, Op.add)
    ts(cf(21), cf(3), -2.0, Op.mult, cf(2), Op.add)
    ts(r("tk0", 0, 2), r("ofl", 15, 32, st=16), cf(19), Op.subtract, 0.0, Op.is_gt)
    tt(r("nbm", 0, 8), r("nba", 0, 8), r("nbn", 0, 8), Op.add)
    ts(cf(22), cf(4), -2.0, Op.mult, cf(2), Op.add)
    ts(cf(23), cf(4), -2.0, Op.mult, cf(21), Op.add)

    def settle(first):
        if first:
            ts(r("nf", 0, 2), r("tk0", 0, 2), -1.0, Op.mult, 1.0, Op.add)
            ts(r("cf", 12, 14), place2, -0.5, Op.add, -2.0 ** -120, Op.mult)
        else:
            tt(r("nf", 0, 2), r("nf", 0, 2), r("tk", 0, 2), Op.subtract)
        for h in (0, 1):
            ts(r("nbu", 4 * h, 4 * h + 4), r("nbm", 4 * h, 4 * h + 4), r("nf", h, h + 1), Op.mult, float(NONE), Op.add)

    def masks(t):
        scatter(tab, r("land%d" % t, 0, 14), r("posc", P * t, P * t + 224))
        gather(r("lk", 0, 128), tab, r("nbu", 0, 8))
        run_on(r("pv", 0, 128), r("lk", 0, 128), 128)
        ts(r("zo", 0, 8), r("pv", 15, 128, st=16), cf(19), Op.subtract)
        ts(r("zf", 0, 8), r("pv", 15, 128, st=16), cf(19), Op.subtract, -1.0, Op.add)

    settle(True)
    for d, b in enumerate((2, 21, 22, 23)):
        act(r("plm", 64 * d, 64 * d + 64), r("ic", 64 * d, 64 * d + 64), Fn.Identity, bias=cf(b))
    for h in (0, 1):
        act(r("ed", 512 * h + 1, 512 * h + 512, st=2), r("plm", 0, 256), Fn.Identity, bias=r("cf", 12 + h, 13 + h), scale=2.0 ** -120)
    masks(0)
    fill(r("ones", 0, 2), 1.0)
    for h in (0, 1):
        fill(r("zsb", ZW * h, ZW * h + 1), LOW)
        fill(r("gs", 96 * h + 64, 96 * h + 96), LOW)
    ts(r("negm", 0, 64), r("c16", 0, 64), cf(1), Op.not_equal, LOW, Op.mult)
    ts(r("segm", 0, 64), r("c16", 0, 64), 0.0, Op.is_equal, LOW, Op.mult)

    def digits(h):
        ts(r("dg", 16 + h, 23 + h, st=6), r("ones", 0, 2), cf(2), Op.mult, float(OFF + 16 + 128 * h), Op.add)
        ts(r("dg", 48 + 6 * h, 50 + 6 * h), r("ones", 0, 2), cf(0), Op.mult, -16.0, Op.add)

    digits(0)

    def move(e, out, a):
        if e == "v":
            cp(out, a)
        else:
            act(out, a, Fn.Copy)

    for t in range(R):
        c = "comb%d" % t
        more = t < R - 1
        zs = lambda h, a, w: r("zsb", ZW * h + 1 + P * t + a, ZW * h + 1 + P * t + a + w)
        for h in (0, 1):
            mm("zz", 2 + h, 128, "qx", 128 * h, c, P * t + 192)
            act(zs(h, 192, 64), r("zz", 1024 + 512 * h, 1088 + 512 * h), Fn.Copy)
        for h in (0, 1):
            mm("zz", h, 192, "qx", 128 * h, c, P * t)
            act(zs(h, 0, 192), r("zz", 512 * h, 512 * h + 192), Fn.Copy)

        def scores(h):
            w, o, q = r("zsb", ZW * h, ZW * h + 1 + P * t + P), r("zo", 4 * h, 4 * h + 4), r("gs", 96 * h, 96 * h + 64)
            op("v", lambda: g.vector.tensor_tensor(ap(q), ap(w).indirect(ap(o)), T.negm[:, 0:64], Op.add), [w, o, r("negm", 0, 64)], [q])

        def own_scores(h):
            scan(r("sbx", 64 * h, 64 * h + 64), r("segm", 0, 64), r("gs", 96 * h, 96 * h + 64), LOW, Op.add, Op.max)

        sb = lambda h: r("sbx", 15 + 64 * h, 64 + 64 * h, st=16)
        bst = lambda h: r("sc", 96 * h + 95, 96 * h + 96)
        k4 = lambda name, h: r(name, 4 * h, 4 * h + 4)
        isbest = lambda h: ts(k4("e8", h), sb(h), bst(h), Op.is_equal)
        scores(0)
        if t == 0:
            digits(1)
        scores(1)
        for h in (0, 1):
            a = r("gs", 96 * h, 96 * h + 96)
            scan(r("sc", 96 * h, 96 * h + 96), a, a, LOW, Op.max, Op.max)
        for h in (0, 1):
            tr(r("row", 32 * h, 32 * h + 32), r("sc", 96 * h + 64, 96 * h + 96))
        if more:
            lst = []
            for t2 in range(t + 1, R):
                lst += copies(c, P * t, "comb%d" % t2, P * t, P)
            if t == 0:
                lst += copies("qx", 0, "finw", 0, P)
            dmas("dc%d" % t, lst)
        own_scores(0)
        for b in range(4):
            move("v" if b < 2 else "s", r("row", 64, 128, 32 * b, 32 * b + 32), r("row", 0, 64, 32 * (b ^ 1), 32 * (b ^ 1) + 32))
        own_scores(1)
        for b in (0, 1):
            move("v" if b < 1 else "s", r("row", 128, 256, 64 * b, 64 * b + 64), r("row", 0, 128, 64 * (1 - b), 64 * (1 - b) + 64))
        isbest(0)
        isbest(1)

        def differ(e, h, i):
            a, o = r("row", 128 * i, 128 * i + 128), r("ed", 512 * h + 256 * i, 512 * h + 256 * i + 256, st=2)
            if e == "v":
                ts(o, a, -1.0, Op.mult, bst(h), Op.add)
            else:
                act(o, a, Fn.Identity, bias=bst(h), scale=-1.0)

        differ("v", 0, 0)
        tt(r("t8", 0, 8), r("e8", 0, 8), r("zf", 0, 8), Op.mult)
        differ("s", 0, 1)
        differ("s", 1, 0)
        differ("s", 1, 1)
        for h in (0, 1):
            act(k4("ne8", h), sb(h), Fn.Sign, bias=bst(h), scale=-1.0)

        def ahead(x, w):
            scan(r("cm", x, x + w), r("ste", 0, w), r("ed", x, x + w), 0.0, Op.mult, Op.add)

        def count(h):
            act(r("sg", 256 * h, 256 * h + 256), r("cm", 512 * h + 1, 512 * h + 512, st=2), Fn.Sign, accum=r("rs", h, h + 1))

        ahead(0, 256)
        ahead(256, 256)
        count(0)
        ahead(512, 512)
        count(1)
        scan(r("sf", 0, 8), r("ne8", 0, 8), r("t8", 0, 8), 0.0, Op.mult, Op.add)
        ts(r("val", 0, 2), r("sc", 95, 192, st=96), -1e29, Op.is_gt)
        loc2 = r("sf", 3, 8, st=4)
        top = 8 if t == 2 else 0
        ts(r("hi", 0, 2), loc2, 1.0 / 32, Op.mult)

        def slots(h):
            ts(r("oh", h, 512, st=2), r("pat", 0, 256), r("rs", h, h + 1), Op.is_equal, r("val", h, h + 1), Op.mult)

        slots(0)
        ts(r("hf", 0, 2), r("hi", 0, 2), 32.0, Op.mult)
        for u in (0, 1):
            act(r("dg", 6 * u, 6 * u + 2), r("hf", 0, 2), Fn.Copy, bias=-32.0 * top)
            tt(r("dg", 32 + 6 * u, 34 + 6 * u), loc2, r("hf", 0, 2), Op.subtract)
        slots(1)
        quant("dgq", "dgqs", 0, 128, "dg", 0, 512)
        quant("ohq", "ohqs", 0, 128, "oh", 0, 512)
        mm("zz", 2, 128, "ohq", 0, "dgq", 0)
        if t == 0:
            ts(nb3, nbo, 1.0, Op.add)
        ts(r("tk", 0, 1), r("rs", 0, 1), 193.0, Op.is_gt, r("val", 0, 1), Op.mult)
        ts(r("tk", 1, 2), r("rs", 1, 2), 193.0, Op.is_gt, r("val", 1, 2), Op.mult)
        tt(r("u8", 0, 8), r("e8", 0, 8), nb3, Op.mult)
        scan(r("sn", 0, 8), r("ne8", 0, 8), r("u8", 0, 8), 0.0, Op.mult, Op.add)
        out = lambda i: r("zz", 1024 + i, 1025 + i)
        for u in (0, 1):
            ts(r("offp", u, u + 1), out(u), out(8 + u), Op.add, 32.0 * top, Op.add)
        for u, k in enumerate((1, 25)):
            ts(r("pl", u, u + 1), out(4 + u), out(12 + u), Op.add, cf(k), Op.max)
        pick("pk", 0, c, P * t + P, "offp", 0, 2)
        ts(r("offo", 0, 2), r("pl", 0, 2), -float(OFF), Op.add, 0.0, Op.max)
        for b in range(4):
            gather_s(r("od", 32 * b, 32 * b + 32), r("own", 256 * b, 256 * b + 256), r("offo", 0, 2))
        my = "my%d" % (t + 1)
        ts(r(my, 0, 2), r("pl", 0, 2), float(STR * rank), Op.add)
        if more:
            send_list(t + 1)

        def parents():
            if t == 0:
                ts(r("z2", 0, 2), place2, float(P * rank + 1), Op.add)
                tt(r("w3", 0, 2), r("z2", 0, 2), r("tk0", 0, 2), Op.mult)
                ts(r("pa2", 0, 2), r("w3", 0, 2), -1.0, Op.add)
            tt(r("y2", 0, 2), r("sn", 3, 8, st=4), r("tk", 0, 2), Op.mult)
            tt(r("pa2", 0, 2), r("pa2", 0, 2), r("y2", 0, 2), Op.add)

        for b in range(4):
            mm("dec", b, 128, "eq", 128 * b, "pk", 0)
        lv = P - 1 + S * t
        scatter(r("loc", 0, TAB), r(my, 0, 2), r("posc", lv, lv + S))
        if not more:
            parents()
            dmas("dpa", [("y", T.pa[0:1, 128 * h:128 * h + 128], T.pa2[:, h:h + 1], [r("pa2", h, h + 1)], []) for h in (0, 1)])
        half_row = lambda m: run_on(r("flx", 128 * m, 128 * m + 128), r("loc", base + 128 * m, base + 128 * m + 128), 128)
        half_list = lambda m: ts(r("fo", 8 * m, 8 * m + 8), r("flx", 128 * m + 15, 128 * m + 128, st=16), cf(19), Op.subtract)
        for b in range(4):
            tt(r("ht", b, 128, st=4), r("dec", 512 * b, 512 * b + 32), r("od", 32 * b, 32 * b + 32), Op.add)
            if not more and b < 2:
                half_row(b)
            elif not more:
                half_list(b - 2)
        if more:
            d, o = "comb%d" % (t + 1), P * (t + 1) + 224
            quant(d, d + "s", o, o + 128, "ht", 0, 512)
            send_cols(t + 1)
            dmas("df%d" % t, copies(d, o, "finw", P + S * t, S))
            scatter(tab, r(my, 0, 2), r("posc", P * (t + 1) + 224, P * (t + 1) + 256))
            settle(False)
            masks(t + 1)
            parents()
            if t == 0:
                quant("qw", "qws", 0, 256, "wt", 0, 1024)
        else:
            quant("finw", "finws", 320, 448, "ht", 0, 512)

    for m in (0, 1):
        pick("fin", 128 * m, "finw", 352, "fo", 8 * m, 8 * m + 8)
        for o in (0, 1):
            mm("zz", 2 * m + o, 128, "qw", 128 * o, "fin", 128 * m)
    for m in (0, 1):
        cp(r("sy", 128 * m, 128 * m + 128), r("zz", 1024 * m, 1024 * m + 128))
        act(r("sy", 256 + 128 * m, 384 + 128 * m), r("zz", 1024 * m + 512, 1024 * m + 640), Fn.Copy)
    dmas("dout", [("y", T.oc[:], T.fin[:].bitcast(dt.uint8), [r("fin", 0, 256)], [])] +
         [("y", T.osc[4 * k:4 * k + 4, :], T.fins[32 * k:32 * k + 4, :], [r("fins", 0, 256)], []) for k in range(4)] +
         [(q, T.y[:, 256 * o:256 * o + 256], T.sy[:, 256 * o:256 * o + 256], [r("sy", 256 * o, 256 * o + 256)], []) for o, q in enumerate("ys")])
    for sem in cnt:
        if known["g"].get(sem, 0) < cnt[sem]:
            g.wait_ge(T.sem[sem], cnt[sem])
